import numpy as np
import ml_dtypes


def mxq(x, axis, fmt="e4m3"):
    dtype, down = {"e4m3": (ml_dtypes.float8_e4m3fn, 7), "e5m2": (ml_dtypes.float8_e5m2, 14)}[fmt]
    v = np.moveaxis(np.asarray(x, np.float32).astype(ml_dtypes.bfloat16).astype(np.float64), axis, -1)
    blocks = v.reshape(v.shape[:-1] + (-1, 32))
    amax = np.abs(blocks).max(-1, keepdims=True)
    byte = np.maximum(np.where(amax > 0, np.frexp(amax)[1] - 1 + 127, 0) - down, 1)
    scale = np.exp2(byte - 127.0)
    codes = (blocks / scale).astype(np.float32).astype(dtype).astype(np.float64)
    return np.moveaxis((codes * scale).reshape(v.shape), -1, axis)


WIDE = False


def mx_kscale(k):
    if not WIDE:
        return np.ones(k)
    levels = np.array([10, -10, 5, -5, 0])
    if k % 512:
        return np.exp2(np.random.permutation(np.resize(levels, k // 32))).repeat(32)
    a = np.empty((k // 512, 16))
    for p in range(k // 512):
        a[p, :8] = np.random.permutation(np.resize(levels, 8))
        for g in range(8):
            far = levels[np.abs(levels - a[p, g]) >= 10]
            a[p, g + 8] = far[np.random.randint(len(far))]
    return np.exp2(a.ravel()).repeat(32)


def f64(x):
    return np.asarray(x).astype(np.float64)


def striped(idx):
    return np.tile(idx.reshape(-1, 16).T, (8, 1)).astype(np.uint16)


def unstriped(offs):
    return offs[:16].T.reshape(-1).astype(np.int64)


K, T, D, S, V, H, N = 1024, 1024, 3, 512, 256, 1024, 128
P = 2 ** 7


def setup_inputs():
    n = np.random.standard_normal
    s = mx_kscale(K)[:, None]
    u = mx_kscale(H)
    q = np.random.permutation(S)
    return {
        "xT": (n((K, T)) * s).astype(np.float32),
        "w1": (n((K, H)) / np.sqrt(K) / s * u).astype(np.float32),
        "w2": (n((H, N)) / np.sqrt(H) / u[:, None]).astype(np.float32),
        "gate": np.tile(np.random.uniform(0.2, 1.0, (D, 1, V)) / np.sqrt(D), (1, P, 1)).astype(np.float32),
        "offs": striped(np.random.permutation(T)[:S]),
        "pos1": striped(q[:V]),
        "pos2": striped(q[V:]),
        "pos3": striped(np.random.permutation(S)[:V]),
    }


def reference(xT, w1, w2, gate, offs, pos1, pos2, pos3):
    h = mxq(f64(w1), 0, "e4m3").T @ mxq(f64(xT)[:, unstriped(offs)], 0, "e4m3")
    z = sum(f64(gate)[d, :1] * h[:, unstriped(p)] for d, p in enumerate((pos1, pos2, pos3)))
    return mxq(f64(w2), 0, "e4m3").T @ mxq(z, 0, "e4m3")

@@ -1,0 +1,298 @@
+from contextlib import ExitStack
+
+import concourse.mybir as mybir
+from concourse.masks import make_identity
+
+F32 = mybir.dt.float32
+BF16 = mybir.dt.bfloat16
+U32 = mybir.dt.uint32
+U16 = mybir.dt.uint16
+U8 = mybir.dt.uint8
+FP8X4 = mybir.dt.float8_e4m3fn_x4
+COPY = mybir.ActivationFunctionType.Copy
+MULT = mybir.AluOpType.mult
+
+P = 128
+K, T, D, S, V, H, N = 1024, 1024, 3, 512, 256, 1024, 128
+PASSES = K // 512
+GROUPS = H // 512
+CHUNKS = ((0, 128), (128, 128), (256, 256), (512, 256), (768, 256))
+W1_CAST = ["ss","ss","sv","vs","vs"]
+
+FLOPS = 2 * K * H * S + 2 * H * N * V
+
+
+def tile_picked_sage_none_e_kernel(tc, xT, w1, w2, gate, offs, pos1, pos2, pos3, out):
+    nc = tc.nc
+    with ExitStack() as ctx:
+        lists = ctx.enter_context(tc.tile_pool(name="lists", bufs=1))
+        keep = ctx.enter_context(tc.tile_pool(name="keep", bufs=1))
+        picks = ctx.enter_context(tc.tile_pool(name="picks", bufs=4))
+        ps_h = ctx.enter_context(tc.psum_pool(name="ps_h", bufs=3))
+        ps_z = ctx.enter_context(tc.psum_pool(name="ps_z", bufs=2))
+        ps_1 = ctx.enter_context(tc.psum_pool(name="ps_1", bufs=1))
+
+        offs_t = lists.tile([P, S // 16], U16, name="offs_t")
+        pos_t = [lists.tile([P, V // 16], U16, name=f"pos_t{d}") for d in range(D)]
+        ident = keep.tile([P, P], F32, name="ident")
+        make_identity(nc, ident[:])
+
+        x_view = xT.rearrange("(s p u e) t -> s u p e t", s=PASSES, p=P, u=2, e=2)
+        w1_view = w1.rearrange("(s p j) c -> s p j c", s=PASSES, p=P, j=4)
+        x_raw, w1_raw = {}, {}
+        gate_t = keep.tile([P, D, V], F32, name="gate_t")
+
+        def load_x(s, u, parts):
+            w = T // parts
+            for n in range(parts):
+                t = keep.tile([P, 2, w], F32, name=f"x_raw{s}{u}{n}")
+                nc.sync.dma_start(t[:], x_view[s, u][:, :, n * w : (n + 1) * w])
+                x_raw[s, u, n] = t
+
+        def load_w1(c, s):
+            c0, width = CHUNKS[c]
+            t = keep.tile([P, 4, width], F32, name=f"w1_raw{c}{s}")
+            nc.sync.dma_start(t[:], w1_view[s][:, :, c0 : c0 + width])
+            w1_raw[c, s] = t
+
+        load_x(0, 0, 2)
+        nc.sync.dma_start(offs_t[:], offs)
+        load_w1(0, 0)
+        load_x(0, 1, 1)
+        load_w1(0, 1)
+        load_x(1, 0, 1)
+        load_x(1, 1, 2)
+        for d, src in enumerate((pos1, pos2, pos3)):
+            nc.sync.dma_start(pos_t[d][:], src)
+        load_w1(1, 0)
+        load_w1(1, 1)
+        nc.sync.dma_start(gate_t[:], gate.rearrange("d p v -> p d v"))
+        for c in (2, 3, 4):
+            for s in range(PASSES):
+                load_w1(c, s)
+        w2_raw = keep.tile([P, GROUPS, 4, N], F32, name="w2_raw")
+        nc.sync.dma_start(w2_raw[:], w2.rearrange("(g p j) n -> p g j n", g=GROUPS, j=4))
+
+        def cast4(engine, dst, src):
+            o = dst.rearrange("p (q i) j -> p q j i", i=4)
+            i = src.rearrange("p j (q i) -> p q j i", i=4)
+            if engine == "v":
+                nc.vector.tensor_copy(o, i)
+            else:
+                nc.scalar.activation(o, i, COPY)
+
+        x_codes, x_scales, xg = {}, {}, {}
+
+        def pick_pairs(s, u):
+            if u == 0:
+                xg[s] = keep.tile([P, S, 4], BF16, name=f"xg{s}", align_bytes=64)
+            xg_words = xg[s][:].rearrange("p n k -> p (n k)").bitcast(U32).rearrange("p (n u) -> p n u", u=2)
+            xb = keep.tile([P, T, 2], BF16, name=f"xb{s}{u}")
+            parts = 2 if (s, u, 1) in x_raw else 1
+            w = T // parts
+            for n in range(parts):
+                raw = x_raw[s, u, n]
+                mid = 0 if (s, u, n) == (1, 1, 1) else w * 3 // 4
+                for engine, a, b in (("s", mid, w), ("v", 0, mid)):
+                    if a == b:
+                        continue
+                    dst, src = xb[:, n * w + a : n * w + b, :], raw[:, :, a:b].rearrange("p e t -> p t e")
+                    if engine == "v":
+                        nc.vector.tensor_copy(dst, src)
+                    else:
+                        nc.scalar.activation(dst, src, COPY)
+            window = xb[:].rearrange("p t e -> p (t e)").bitcast(U32)
+            nc.vector.tensor_copy(xg_words[:, :, u], window.indirect(offs_t[:]))
+            if u == 1:
+                codes = keep.tile([P, S], U32, name=f"x_codes{s}", align_bytes=64)
+                scales = keep.tile([P, S], U8, name=f"x_scales{s}", align_bytes=64)
+                nc.vector.quantize_mx(
+                    out=codes[:].bitcast(FP8X4), scales=scales[:], in_=xg[s][:].rearrange("p n k -> p (n k)")
+                )
+                x_codes[s], x_scales[s] = codes, scales
+
+        w1_codes, w1_scales, h_tiles, z_codes = {}, {}, {}, {}
+
+        def quantise_w1(c):
+            start, width = CHUNKS[c]
+            grouped = keep.tile([P, PASSES, width, 4], BF16, name=f"w1_g{c}", align_bytes=64)
+            codes = keep.tile([P, PASSES, width], U32, name=f"w1_codes{c}", align_bytes=64)
+            scales = keep.tile([P, PASSES, width], U8, name=f"w1_scales{c}", align_bytes=64)
+            for s in range(PASSES):
+                cast4(W1_CAST[c][s], grouped[:, s], w1_raw[c, s][:])
+            nc.vector.quantize_mx(
+                out=codes[:].rearrange("p s n -> p (s n)").bitcast(FP8X4),
+                scales=scales[:].rearrange("p s n -> p (s n)"),
+                in_=grouped[:].rearrange("p s n k -> p (s n k)"),
+            )
+            w1_codes[c], w1_scales[c] = codes, scales
+
+        def project(c):
+            start, width = CHUNKS[c]
+            for first in range(0, width, P):
+                r = (start + first) // P
+                cols = slice(first, first + P)
+                acc = ps_h.tile([P, S], F32, name="acc")
+                for s in range(PASSES):
+                    nc.tensor.matmul_mx(
+                        out=acc[:],
+                        lhsT=w1_codes[c][:, s, cols].bitcast(FP8X4),
+                        lhsT_scale=w1_scales[c][:, s, cols],
+                        rhs=x_codes[s][:].bitcast(FP8X4),
+                        rhs_scale=x_scales[s][:],
+                        start=(s == 0),
+                        stop=(s == PASSES - 1),
+                    )
+                h = keep.tile([P, S], F32, name=f"h{r}")
+                nc.scalar.activation(h[:], acc[:], COPY)
+                h_tiles[r] = h
+
+        def project_first():
+            h = keep.tile([P, S], F32, name="h0")
+            for a in range(2):
+                part = slice(a * 256, a * 256 + 256)
+                acc = ps_h.tile([P, S], F32, name="acc")
+                for s in range(PASSES):
+                    nc.tensor.matmul_mx(
+                        out=acc[:, 0:256],
+                        lhsT=w1_codes[0][:, s, :].bitcast(FP8X4),
+                        lhsT_scale=w1_scales[0][:, s, :],
+                        rhs=x_codes[s][:, part].bitcast(FP8X4),
+                        rhs_scale=x_scales[s][:, part],
+                        start=(s == 0),
+                        stop=(s == PASSES - 1),
+                    )
+                nc.scalar.activation(h[:, part], acc[:, 0:256], COPY)
+            h_tiles[0] = h
+
+        zT = keep.tile([P, 2, H], BF16, name="zT")
+        w2_c = keep.tile([P, GROUPS, N], U32, name="w2_c", align_bytes=64)
+        w2_s = keep.tile([P, GROUPS, N], U8, name="w2_s", align_bytes=64)
+
+        def pick_h(r, d):
+            g = picks.tile([P, V], F32, name=f"picked{d}")
+            nc.vector.tensor_tensor(g[:], h_tiles[r][:].indirect(pos_t[d][:]), gate_t[:, d, :], MULT)
+            return g
+
+        def add_turned(dst, g, vh, d):
+            nc.tensor.matmul(
+                dst, g[:, vh * P : vh * P + P], ident[:], start=(d == 0), stop=(d == D - 1), is_transpose=True
+            )
+
+        def aggregate(rows):
+            zps = ps_z.tile([P, 2, len(rows), P], F32, name="zps")
+            for n, r in enumerate(rows):
+                picked = [pick_h(r, d) for d in range(D)]
+                for vh in range(2):
+                    for d in range(D):
+                        add_turned(zps[:, vh, n, :], picked[d], vh, d)
+            first, last = rows[0] * P, rows[-1] * P + P
+            nc.scalar.activation(zT[:, :, first:last], zps[:].rearrange("p h r i -> p h (r i)"), COPY)
+
+        def second_operand(g):
+            zw = ps_1.tile([P, 2, 2, P], F32, name="zw")
+            for vh in range(2):
+                words = zT[:, vh, g * 512 : (g + 1) * 512].bitcast(F32)
+                for u in range(2):
+                    nc.tensor.transpose(zw[:, vh, u, :], words[:, u::2], ident[:])
+            zq = keep.tile([P, 2, P, 4], BF16, name="zq", align_bytes=64)
+            zq_words = zq[:].rearrange("p h v k -> p (h v k)").bitcast(F32)
+            nc.scalar.copy(
+                zq_words.rearrange("p (h v u) -> p h v u", h=2, u=2), zw[:].rearrange("p h u v -> p h v u")
+            )
+            zc = keep.tile([P, V], U32, name="zc", align_bytes=64)
+            zs = keep.tile([P, V], U8, name="zs", align_bytes=64)
+            nc.vector.quantize_mx(
+                out=zc[:].bitcast(FP8X4), scales=zs[:], in_=zq[:].rearrange("p h v k -> p (h v k)")
+            )
+            for vh in range(2):
+                z_codes[g, vh] = (zc[:, vh * P : vh * P + P], zs[:, vh * P : vh * P + P])
+
+        def weights2():
+            w2_g = keep.tile([P, GROUPS, N, 4], BF16, name="w2_g", align_bytes=64)
+            for g in range(GROUPS):
+                cast4("s", w2_g[:, g], w2_raw[:, g])
+            nc.vector.quantize_mx(
+                out=w2_c[:].rearrange("p g n -> p (g n)").bitcast(FP8X4),
+                scales=w2_s[:].rearrange("p g n -> p (g n)"),
+                in_=w2_g[:].rearrange("p g n k -> p (g n k)"),
+            )
+
+        def tail():
+            r = H // P - 1
+            banks = [ps_h.tile([P, S], F32, name="acc") for vh in range(2)]
+            for vh in range(2):
+                for d in range(D):
+                    g = picks.tile([P, P], F32, name=f"half{d}")
+                    part = pos_t[d][:, vh * (P // 16) : (vh + 1) * (P // 16)]
+                    nc.vector.tensor_tensor(
+                        g[:], h_tiles[r][:].indirect(part), gate_t[:, d, vh * P : vh * P + P], MULT
+                    )
+                    nc.tensor.matmul(
+                        banks[vh][:, 0:P], g[:], ident[:], start=(d == 0), stop=(d == D - 1), is_transpose=True
+                    )
+            for vh in range(2):
+                dst, src = zT[:, vh, r * P : r * P + P], banks[vh][:, 0:P]
+                if vh == 0:
+                    nc.scalar.activation(dst, src, COPY)
+                else:
+                    nc.vector.tensor_copy(dst, src)
+            res = keep.tile([N, V], F32, name="res")
+            for vh in range(2):
+                zw = ps_h.tile([P, S], F32, name="acc")
+                words = zT[:, vh, 512:1024].bitcast(F32)
+                for u in range(2):
+                    nc.tensor.transpose(zw[:, u * P : u * P + P], words[:, u::2], ident[:])
+                zq = keep.tile([P, P, 4], BF16, name=f"zq_tail{vh}", align_bytes=64)
+                dst = zq[:].rearrange("p v k -> p (v k)").bitcast(F32).rearrange("p (v u) -> p v u", u=2)
+                src = zw[:, 0 : 2 * P].rearrange("p (u v) -> p v u", u=2)
+                if vh == 0:
+                    nc.scalar.copy(dst, src)
+                else:
+                    nc.vector.tensor_copy(dst, src)
+                zc = keep.tile([P, P], U32, name=f"zc_tail{vh}", align_bytes=64)
+                zs = keep.tile([P, P], U8, name=f"zs_tail{vh}", align_bytes=64)
+                nc.vector.quantize_mx(
+                    out=zc[:].bitcast(FP8X4), scales=zs[:], in_=zq[:].rearrange("p v k -> p (v k)")
+                )
+                z_codes[1, vh] = (zc[:], zs[:])
+                acc_o = ps_1.tile([N, P], F32, name=f"acc_o{vh}")
+                for g in range(GROUPS):
+                    zc, zs = z_codes[g, vh]
+                    nc.tensor.matmul_mx(
+                        out=acc_o[:],
+                        lhsT=w2_c[:, g, :].bitcast(FP8X4),
+                        lhsT_scale=w2_s[:, g, :],
+                        rhs=zc.bitcast(FP8X4),
+                        rhs_scale=zs,
+                        start=(g == 0),
+                        stop=(g == GROUPS - 1),
+                    )
+                cols = slice(vh * P, vh * P + P)
+                if vh == 0:
+                    nc.scalar.activation(res[:, cols], acc_o[:], COPY)
+                else:
+                    nc.vector.tensor_copy(res[:, cols], acc_o[:])
+                nc.sync.dma_start(out[:, cols], res[:, cols])
+
+        pick_pairs(0, 0)
+        quantise_w1(0)
+        pick_pairs(0, 1)
+        pick_pairs(1, 0)
+        pick_pairs(1, 1)
+        project_first()
+        quantise_w1(1)
+        quantise_w1(2)
+        project(1)
+        project(2)
+        quantise_w1(3)
+        aggregate((0, 1))
+        project(3)
+        weights2()
+        quantise_w1(4)
+        aggregate((2, 3))
+        project(4)
+        aggregate((4, 5))
+        aggregate((6,))
+        second_operand(0)
+        tail()

@@ -16,8 +16,13 @@ P = 128
 K, T, D, S, V, H, N = 1024, 1024, 3, 512, 256, 1024, 128
 PASSES = K // 512
 GROUPS = H // 512
-CHUNKS = ((0, 128), (128, 128), (256, 256), (512, 256), (768, 256))
-W1_CAST = ["ss","ss","sv","vs","vs"]
+ROWS = H // P
+HALF = S // 2
+X_PIECES = ((0, 0, 512, 128), (0, 512, 512, 320), (1, 0, 256, 0), (1, 256, 256, 0), (1, 512, 256, 96), (1, 768, 256, 160))
+W1_CHUNKS = tuple((r, 1) for r in range(ROWS))
+HELD = {(0, 2): 2, (1, 1): 3}
+H_AFTER = {1: 2, 2: 4, 3: 5, 4: 6, 5: 7}
+REGION = 3072
 
 FLOPS = 2 * K * H * S + 2 * H * N * V
 
@@ -27,7 +32,8 @@ def tile_picked_sage_none_e_kernel(tc, xT, w1, w2, gate, offs, pos1, pos2, pos3,
     with ExitStack() as ctx:
         lists = ctx.enter_context(tc.tile_pool(name="lists", bufs=1))
         keep = ctx.enter_context(tc.tile_pool(name="keep", bufs=1))
-        picks = ctx.enter_context(tc.tile_pool(name="picks", bufs=4))
+        share = ctx.enter_context(tc.tile_pool(name="share", bufs=1))
+        picks = ctx.enter_context(tc.tile_pool(name="picks", bufs=3))
         ps_h = ctx.enter_context(tc.psum_pool(name="ps_h", bufs=3))
         ps_z = ctx.enter_context(tc.psum_pool(name="ps_z", bufs=2))
         ps_1 = ctx.enter_context(tc.psum_pool(name="ps_1", bufs=1))
@@ -36,40 +42,41 @@ def tile_picked_sage_none_e_kernel(tc, xT, w1, w2, gate, offs, pos1, pos2, pos3,
         pos_t = [lists.tile([P, V // 16], U16, name=f"pos_t{d}") for d in range(D)]
         ident = keep.tile([P, P], F32, name="ident")
         make_identity(nc, ident[:])
+        all_scales = keep.tile([P, T], U8, name="all_scales", align_bytes=64)
+        nc.gpsimd.memset(all_scales[:], 0)
 
-        x_view = xT.rearrange("(s p u e) t -> s u p e t", s=PASSES, p=P, u=2, e=2)
+        x_view = xT.rearrange("(s p j) t -> s p j t", s=PASSES, p=P, j=4)
         w1_view = w1.rearrange("(s p j) c -> s p j c", s=PASSES, p=P, j=4)
-        x_raw, w1_raw = {}, {}
+        x_raw, w1_raw = [], {}
         gate_t = keep.tile([P, D, V], F32, name="gate_t")
 
-        def load_x(s, u, parts):
-            w = T // parts
-            for n in range(parts):
-                t = keep.tile([P, 2, w], F32, name=f"x_raw{s}{u}{n}")
-                nc.sync.dma_start(t[:], x_view[s, u][:, :, n * w : (n + 1) * w])
-                x_raw[s, u, n] = t
+        def load_x(n):
+            s, first, count, vshare = X_PIECES[n]
+            t = keep.tile([P, 4, count], F32, name=f"x_raw{n}")
+            nc.sync.dma_start(t[:], x_view[s][:, :, first : first + count])
+            x_raw.append(t)
 
-        def load_w1(c, s):
-            c0, width = CHUNKS[c]
-            t = keep.tile([P, 4, width], F32, name=f"w1_raw{c}{s}")
-            nc.sync.dma_start(t[:], w1_view[s][:, :, c0 : c0 + width])
-            w1_raw[c, s] = t
+        def load_w1(c):
+            r0, rows = W1_CHUNKS[c]
+            for s in range(PASSES):
+                if s == 0:
+                    t = keep.tile([P, 4, rows * P], F32, name=f"w1_raw{c}{s}")
+                else:
+                    t = share.tile([P, 4, rows * P], F32, name=f"w1_raw{c}{s}", offset=c * REGION, align_bytes=64)
+                nc.sync.dma_start(t[:], w1_view[s][:, :, r0 * P : (r0 + rows) * P])
+                w1_raw[c, s] = t
 
-        load_x(0, 0, 2)
+        load_x(0)
         nc.sync.dma_start(offs_t[:], offs)
-        load_w1(0, 0)
-        load_x(0, 1, 1)
-        load_w1(0, 1)
-        load_x(1, 0, 1)
-        load_x(1, 1, 2)
         for d, src in enumerate((pos1, pos2, pos3)):
             nc.sync.dma_start(pos_t[d][:], src)
-        load_w1(1, 0)
-        load_w1(1, 1)
+        for n in range(1, len(X_PIECES)):
+            load_x(n)
+        load_w1(0)
+        load_w1(1)
         nc.sync.dma_start(gate_t[:], gate.rearrange("d p v -> p d v"))
-        for c in (2, 3, 4):
-            for s in range(PASSES):
-                load_w1(c, s)
+        for c in range(2, len(W1_CHUNKS)):
+            load_w1(c)
         w2_raw = keep.tile([P, GROUPS, 4, N], F32, name="w2_raw")
         nc.sync.dma_start(w2_raw[:], w2.rearrange("(g p j) n -> p g j n", g=GROUPS, j=4))
 
@@ -81,120 +88,117 @@ def tile_picked_sage_none_e_kernel(tc, xT, w1, w2, gate, offs, pos1, pos2, pos3,
             else:
                 nc.scalar.activation(o, i, COPY)
 
-        x_codes, x_scales, xg = {}, {}, {}
+        all_codes = [keep.tile([P, T], U32, name=f"all_codes{s}", align_bytes=64) for s in range(PASSES)]
+        x_codes, x_scales = {}, {}
 
-        def pick_pairs(s, u):
-            if u == 0:
-                xg[s] = keep.tile([P, S, 4], BF16, name=f"xg{s}", align_bytes=64)
-            xg_words = xg[s][:].rearrange("p n k -> p (n k)").bitcast(U32).rearrange("p (n u) -> p n u", u=2)
-            xb = keep.tile([P, T, 2], BF16, name=f"xb{s}{u}")
-            parts = 2 if (s, u, 1) in x_raw else 1
-            w = T // parts
-            for n in range(parts):
-                raw = x_raw[s, u, n]
-                mid = 0 if (s, u, n) == (1, 1, 1) else w * 3 // 4
-                for engine, a, b in (("s", mid, w), ("v", 0, mid)):
-                    if a == b:
-                        continue
-                    dst, src = xb[:, n * w + a : n * w + b, :], raw[:, :, a:b].rearrange("p e t -> p t e")
-                    if engine == "v":
-                        nc.vector.tensor_copy(dst, src)
-                    else:
-                        nc.scalar.activation(dst, src, COPY)
-            window = xb[:].rearrange("p t e -> p (t e)").bitcast(U32)
-            nc.vector.tensor_copy(xg_words[:, :, u], window.indirect(offs_t[:]))
-            if u == 1:
-                codes = keep.tile([P, S], U32, name=f"x_codes{s}", align_bytes=64)
-                scales = keep.tile([P, S], U8, name=f"x_scales{s}", align_bytes=64)
-                nc.vector.quantize_mx(
-                    out=codes[:].bitcast(FP8X4), scales=scales[:], in_=xg[s][:].rearrange("p n k -> p (n k)")
-                )
-                x_codes[s], x_scales[s] = codes, scales
+        def quantise_x(n):
+            s, first, count, vshare = X_PIECES[n]
+            grouped = keep.tile([P, count, 4], BF16, name=f"x_g{n}", align_bytes=64)
+            cast4("s", grouped[:, vshare:count], x_raw[n][:, :, vshare:count])
+            if vshare:
+                cast4("v", grouped[:, 0:vshare], x_raw[n][:, :, 0:vshare])
+            nc.vector.quantize_mx(
+                out=all_codes[s][:, first : first + count].bitcast(FP8X4),
+                scales=all_scales[4 * s : P, first : first + count],
+                in_=grouped[:].rearrange("p n k -> p (n k)"),
+            )
 
-        w1_codes, w1_scales, h_tiles, z_codes = {}, {}, {}, {}
+        def pick_codes(s, a, b, held):
+            if held:
+                codes = share.tile([P, b - a], U32, name=f"x_codes{s}{a}", offset=0, align_bytes=64)
+            else:
+                codes = keep.tile([P, b - a], U32, name=f"x_codes{s}{a}", align_bytes=64)
+            nc.vector.tensor_copy(codes[:], all_codes[s][:].indirect(offs_t[:, a // 16 : b // 16]))
+            for part in range(a // HALF, b // HALF):
+                x_codes[s, part] = codes[:, part * HALF - a : part * HALF - a + HALF]
+
+        def pick_scales(part):
+            if part == 1:
+                scales = share.tile([P, HALF], U8, name=f"x_scales{part}", offset=1024, align_bytes=64)
+            else:
+                scales = keep.tile([P, HALF], U8, name=f"x_scales{part}", align_bytes=64)
+            a = part * HALF // 16
+            nc.vector.tensor_copy(scales[:], all_scales[:].indirect(offs_t[:, a : a + HALF // 16]))
+            x_scales[part] = scales
+
+        w1_codes, w1_scales, h_tiles, accs, z_codes = {}, {}, {}, {}, {}
 
         def quantise_w1(c):
-            start, width = CHUNKS[c]
-            grouped = keep.tile([P, PASSES, width, 4], BF16, name=f"w1_g{c}", align_bytes=64)
-            codes = keep.tile([P, PASSES, width], U32, name=f"w1_codes{c}", align_bytes=64)
-            scales = keep.tile([P, PASSES, width], U8, name=f"w1_scales{c}", align_bytes=64)
+            r0, rows = W1_CHUNKS[c]
+            grouped = keep.tile([P, PASSES, rows * P, 4], BF16, name=f"w1_g{c}", align_bytes=64)
+            codes = keep.tile([P, PASSES, rows * P], U32, name=f"w1_codes{c}", align_bytes=64)
+            scales = keep.tile([P, PASSES, rows * P], U8, name=f"w1_scales{c}", align_bytes=64)
             for s in range(PASSES):
-                cast4(W1_CAST[c][s], grouped[:, s], w1_raw[c, s][:])
+                cast4("s", grouped[:, s], w1_raw[c, s][:])
             nc.vector.quantize_mx(
                 out=codes[:].rearrange("p s n -> p (s n)").bitcast(FP8X4),
                 scales=scales[:].rearrange("p s n -> p (s n)"),
                 in_=grouped[:].rearrange("p s n k -> p (s n k)"),
             )
-            w1_codes[c], w1_scales[c] = codes, scales
+            for n in range(rows):
+                w1_codes[r0 + n] = codes[:, :, n * P : n * P + P]
+                w1_scales[r0 + n] = scales[:, :, n * P : n * P + P]
 
-        def project(c):
-            start, width = CHUNKS[c]
-            for first in range(0, width, P):
-                r = (start + first) // P
-                cols = slice(first, first + P)
-                acc = ps_h.tile([P, S], F32, name="acc")
-                for s in range(PASSES):
-                    nc.tensor.matmul_mx(
-                        out=acc[:],
-                        lhsT=w1_codes[c][:, s, cols].bitcast(FP8X4),
-                        lhsT_scale=w1_scales[c][:, s, cols],
-                        rhs=x_codes[s][:].bitcast(FP8X4),
-                        rhs_scale=x_scales[s][:],
-                        start=(s == 0),
-                        stop=(s == PASSES - 1),
-                    )
-                h = keep.tile([P, S], F32, name=f"h{r}")
-                nc.scalar.activation(h[:], acc[:], COPY)
-                h_tiles[r] = h
+        def project(r, part):
+            if part == 0 or r == 0:
+                accs[r, part] = ps_h.tile([P, S], F32, name="acc")
+            else:
+                accs[r, part] = accs[r, 0]
+            for s in range(PASSES):
+                nc.tensor.matmul_mx(
+                    out=accs[r, part][:, part * HALF : part * HALF + HALF],
+                    lhsT=w1_codes[r][:, s, :].bitcast(FP8X4),
+                    lhsT_scale=w1_scales[r][:, s, :],
+                    rhs=x_codes[s, part].bitcast(FP8X4),
+                    rhs_scale=x_scales[part][4 * s : P, :],
+                    start=(s == 0),
+                    stop=(s == PASSES - 1),
+                )
 
-        def project_first():
-            h = keep.tile([P, S], F32, name="h0")
-            for a in range(2):
-                part = slice(a * 256, a * 256 + 256)
-                acc = ps_h.tile([P, S], F32, name="acc")
-                for s in range(PASSES):
-                    nc.tensor.matmul_mx(
-                        out=acc[:, 0:256],
-                        lhsT=w1_codes[0][:, s, :].bitcast(FP8X4),
-                        lhsT_scale=w1_scales[0][:, s, :],
-                        rhs=x_codes[s][:, part].bitcast(FP8X4),
-                        rhs_scale=x_scales[s][:, part],
-                        start=(s == 0),
-                        stop=(s == PASSES - 1),
-                    )
-                nc.scalar.activation(h[:, part], acc[:, 0:256], COPY)
-            h_tiles[0] = h
+        def fetch_h(r, a, b):
+            if a == 0 and r in H_AFTER:
+                h_tiles[r] = share.tile([P, S], F32, name=f"h{r}", offset=H_AFTER[r] * REGION + 1024)
+            elif a == 0:
+                h_tiles[r] = keep.tile([P, S], F32, name=f"h{r}")
+            nc.scalar.activation(h_tiles[r][:, a:b], accs[r, a // HALF][:, a:b], COPY)
 
-        zT = keep.tile([P, 2, H], BF16, name="zT")
+        zT = {(g, vh): keep.tile([P, 2, P, 2], BF16, name=f"zT{g}{vh}") for g in range(GROUPS) for vh in range(2)}
         w2_c = keep.tile([P, GROUPS, N], U32, name="w2_c", align_bytes=64)
         w2_s = keep.tile([P, GROUPS, N], U8, name="w2_s", align_bytes=64)
+        z_banks = {}
 
         def pick_h(r, d):
-            g = picks.tile([P, V], F32, name=f"picked{d}")
-            nc.vector.tensor_tensor(g[:], h_tiles[r][:].indirect(pos_t[d][:]), gate_t[:, d, :], MULT)
-            return g
-
-        def add_turned(dst, g, vh, d):
-            nc.tensor.matmul(
-                dst, g[:, vh * P : vh * P + P], ident[:], start=(d == 0), stop=(d == D - 1), is_transpose=True
-            )
-
-        def aggregate(rows):
-            zps = ps_z.tile([P, 2, len(rows), P], F32, name="zps")
-            for n, r in enumerate(rows):
-                picked = [pick_h(r, d) for d in range(D)]
+            if r % 4 == 0 and d == 0:
                 for vh in range(2):
-                    for d in range(D):
-                        add_turned(zps[:, vh, n, :], picked[d], vh, d)
-            first, last = rows[0] * P, rows[-1] * P + P
-            nc.scalar.activation(zT[:, :, first:last], zps[:].rearrange("p h r i -> p h (r i)"), COPY)
+                    z_banks[r // 4, vh] = ps_z.tile([P, 512], F32, name=f"zps{vh}")
+            if (r, d) in HELD:
+                g = share.tile([P, V], F32, name=f"held{r}", offset=HELD[r, d] * REGION)
+            else:
+                g = picks.tile([P, V], F32, name=f"picked{d}")
+            nc.vector.tensor_tensor(g[:], h_tiles[r][:].indirect(pos_t[d][:]), gate_t[:, d, :], MULT)
+            for vh in range(2):
+                dst = z_banks[r // 4, vh][:, (r % 4) * P : (r % 4) * P + P]
+                nc.tensor.matmul(
+                    dst, g[:, vh * P : vh * P + P], ident[:], start=(d == 0), stop=(d == D - 1), is_transpose=True
+                )
+
+        def round_z(engine, g, vh, bank, first, rows):
+            dst = zT[g, vh][:, :, 32 * first : 32 * (first + rows), :]
+            src = bank.rearrange("v (p u e) -> v u p e", u=2, e=2)
+            if engine == "v":
+                nc.vector.tensor_copy(dst, src)
+            else:
+                nc.scalar.activation(dst, src, COPY)
+
+        def turn_back(dst, g, vh, u):
+            words = zT[g, vh][:].rearrange("v u p e -> v (u p e)").bitcast(F32)
+            nc.tensor.transpose(dst, words[:, u * P : u * P + P], ident[:])
 
         def second_operand(g):
             zw = ps_1.tile([P, 2, 2, P], F32, name="zw")
             for vh in range(2):
-                words = zT[:, vh, g * 512 : (g + 1) * 512].bitcast(F32)
                 for u in range(2):
-                    nc.tensor.transpose(zw[:, vh, u, :], words[:, u::2], ident[:])
+                    turn_back(zw[:, vh, u, :], g, vh, u)
             zq = keep.tile([P, 2, P, 4], BF16, name="zq", align_bytes=64)
             zq_words = zq[:].rearrange("p h v k -> p (h v k)").bitcast(F32)
             nc.scalar.copy(
@@ -219,7 +223,7 @@ def tile_picked_sage_none_e_kernel(tc, xT, w1, w2, gate, offs, pos1, pos2, pos3,
             )
 
         def tail():
-            r = H // P - 1
+            r = ROWS - 1
             banks = [ps_h.tile([P, S], F32, name="acc") for vh in range(2)]
             for vh in range(2):
                 for d in range(D):
@@ -232,17 +236,12 @@ def tile_picked_sage_none_e_kernel(tc, xT, w1, w2, gate, offs, pos1, pos2, pos3,
                         banks[vh][:, 0:P], g[:], ident[:], start=(d == 0), stop=(d == D - 1), is_transpose=True
                     )
             for vh in range(2):
-                dst, src = zT[:, vh, r * P : r * P + P], banks[vh][:, 0:P]
-                if vh == 0:
-                    nc.scalar.activation(dst, src, COPY)
-                else:
-                    nc.vector.tensor_copy(dst, src)
+                round_z("sv"[vh], 1, vh, banks[vh][:, 0:P], 3, 1)
             res = keep.tile([N, V], F32, name="res")
             for vh in range(2):
-                zw = ps_h.tile([P, S], F32, name="acc")
-                words = zT[:, vh, 512:1024].bitcast(F32)
+                zw = ps_z.tile([P, 512], F32, name=f"zps{vh}")
                 for u in range(2):
-                    nc.tensor.transpose(zw[:, u * P : u * P + P], words[:, u::2], ident[:])
+                    turn_back(zw[:, u * P : u * P + P], 1, vh, u)
                 zq = keep.tile([P, P, 4], BF16, name=f"zq_tail{vh}", align_bytes=64)
                 dst = zq[:].rearrange("p v k -> p (v k)").bitcast(F32).rearrange("p (v u) -> p v u", u=2)
                 src = zw[:, 0 : 2 * P].rearrange("p (u v) -> p v u", u=2)
@@ -256,11 +255,11 @@ def tile_picked_sage_none_e_kernel(tc, xT, w1, w2, gate, offs, pos1, pos2, pos3,
                     out=zc[:].bitcast(FP8X4), scales=zs[:], in_=zq[:].rearrange("p v k -> p (v k)")
                 )
                 z_codes[1, vh] = (zc[:], zs[:])
-                acc_o = ps_1.tile([N, P], F32, name=f"acc_o{vh}")
+                acc_o = ps_h.tile([P, S], F32, name="acc")
                 for g in range(GROUPS):
                     zc, zs = z_codes[g, vh]
                     nc.tensor.matmul_mx(
-                        out=acc_o[:],
+                        out=acc_o[:, 0:P],
                         lhsT=w2_c[:, g, :].bitcast(FP8X4),
                         lhsT_scale=w2_s[:, g, :],
                         rhs=zc.bitcast(FP8X4),
@@ -270,29 +269,53 @@ def tile_picked_sage_none_e_kernel(tc, xT, w1, w2, gate, offs, pos1, pos2, pos3,
                     )
                 cols = slice(vh * P, vh * P + P)
                 if vh == 0:
-                    nc.scalar.activation(res[:, cols], acc_o[:], COPY)
+                    nc.scalar.activation(res[:, cols], acc_o[:, 0:P], COPY)
                 else:
-                    nc.vector.tensor_copy(res[:, cols], acc_o[:])
+                    nc.vector.tensor_copy(res[:, cols], acc_o[:, 0:P])
                 nc.sync.dma_start(out[:, cols], res[:, cols])
 
-        pick_pairs(0, 0)
+        for n in range(len(X_PIECES)):
+            quantise_x(n)
+            if n == 1:
+                pick_codes(0, 0, S, False)
+        pick_codes(1, 0, HALF, False)
+        pick_scales(0)
         quantise_w1(0)
-        pick_pairs(0, 1)
-        pick_pairs(1, 0)
-        pick_pairs(1, 1)
-        project_first()
-        quantise_w1(1)
-        quantise_w1(2)
-        project(1)
-        project(2)
-        quantise_w1(3)
-        aggregate((0, 1))
-        project(3)
-        weights2()
-        quantise_w1(4)
-        aggregate((2, 3))
-        project(4)
-        aggregate((4, 5))
-        aggregate((6,))
-        second_operand(0)
+        project(0, 0)
+        fetch_h(0, 0, HALF)
+        pick_codes(1, HALF, S, True)
+        pick_scales(1)
+        project(0, 1)
+        fetch_h(0, HALF, S)
+
+        def weights1(r):
+            quantise_w1(r)
+            project(r, 0)
+            project(r, 1)
+
+        weights1(1)
+        pick_h(0, 0)
+        pick_h(0, 1)
+        weights1(2)
+        fetch_h(1, 0, S)
+        pick_h(0, 2)
+        pick_h(1, 0)
+        weights1(3)
+        pick_h(1, 1)
+        pick_h(1, 2)
+        for r in range(2, ROWS - 1):
+            if r + 2 < ROWS:
+                weights1(r + 2)
+            fetch_h(r, 0, S)
+            if r == 5:
+                for vh in range(2):
+                    round_z("s", 0, vh, z_banks[0, vh][:], 0, 4)
+            if r == 6:
+                fetch_h(7, 0, S)
+                weights2()
+                second_operand(0)
+            for d in range(D):
+                pick_h(r, d)
+        for vh in range(2):
+            round_z("s", 1, vh, z_banks[1, vh][:, 0 : 3 * P], 0, 3)
         tail()

@@ -20,8 +20,10 @@ ROWS = H // P
 HALF = S // 2
 X_PIECES = ((0, 0, 512, 128), (0, 512, 512, 320), (1, 0, 256, 0), (1, 256, 256, 0), (1, 512, 256, 96), (1, 768, 256, 160))
 W1_CHUNKS = tuple((r, 1) for r in range(ROWS))
-HELD = {(0, 2): 2, (1, 1): 3}
-H_AFTER = {1: 2, 2: 4, 3: 5, 4: 6, 5: 7}
+LAST0 = 1
+PARTS = ((0, 256), (256, 384), (384, 512))
+HELD = {(r, 2): r + 2 for r in range(ROWS - 2)}
+H_AFTER = {r: r + 1 for r in range(1, ROWS - 1)}
 REGION = 3072
 
 FLOPS = 2 * K * H * S + 2 * H * N * V
@@ -67,14 +69,15 @@ def tile_picked_sage_none_e_kernel(tc, xT, w1, w2, gate, offs, pos1, pos2, pos3,
                 w1_raw[c, s] = t
 
         load_x(0)
+        load_x(1)
         nc.sync.dma_start(offs_t[:], offs)
+        for n in range(2, len(X_PIECES)):
+            load_x(n)
+        for c in range(2):
+            load_w1(c)
+        nc.sync.dma_start(gate_t[:], gate.rearrange("d p v -> p d v"))
         for d, src in enumerate((pos1, pos2, pos3)):
             nc.sync.dma_start(pos_t[d][:], src)
-        for n in range(1, len(X_PIECES)):
-            load_x(n)
-        load_w1(0)
-        load_w1(1)
-        nc.sync.dma_start(gate_t[:], gate.rearrange("d p v -> p d v"))
         for c in range(2, len(W1_CHUNKS)):
             load_w1(c)
         w2_raw = keep.tile([P, GROUPS, 4, N], F32, name="w2_raw")
@@ -89,7 +92,6 @@ def tile_picked_sage_none_e_kernel(tc, xT, w1, w2, gate, offs, pos1, pos2, pos3,
                 nc.scalar.activation(o, i, COPY)
 
         all_codes = [keep.tile([P, T], U32, name=f"all_codes{s}", align_bytes=64) for s in range(PASSES)]
-        x_codes, x_scales = {}, {}
 
         def quantise_x(n):
             s, first, count, vshare = X_PIECES[n]
@@ -103,23 +105,26 @@ def tile_picked_sage_none_e_kernel(tc, xT, w1, w2, gate, offs, pos1, pos2, pos3,
                 in_=grouped[:].rearrange("p n k -> p (n k)"),
             )
 
-        def pick_codes(s, a, b, held):
-            if held:
-                codes = share.tile([P, b - a], U32, name=f"x_codes{s}{a}", offset=0, align_bytes=64)
-            else:
-                codes = keep.tile([P, b - a], U32, name=f"x_codes{s}{a}", align_bytes=64)
-            nc.vector.tensor_copy(codes[:], all_codes[s][:].indirect(offs_t[:, a // 16 : b // 16]))
-            for part in range(a // HALF, b // HALF):
-                x_codes[s, part] = codes[:, part * HALF - a : part * HALF - a + HALF]
+        codes0 = keep.tile([P, S], U32, name="codes0", align_bytes=64)
+        codes1 = [
+            keep.tile([P, HALF], U32, name="codes1a", align_bytes=64),
+            share.tile([P, HALF], U32, name="codes1b", offset=0, align_bytes=64),
+        ]
+        x_scales = [
+            keep.tile([P, HALF], U8, name="scales_a", align_bytes=64),
+            share.tile([P, HALF], U8, name="scales_b", offset=1024, align_bytes=64),
+        ]
 
-        def pick_scales(part):
-            if part == 1:
-                scales = share.tile([P, HALF], U8, name=f"x_scales{part}", offset=1024, align_bytes=64)
-            else:
-                scales = keep.tile([P, HALF], U8, name=f"x_scales{part}", align_bytes=64)
-            a = part * HALF // 16
-            nc.vector.tensor_copy(scales[:], all_scales[:].indirect(offs_t[:, a : a + HALF // 16]))
-            x_scales[part] = scales
+        def x_operand(s, a, b):
+            part, first = divmod(a, HALF)
+            codes = codes0[:, a:b] if s == 0 else codes1[part][:, first : first + b - a]
+            return codes, x_scales[part][:, first : first + b - a]
+
+        def pick_codes(s, a, b):
+            nc.vector.tensor_copy(x_operand(s, a, b)[0], all_codes[s][:].indirect(offs_t[:, a // 16 : b // 16]))
+
+        def pick_scales(a, b):
+            nc.vector.tensor_copy(x_operand(1, a, b)[1], all_scales[:].indirect(offs_t[:, a // 16 : b // 16]))
 
         w1_codes, w1_scales, h_tiles, accs, z_codes = {}, {}, {}, {}, {}
 
@@ -139,18 +144,17 @@ def tile_picked_sage_none_e_kernel(tc, xT, w1, w2, gate, offs, pos1, pos2, pos3,
                 w1_codes[r0 + n] = codes[:, :, n * P : n * P + P]
                 w1_scales[r0 + n] = scales[:, :, n * P : n * P + P]
 
-        def project(r, part):
-            if part == 0 or r == 0:
-                accs[r, part] = ps_h.tile([P, S], F32, name="acc")
-            else:
-                accs[r, part] = accs[r, 0]
+        def project(r, a, b):
+            if a == 0 or r == 0:
+                accs[r] = ps_h.tile([P, S], F32, name="acc")
             for s in range(PASSES):
+                codes, scales = x_operand(s, a, b)
                 nc.tensor.matmul_mx(
-                    out=accs[r, part][:, part * HALF : part * HALF + HALF],
+                    out=accs[r][:, a:b],
                     lhsT=w1_codes[r][:, s, :].bitcast(FP8X4),
                     lhsT_scale=w1_scales[r][:, s, :],
-                    rhs=x_codes[s, part].bitcast(FP8X4),
-                    rhs_scale=x_scales[part][4 * s : P, :],
+                    rhs=codes.bitcast(FP8X4),
+                    rhs_scale=scales[4 * s : P, :],
                     start=(s == 0),
                     stop=(s == PASSES - 1),
                 )
@@ -158,13 +162,16 @@ def tile_picked_sage_none_e_kernel(tc, xT, w1, w2, gate, offs, pos1, pos2, pos3,
         def fetch_h(r, a, b):
             if a == 0 and r in H_AFTER:
                 h_tiles[r] = share.tile([P, S], F32, name=f"h{r}", offset=H_AFTER[r] * REGION + 1024)
+            elif a == 0 and r == ROWS - 1:
+                h_tiles[r] = share.tile([P, S], F32, name=f"h{r}", offset=ROWS * REGION)
             elif a == 0:
                 h_tiles[r] = keep.tile([P, S], F32, name=f"h{r}")
-            nc.scalar.activation(h_tiles[r][:, a:b], accs[r, a // HALF][:, a:b], COPY)
+            nc.scalar.activation(h_tiles[r][:, a:b], accs[r][:, a:b], COPY)
 
         zT = {(g, vh): keep.tile([P, 2, P, 2], BF16, name=f"zT{g}{vh}") for g in range(GROUPS) for vh in range(2)}
-        w2_c = keep.tile([P, GROUPS, N], U32, name="w2_c", align_bytes=64)
         w2_s = keep.tile([P, GROUPS, N], U8, name="w2_s", align_bytes=64)
+        w2_g = keep.tile([P, GROUPS, N, 4], BF16, name="w2_g", align_bytes=64)
+        zq0 = keep.tile([P, 2, P, 4], BF16, name="zq0", align_bytes=64)
         z_banks = {}
 
         def pick_h(r, d):
@@ -172,7 +179,7 @@ def tile_picked_sage_none_e_kernel(tc, xT, w1, w2, gate, offs, pos1, pos2, pos3,
                 for vh in range(2):
                     z_banks[r // 4, vh] = ps_z.tile([P, 512], F32, name=f"zps{vh}")
             if (r, d) in HELD:
-                g = share.tile([P, V], F32, name=f"held{r}", offset=HELD[r, d] * REGION)
+                g = share.tile([P, V], F32, name=f"held{r}{d}", offset=HELD[r, d] * REGION)
             else:
                 g = picks.tile([P, V], F32, name=f"picked{d}")
             nc.vector.tensor_tensor(g[:], h_tiles[r][:].indirect(pos_t[d][:]), gate_t[:, d, :], MULT)
@@ -194,32 +201,14 @@ def tile_picked_sage_none_e_kernel(tc, xT, w1, w2, gate, offs, pos1, pos2, pos3,
             words = zT[g, vh][:].rearrange("v u p e -> v (u p e)").bitcast(F32)
             nc.tensor.transpose(dst, words[:, u * P : u * P + P], ident[:])
 
-        def second_operand(g):
+        def first_group_back():
             zw = ps_1.tile([P, 2, 2, P], F32, name="zw")
             for vh in range(2):
                 for u in range(2):
-                    turn_back(zw[:, vh, u, :], g, vh, u)
-            zq = keep.tile([P, 2, P, 4], BF16, name="zq", align_bytes=64)
-            zq_words = zq[:].rearrange("p h v k -> p (h v k)").bitcast(F32)
+                    turn_back(zw[:, vh, u, :], 0, vh, u)
+            zq_words = zq0[:].rearrange("p h v k -> p (h v k)").bitcast(F32)
             nc.scalar.copy(
                 zq_words.rearrange("p (h v u) -> p h v u", h=2, u=2), zw[:].rearrange("p h u v -> p h v u")
-            )
-            zc = keep.tile([P, V], U32, name="zc", align_bytes=64)
-            zs = keep.tile([P, V], U8, name="zs", align_bytes=64)
-            nc.vector.quantize_mx(
-                out=zc[:].bitcast(FP8X4), scales=zs[:], in_=zq[:].rearrange("p h v k -> p (h v k)")
-            )
-            for vh in range(2):
-                z_codes[g, vh] = (zc[:, vh * P : vh * P + P], zs[:, vh * P : vh * P + P])
-
-        def weights2():
-            w2_g = keep.tile([P, GROUPS, N, 4], BF16, name="w2_g", align_bytes=64)
-            for g in range(GROUPS):
-                cast4("s", w2_g[:, g], w2_raw[:, g])
-            nc.vector.quantize_mx(
-                out=w2_c[:].rearrange("p g n -> p (g n)").bitcast(FP8X4),
-                scales=w2_s[:].rearrange("p g n -> p (g n)"),
-                in_=w2_g[:].rearrange("p g n k -> p (g n k)"),
             )
 
         def tail():
@@ -227,7 +216,10 @@ def tile_picked_sage_none_e_kernel(tc, xT, w1, w2, gate, offs, pos1, pos2, pos3,
             banks = [ps_h.tile([P, S], F32, name="acc") for vh in range(2)]
             for vh in range(2):
                 for d in range(D):
-                    g = picks.tile([P, P], F32, name=f"half{d}")
+                    if (vh, d) == (1, D - 1):
+                        g = share.tile([P, P], F32, name="last_half", offset=ROWS * REGION + 2048)
+                    else:
+                        g = picks.tile([P, P], F32, name=f"half{d}")
                     part = pos_t[d][:, vh * (P // 16) : (vh + 1) * (P // 16)]
                     nc.vector.tensor_tensor(
                         g[:], h_tiles[r][:].indirect(part), gate_t[:, d, vh * P : vh * P + P], MULT
@@ -237,14 +229,27 @@ def tile_picked_sage_none_e_kernel(tc, xT, w1, w2, gate, offs, pos1, pos2, pos3,
                     )
             for vh in range(2):
                 round_z("sv"[vh], 1, vh, banks[vh][:, 0:P], 3, 1)
+            zw = [ps_z.tile([P, 512], F32, name=f"zps{vh}") for vh in range(2)]
+            for vh in range(2):
+                for u in range(2):
+                    turn_back(zw[vh][:, u * P : u * P + P], 1, vh, u)
+            w2_c = share.tile([P, GROUPS, N], U32, name="w2_c", offset=ROWS * REGION, align_bytes=64)
+            nc.vector.quantize_mx(
+                out=w2_c[:].rearrange("p g n -> p (g n)").bitcast(FP8X4),
+                scales=w2_s[:].rearrange("p g n -> p (g n)"),
+                in_=w2_g[:].rearrange("p g n k -> p (g n k)"),
+            )
+            zc0 = share.tile([P, V], U32, name="zc0", offset=ROWS * REGION + 2048, align_bytes=64)
+            zs0 = keep.tile([P, V], U8, name="zs0", align_bytes=64)
+            nc.vector.quantize_mx(
+                out=zc0[:].bitcast(FP8X4), scales=zs0[:], in_=zq0[:].rearrange("p h v k -> p (h v k)")
+            )
             res = keep.tile([N, V], F32, name="res")
             for vh in range(2):
-                zw = ps_z.tile([P, 512], F32, name=f"zps{vh}")
-                for u in range(2):
-                    turn_back(zw[:, u * P : u * P + P], 1, vh, u)
+                cols = slice(vh * P, vh * P + P)
                 zq = keep.tile([P, P, 4], BF16, name=f"zq_tail{vh}", align_bytes=64)
                 dst = zq[:].rearrange("p v k -> p (v k)").bitcast(F32).rearrange("p (v u) -> p v u", u=2)
-                src = zw[:, 0 : 2 * P].rearrange("p (u v) -> p v u", u=2)
+                src = zw[vh][:, 0 : 2 * P].rearrange("p (u v) -> p v u", u=2)
                 if vh == 0:
                     nc.scalar.copy(dst, src)
                 else:
@@ -254,20 +259,17 @@ def tile_picked_sage_none_e_kernel(tc, xT, w1, w2, gate, offs, pos1, pos2, pos3,
                 nc.vector.quantize_mx(
                     out=zc[:].bitcast(FP8X4), scales=zs[:], in_=zq[:].rearrange("p v k -> p (v k)")
                 )
-                z_codes[1, vh] = (zc[:], zs[:])
                 acc_o = ps_h.tile([P, S], F32, name="acc")
-                for g in range(GROUPS):
-                    zc, zs = z_codes[g, vh]
+                for g, (codes, scales) in enumerate(((zc0[:, cols], zs0[:, cols]), (zc[:], zs[:]))):
                     nc.tensor.matmul_mx(
                         out=acc_o[:, 0:P],
                         lhsT=w2_c[:, g, :].bitcast(FP8X4),
                         lhsT_scale=w2_s[:, g, :],
-                        rhs=zc.bitcast(FP8X4),
-                        rhs_scale=zs,
+                        rhs=codes.bitcast(FP8X4),
+                        rhs_scale=scales,
                         start=(g == 0),
                         stop=(g == GROUPS - 1),
                     )
-                cols = slice(vh * P, vh * P + P)
                 if vh == 0:
                     nc.scalar.activation(res[:, cols], acc_o[:, 0:P], COPY)
                 else:
@@ -276,46 +278,36 @@ def tile_picked_sage_none_e_kernel(tc, xT, w1, w2, gate, offs, pos1, pos2, pos3,
 
         for n in range(len(X_PIECES)):
             quantise_x(n)
-            if n == 1:
-                pick_codes(0, 0, S, False)
-        pick_codes(1, 0, HALF, False)
-        pick_scales(0)
-        quantise_w1(0)
-        project(0, 0)
-        fetch_h(0, 0, HALF)
-        pick_codes(1, HALF, S, True)
-        pick_scales(1)
-        project(0, 1)
-        fetch_h(0, HALF, S)
+            if n == LAST0:
+                nc.vector.tensor_copy(codes0[:], all_codes[0][:].indirect(offs_t[:]))
+        for a, b in PARTS:
+            pick_codes(1, a, b)
+            pick_scales(a, b)
+            if a == 0:
+                quantise_w1(0)
+            project(0, a, b)
+            fetch_h(0, a, b)
 
         def weights1(r):
             quantise_w1(r)
-            project(r, 0)
-            project(r, 1)
+            project(r, 0, HALF)
+            project(r, HALF, S)
 
         weights1(1)
-        pick_h(0, 0)
-        pick_h(0, 1)
-        weights1(2)
-        fetch_h(1, 0, S)
-        pick_h(0, 2)
-        pick_h(1, 0)
-        weights1(3)
-        pick_h(1, 1)
-        pick_h(1, 2)
-        for r in range(2, ROWS - 1):
+        for r in range(ROWS - 1):
+            pick_h(r, 0)
+            pick_h(r, 1)
             if r + 2 < ROWS:
                 weights1(r + 2)
-            fetch_h(r, 0, S)
-            if r == 5:
+            fetch_h(r + 1, 0, S)
+            if r == 4:
                 for vh in range(2):
                     round_z("s", 0, vh, z_banks[0, vh][:], 0, 4)
             if r == 6:
-                fetch_h(7, 0, S)
-                weights2()
-                second_operand(0)
-            for d in range(D):
-                pick_h(r, d)
+                first_group_back()
+                for g in range(GROUPS):
+                    cast4("s", w2_g[:, g], w2_raw[:, g])
+            pick_h(r, 2)
         for vh in range(2):
             round_z("s", 1, vh, z_banks[1, vh][:, 0 : 3 * P], 0, 3)
         tail()

@@ -24,7 +24,7 @@ LAST0 = 1
 PARTS = ((0, 256), (256, 384), (384, 512))
 HELD = {(r, 2): r + 2 for r in range(ROWS - 2)}
 H_AFTER = {r: r + 1 for r in range(1, ROWS - 1)}
-REGION = 3072
+REGION = 4096
 
 FLOPS = 2 * K * H * S + 2 * H * N * V
 
@@ -61,10 +61,7 @@ def tile_picked_sage_none_e_kernel(tc, xT, w1, w2, gate, offs, pos1, pos2, pos3,
         def load_w1(c):
             r0, rows = W1_CHUNKS[c]
             for s in range(PASSES):
-                if s == 0:
-                    t = keep.tile([P, 4, rows * P], F32, name=f"w1_raw{c}{s}")
-                else:
-                    t = share.tile([P, 4, rows * P], F32, name=f"w1_raw{c}{s}", offset=c * REGION, align_bytes=64)
+                t = share.tile([P, 4, rows * P], F32, name=f"w1_raw{c}{s}", offset=c * REGION + s * 2048, align_bytes=64)
                 nc.sync.dma_start(t[:], w1_view[s][:, :, r0 * P : (r0 + rows) * P])
                 w1_raw[c, s] = t
 
@@ -78,10 +75,11 @@ def tile_picked_sage_none_e_kernel(tc, xT, w1, w2, gate, offs, pos1, pos2, pos3,
         nc.sync.dma_start(gate_t[:], gate.rearrange("d p v -> p d v"))
         for d, src in enumerate((pos1, pos2, pos3)):
             nc.sync.dma_start(pos_t[d][:], src)
-        for c in range(2, len(W1_CHUNKS)):
+        for c in range(2, len(W1_CHUNKS) - 1):
             load_w1(c)
         w2_raw = keep.tile([P, GROUPS, 4, N], F32, name="w2_raw")
         nc.sync.dma_start(w2_raw[:], w2.rearrange("(g p j) n -> p g j n", g=GROUPS, j=4))
+        load_w1(len(W1_CHUNKS) - 1)
 
         def cast4(engine, dst, src):
             o = dst.rearrange("p (q i) j -> p q j i", i=4)
@@ -108,11 +106,11 @@ def tile_picked_sage_none_e_kernel(tc, xT, w1, w2, gate, offs, pos1, pos2, pos3,
         codes0 = keep.tile([P, S], U32, name="codes0", align_bytes=64)
         codes1 = [
             keep.tile([P, HALF], U32, name="codes1a", align_bytes=64),
-            share.tile([P, HALF], U32, name="codes1b", offset=0, align_bytes=64),
+            share.tile([P, HALF], U32, name="codes1b", offset=2048, align_bytes=64),
         ]
         x_scales = [
             keep.tile([P, HALF], U8, name="scales_a", align_bytes=64),
-            share.tile([P, HALF], U8, name="scales_b", offset=1024, align_bytes=64),
+            share.tile([P, HALF], U8, name="scales_b", offset=3072, align_bytes=64),
         ]
 
         def x_operand(s, a, b):
@@ -161,7 +159,7 @@ def tile_picked_sage_none_e_kernel(tc, xT, w1, w2, gate, offs, pos1, pos2, pos3,
 
         def fetch_h(r, a, b):
             if a == 0 and r in H_AFTER:
-                h_tiles[r] = share.tile([P, S], F32, name=f"h{r}", offset=H_AFTER[r] * REGION + 1024)
+                h_tiles[r] = share.tile([P, S], F32, name=f"h{r}", offset=H_AFTER[r] * REGION)
             elif a == 0 and r == ROWS - 1:
                 h_tiles[r] = share.tile([P, S], F32, name=f"h{r}", offset=ROWS * REGION)
             elif a == 0:
@@ -179,7 +177,7 @@ def tile_picked_sage_none_e_kernel(tc, xT, w1, w2, gate, offs, pos1, pos2, pos3,
                 for vh in range(2):
                     z_banks[r // 4, vh] = ps_z.tile([P, 512], F32, name=f"zps{vh}")
             if (r, d) in HELD:
-                g = share.tile([P, V], F32, name=f"held{r}{d}", offset=HELD[r, d] * REGION)
+                g = share.tile([P, V], F32, name=f"held{r}{d}", offset=HELD[r, d] * REGION + 2048)
             else:
                 g = picks.tile([P, V], F32, name=f"picked{d}")
             nc.vector.tensor_tensor(g[:], h_tiles[r][:].indirect(pos_t[d][:]), gate_t[:, d, :], MULT)
@@ -299,14 +297,16 @@ def tile_picked_sage_none_e_kernel(tc, xT, w1, w2, gate, offs, pos1, pos2, pos3,
             pick_h(r, 1)
             if r + 2 < ROWS:
                 weights1(r + 2)
-            fetch_h(r + 1, 0, S)
             if r == 4:
-                for vh in range(2):
-                    round_z("s", 0, vh, z_banks[0, vh][:], 0, 4)
+                cast4("s", w2_g[:, 0], w2_raw[:, 0])
+            if r == 5:
+                round_z("s", 0, 0, z_banks[0, 0][:], 0, 4)
+            fetch_h(r + 1, 0, S)
+            if r == 5:
+                round_z("s", 0, 1, z_banks[0, 1][:], 0, 4)
+                cast4("s", w2_g[:, 1], w2_raw[:, 1])
             if r == 6:
                 first_group_back()
-                for g in range(GROUPS):
-                    cast4("s", w2_g[:, g], w2_raw[:, g])
             pick_h(r, 2)
         for vh in range(2):
             round_z("s", 1, vh, z_banks[1, vh][:, 0 : 3 * P], 0, 3)

@@ -72,10 +72,14 @@ def tile_picked_sage_none_e_kernel(tc, xT, w1, w2, gate, offs, pos1, pos2, pos3,
             load_x(n)
         for c in range(2):
             load_w1(c)
-        nc.sync.dma_start(gate_t[:], gate.rearrange("d p v -> p d v"))
-        for d, src in enumerate((pos1, pos2, pos3)):
-            nc.sync.dma_start(pos_t[d][:], src)
-        for c in range(2, len(W1_CHUNKS) - 1):
+        gate_view = gate.rearrange("d p v -> p d v")
+        nc.sync.dma_start(pos_t[0][:], pos1)
+        nc.sync.dma_start(gate_t[:, 0:2], gate_view[:, 0:2])
+        nc.sync.dma_start(pos_t[1][:], pos2)
+        load_w1(2)
+        nc.sync.dma_start(gate_t[:, 2], gate_view[:, 2])
+        nc.sync.dma_start(pos_t[2][:], pos3)
+        for c in range(3, len(W1_CHUNKS) - 1):
             load_w1(c)
         w2_raw = keep.tile([P, GROUPS, 4, N], F32, name="w2_raw")
         nc.sync.dma_start(w2_raw[:], w2.rearrange("(g p j) n -> p g j n", g=GROUPS, j=4))
@@ -279,8 +283,9 @@ def tile_picked_sage_none_e_kernel(tc, xT, w1, w2, gate, offs, pos1, pos2, pos3,
             if n == LAST0:
                 nc.vector.tensor_copy(codes0[:], all_codes[0][:].indirect(offs_t[:]))
         for a, b in PARTS:
+            if a % HALF == 0:
+                pick_scales(a, a + HALF)
             pick_codes(1, a, b)
-            pick_scales(a, b)
             if a == 0:
                 quantise_w1(0)
             project(0, a, b)

@@ -5,6 +5,7 @@ from concourse.masks import make_identity
 
 F32 = mybir.dt.float32
 BF16 = mybir.dt.bfloat16
+I32 = mybir.dt.int32
 U32 = mybir.dt.uint32
 U16 = mybir.dt.uint16
 U8 = mybir.dt.uint8
@@ -45,7 +46,7 @@ def tile_picked_sage_none_e_kernel(tc, xT, w1, w2, gate, offs, pos1, pos2, pos3,
         ident = keep.tile([P, P], F32, name="ident")
         make_identity(nc, ident[:])
         all_scales = keep.tile([P, T], U8, name="all_scales", align_bytes=64)
-        nc.gpsimd.memset(all_scales[:], 0)
+        nc.vector.memset(all_scales[:].bitcast(I32), 0)
 
         x_view = xT.rearrange("(s p j) t -> s p j t", s=PASSES, p=P, j=4)
         w1_view = w1.rearrange("(s p j) c -> s p j c", s=PASSES, p=P, j=4)
@@ -216,18 +217,21 @@ def tile_picked_sage_none_e_kernel(tc, xT, w1, w2, gate, offs, pos1, pos2, pos3,
         def tail():
             r = ROWS - 1
             banks = [ps_h.tile([P, S], F32, name="acc") for vh in range(2)]
-            for vh in range(2):
-                for d in range(D):
-                    if (vh, d) == (1, D - 1):
-                        g = share.tile([P, P], F32, name="last_half", offset=ROWS * REGION + 2048)
-                    else:
-                        g = picks.tile([P, P], F32, name=f"half{d}")
-                    part = pos_t[d][:, vh * (P // 16) : (vh + 1) * (P // 16)]
-                    nc.vector.tensor_tensor(
-                        g[:], h_tiles[r][:].indirect(part), gate_t[:, d, vh * P : vh * P + P], MULT
-                    )
+            for d, first, width in ((0, 0, V), (1, 0, V), (2, 0, P), (2, P, P)):
+                if first:
+                    g = share.tile([P, P], F32, name="last_half", offset=ROWS * REGION + 2048)
+                else:
+                    g = picks.tile([P, width], F32, name=f"picked{d}")
+                part = pos_t[d][:, first // 16 : (first + width) // 16]
+                nc.vector.tensor_tensor(g[:], h_tiles[r][:].indirect(part), gate_t[:, d, first : first + width], MULT)
+                for a in range(0, width, P):
                     nc.tensor.matmul(
-                        banks[vh][:, 0:P], g[:], ident[:], start=(d == 0), stop=(d == D - 1), is_transpose=True
+                        banks[(first + a) // P][:, 0:P],
+                        g[:, a : a + P],
+                        ident[:],
+                        start=(d == 0),
+                        stop=(d == D - 1),
+                        is_transpose=True,
                     )
             for vh in range(2):
                 round_z("sv"[vh], 1, vh, banks[vh][:, 0:P], 3, 1)

@@ -15,17 +15,30 @@ MULT = mybir.AluOpType.mult
 
 P = 128
 K, T, D, S, V, H, N = 1024, 1024, 3, 512, 256, 1024, 128
-PASSES = K // 512
-GROUPS = H // 512
+PASS = 512
+PASSES = K // PASS
+GROUPS = H // PASS
 ROWS = H // P
-HALF = S // 2
-X_PIECES = ((0, 0, 512, 128), (0, 512, 512, 320), (1, 0, 256, 0), (1, 256, 256, 0), (1, 512, 256, 96), (1, 768, 256, 160))
-W1_CHUNKS = tuple((r, 1) for r in range(ROWS))
-LAST0 = 1
-PARTS = ((0, 256), (256, 384), (384, 512))
-HELD = {(r, 2): r + 2 for r in range(ROWS - 2)}
-H_AFTER = {r: r + 1 for r in range(1, ROWS - 1)}
-REGION = 4096
+GROUP_ROWS = PASS // P
+HALVES = V // P
+LIST_HALF = S // 2
+PER_COLUMN = 16
+
+X_PIECES = (
+    (0, 0, 512, 128),
+    (0, 512, 512, 320),
+    (1, 0, 256, 0),
+    (1, 256, 256, 0),
+    (1, 512, 256, 96),
+    (1, 768, 128, 32),
+    (1, 896, 128, 80),
+)
+FIRST_ROW_PARTS = ((0, 256), (256, 384), (384, 512))
+AHEAD = 2
+
+HALF_SLOT = 4 * P * 4
+SLOT = 2 * HALF_SLOT
+LAST_SLOT = ROWS * SLOT
 
 FLOPS = 2 * K * H * S + 2 * H * N * V
 
@@ -35,14 +48,14 @@ def tile_picked_sage_none_e_kernel(tc, xT, w1, w2, gate, offs, pos1, pos2, pos3,
     with ExitStack() as ctx:
         lists = ctx.enter_context(tc.tile_pool(name="lists", bufs=1))
         keep = ctx.enter_context(tc.tile_pool(name="keep", bufs=1))
-        share = ctx.enter_context(tc.tile_pool(name="share", bufs=1))
+        shared = ctx.enter_context(tc.tile_pool(name="shared", bufs=1))
         picks = ctx.enter_context(tc.tile_pool(name="picks", bufs=3))
-        ps_h = ctx.enter_context(tc.psum_pool(name="ps_h", bufs=3))
+        ps_acc = ctx.enter_context(tc.psum_pool(name="ps_acc", bufs=3))
         ps_z = ctx.enter_context(tc.psum_pool(name="ps_z", bufs=2))
-        ps_1 = ctx.enter_context(tc.psum_pool(name="ps_1", bufs=1))
+        ps_back = ctx.enter_context(tc.psum_pool(name="ps_back", bufs=1))
 
-        offs_t = lists.tile([P, S // 16], U16, name="offs_t")
-        pos_t = [lists.tile([P, V // 16], U16, name=f"pos_t{d}") for d in range(D)]
+        offs_t = lists.tile([P, S // PER_COLUMN], U16, name="offs_t")
+        pos_t = [lists.tile([P, V // PER_COLUMN], U16, name=f"pos_t{d}") for d in range(D)]
         ident = keep.tile([P, P], F32, name="ident")
         make_identity(nc, ident[:])
         all_scales = keep.tile([P, T], U8, name="all_scales", align_bytes=64)
@@ -50,110 +63,100 @@ def tile_picked_sage_none_e_kernel(tc, xT, w1, w2, gate, offs, pos1, pos2, pos3,
 
         x_view = xT.rearrange("(s p j) t -> s p j t", s=PASSES, p=P, j=4)
         w1_view = w1.rearrange("(s p j) c -> s p j c", s=PASSES, p=P, j=4)
-        x_raw, w1_raw = [], {}
+        gate_view = gate.rearrange("d p v -> p d v")
+        x_raw, w1_raw = {}, {}
         gate_t = keep.tile([P, D, V], F32, name="gate_t")
 
         def load_x(n):
-            s, first, count, vshare = X_PIECES[n]
-            t = keep.tile([P, 4, count], F32, name=f"x_raw{n}")
-            nc.sync.dma_start(t[:], x_view[s][:, :, first : first + count])
-            x_raw.append(t)
+            s, first, count = X_PIECES[n][:3]
+            x_raw[n] = keep.tile([P, 4, count], F32, name=f"x_raw{n}")
+            nc.sync.dma_start(x_raw[n][:], x_view[s][:, :, first : first + count])
 
-        def load_w1(c):
-            r0, rows = W1_CHUNKS[c]
+        def load_w1(r):
             for s in range(PASSES):
-                t = share.tile([P, 4, rows * P], F32, name=f"w1_raw{c}{s}", offset=c * REGION + s * 2048, align_bytes=64)
-                nc.sync.dma_start(t[:], w1_view[s][:, :, r0 * P : (r0 + rows) * P])
-                w1_raw[c, s] = t
+                place = r * SLOT + s * HALF_SLOT
+                w1_raw[r, s] = shared.tile([P, 4, P], F32, name=f"w1_raw{r}{s}", offset=place, align_bytes=64)
+                nc.sync.dma_start(w1_raw[r, s][:], w1_view[s][:, :, r * P : r * P + P])
 
-        load_x(0)
-        load_x(1)
-        nc.sync.dma_start(offs_t[:], offs)
-        for n in range(2, len(X_PIECES)):
+        pass0_pieces = [n for n, piece in enumerate(X_PIECES) if piece[0] == 0]
+        for n in range(len(X_PIECES)):
             load_x(n)
-        for c in range(2):
-            load_w1(c)
-        gate_view = gate.rearrange("d p v -> p d v")
+            if n == pass0_pieces[-1]:
+                nc.sync.dma_start(offs_t[:], offs)
+        load_w1(0)
+        load_w1(1)
         nc.sync.dma_start(pos_t[0][:], pos1)
         nc.sync.dma_start(gate_t[:, 0:2], gate_view[:, 0:2])
         nc.sync.dma_start(pos_t[1][:], pos2)
         load_w1(2)
         nc.sync.dma_start(gate_t[:, 2], gate_view[:, 2])
         nc.sync.dma_start(pos_t[2][:], pos3)
-        for c in range(3, len(W1_CHUNKS) - 1):
-            load_w1(c)
+        for r in range(3, ROWS - 1):
+            load_w1(r)
         w2_raw = keep.tile([P, GROUPS, 4, N], F32, name="w2_raw")
         nc.sync.dma_start(w2_raw[:], w2.rearrange("(g p j) n -> p g j n", g=GROUPS, j=4))
-        load_w1(len(W1_CHUNKS) - 1)
+        load_w1(ROWS - 1)
 
-        def cast4(engine, dst, src):
-            o = dst.rearrange("p (q i) j -> p q j i", i=4)
-            i = src.rearrange("p j (q i) -> p q j i", i=4)
-            if engine == "v":
-                nc.vector.tensor_copy(o, i)
+        def copy_on(engine, dst, src):
+            if engine == "vector":
+                nc.vector.tensor_copy(dst, src)
             else:
-                nc.scalar.activation(o, i, COPY)
+                nc.scalar.activation(dst, src, COPY)
+
+        def round_rows(engine, dst, src):
+            copy_on(engine, dst.rearrange("p (q c) j -> p q j c", c=4), src.rearrange("p j (q c) -> p q j c", c=4))
 
         all_codes = [keep.tile([P, T], U32, name=f"all_codes{s}", align_bytes=64) for s in range(PASSES)]
 
         def quantise_x(n):
-            s, first, count, vshare = X_PIECES[n]
-            grouped = keep.tile([P, count, 4], BF16, name=f"x_g{n}", align_bytes=64)
-            cast4("s", grouped[:, vshare:count], x_raw[n][:, :, vshare:count])
-            if vshare:
-                cast4("v", grouped[:, 0:vshare], x_raw[n][:, :, 0:vshare])
+            s, first, count, on_vector = X_PIECES[n]
+            rounded = keep.tile([P, count, 4], BF16, name=f"x_bf16_{n}", align_bytes=64)
+            round_rows("scalar", rounded[:, on_vector:count], x_raw[n][:, :, on_vector:count])
+            if on_vector:
+                round_rows("vector", rounded[:, 0:on_vector], x_raw[n][:, :, 0:on_vector])
             nc.vector.quantize_mx(
                 out=all_codes[s][:, first : first + count].bitcast(FP8X4),
                 scales=all_scales[4 * s : P, first : first + count],
-                in_=grouped[:].rearrange("p n k -> p (n k)"),
+                in_=rounded[:].rearrange("p n j -> p (n j)"),
             )
 
         codes0 = keep.tile([P, S], U32, name="codes0", align_bytes=64)
         codes1 = [
-            keep.tile([P, HALF], U32, name="codes1a", align_bytes=64),
-            share.tile([P, HALF], U32, name="codes1b", offset=2048, align_bytes=64),
+            keep.tile([P, LIST_HALF], U32, name="codes1a", align_bytes=64),
+            shared.tile([P, LIST_HALF], U32, name="codes1b", offset=HALF_SLOT, align_bytes=64),
         ]
         x_scales = [
-            keep.tile([P, HALF], U8, name="scales_a", align_bytes=64),
-            share.tile([P, HALF], U8, name="scales_b", offset=3072, align_bytes=64),
+            keep.tile([P, LIST_HALF], U8, name="scales_a", align_bytes=64),
+            shared.tile([P, LIST_HALF], U8, name="scales_b", offset=HALF_SLOT + 4 * LIST_HALF, align_bytes=64),
         ]
 
-        def x_operand(s, a, b):
-            part, first = divmod(a, HALF)
+        def picked_x(s, a, b):
+            part, first = divmod(a, LIST_HALF)
             codes = codes0[:, a:b] if s == 0 else codes1[part][:, first : first + b - a]
             return codes, x_scales[part][:, first : first + b - a]
 
-        def pick_codes(s, a, b):
-            nc.vector.tensor_copy(x_operand(s, a, b)[0], all_codes[s][:].indirect(offs_t[:, a // 16 : b // 16]))
+        def entries_of(tile, a, b):
+            return tile[:, a // PER_COLUMN : b // PER_COLUMN]
 
-        def pick_scales(a, b):
-            nc.vector.tensor_copy(x_operand(1, a, b)[1], all_scales[:].indirect(offs_t[:, a // 16 : b // 16]))
+        w1_codes, w1_scales, h_banks, h_tiles = {}, {}, {}, {}
 
-        w1_codes, w1_scales, h_tiles, accs, z_codes = {}, {}, {}, {}, {}
-
-        def quantise_w1(c):
-            r0, rows = W1_CHUNKS[c]
-            grouped = keep.tile([P, PASSES, rows * P, 4], BF16, name=f"w1_g{c}", align_bytes=64)
-            codes = keep.tile([P, PASSES, rows * P], U32, name=f"w1_codes{c}", align_bytes=64)
-            scales = keep.tile([P, PASSES, rows * P], U8, name=f"w1_scales{c}", align_bytes=64)
+        def quantise_w1(r):
+            rounded = keep.tile([P, PASSES, P, 4], BF16, name=f"w1_bf16_{r}", align_bytes=64)
+            w1_codes[r] = keep.tile([P, PASSES, P], U32, name=f"w1_codes{r}", align_bytes=64)
+            w1_scales[r] = keep.tile([P, PASSES, P], U8, name=f"w1_scales{r}", align_bytes=64)
             for s in range(PASSES):
-                cast4("s", grouped[:, s], w1_raw[c, s][:])
+                round_rows("scalar", rounded[:, s], w1_raw[r, s][:])
             nc.vector.quantize_mx(
-                out=codes[:].rearrange("p s n -> p (s n)").bitcast(FP8X4),
-                scales=scales[:].rearrange("p s n -> p (s n)"),
-                in_=grouped[:].rearrange("p s n k -> p (s n k)"),
+                out=w1_codes[r][:].rearrange("p s c -> p (s c)").bitcast(FP8X4),
+                scales=w1_scales[r][:].rearrange("p s c -> p (s c)"),
+                in_=rounded[:].rearrange("p s c j -> p (s c j)"),
             )
-            for n in range(rows):
-                w1_codes[r0 + n] = codes[:, :, n * P : n * P + P]
-                w1_scales[r0 + n] = scales[:, :, n * P : n * P + P]
 
         def project(r, a, b):
-            if a == 0 or r == 0:
-                accs[r] = ps_h.tile([P, S], F32, name="acc")
             for s in range(PASSES):
-                codes, scales = x_operand(s, a, b)
+                codes, scales = picked_x(s, a, b)
                 nc.tensor.matmul_mx(
-                    out=accs[r][:, a:b],
+                    out=h_banks[r][:, a:b],
                     lhsT=w1_codes[r][:, s, :].bitcast(FP8X4),
                     lhsT_scale=w1_scales[r][:, s, :],
                     rhs=codes.bitcast(FP8X4),
@@ -162,161 +165,159 @@ def tile_picked_sage_none_e_kernel(tc, xT, w1, w2, gate, offs, pos1, pos2, pos3,
                     stop=(s == PASSES - 1),
                 )
 
-        def fetch_h(r, a, b):
-            if a == 0 and r in H_AFTER:
-                h_tiles[r] = share.tile([P, S], F32, name=f"h{r}", offset=H_AFTER[r] * REGION)
-            elif a == 0 and r == ROWS - 1:
-                h_tiles[r] = share.tile([P, S], F32, name=f"h{r}", offset=ROWS * REGION)
-            elif a == 0:
-                h_tiles[r] = keep.tile([P, S], F32, name=f"h{r}")
-            nc.scalar.activation(h_tiles[r][:, a:b], accs[r][:, a:b], COPY)
+        def project_row(r):
+            quantise_w1(r)
+            h_banks[r] = ps_acc.tile([P, S], F32, name="acc")
+            for a in range(0, S, LIST_HALF):
+                project(r, a, a + LIST_HALF)
 
-        zT = {(g, vh): keep.tile([P, 2, P, 2], BF16, name=f"zT{g}{vh}") for g in range(GROUPS) for vh in range(2)}
-        w2_s = keep.tile([P, GROUPS, N], U8, name="w2_s", align_bytes=64)
-        w2_g = keep.tile([P, GROUPS, N, 4], BF16, name="w2_g", align_bytes=64)
-        zq0 = keep.tile([P, 2, P, 4], BF16, name="zq0", align_bytes=64)
+        def fetch_row(r):
+            h_tiles[r] = shared.tile([P, S], F32, name=f"h{r}", offset=(r + 1) * SLOT)
+            nc.scalar.activation(h_tiles[r][:], h_banks[r][:], COPY)
+
+        zT = {
+            (g, half): keep.tile([P, 2, P, 2], BF16, name=f"zT{g}{half}") for g in range(GROUPS) for half in range(HALVES)
+        }
+        w2_scales = keep.tile([P, GROUPS, N], U8, name="w2_scales", align_bytes=64)
+        w2_rounded = keep.tile([P, GROUPS, N, 4], BF16, name="w2_bf16", align_bytes=64)
+        z0_rounded = keep.tile([P, HALVES, P, 4], BF16, name="z0_bf16", align_bytes=64)
         z_banks = {}
 
-        def pick_h(r, d):
-            if r % 4 == 0 and d == 0:
-                for vh in range(2):
-                    z_banks[r // 4, vh] = ps_z.tile([P, 512], F32, name=f"zps{vh}")
-            if (r, d) in HELD:
-                g = share.tile([P, V], F32, name=f"held{r}{d}", offset=HELD[r, d] * REGION + 2048)
-            else:
-                g = picks.tile([P, V], F32, name=f"picked{d}")
-            nc.vector.tensor_tensor(g[:], h_tiles[r][:].indirect(pos_t[d][:]), gate_t[:, d, :], MULT)
-            for vh in range(2):
-                dst = z_banks[r // 4, vh][:, (r % 4) * P : (r % 4) * P + P]
-                nc.tensor.matmul(
-                    dst, g[:, vh * P : vh * P + P], ident[:], start=(d == 0), stop=(d == D - 1), is_transpose=True
-                )
+        def add_turned(dst, picked, d):
+            nc.tensor.matmul(dst, picked, ident[:], start=(d == 0), stop=(d == D - 1), is_transpose=True)
 
-        def round_z(engine, g, vh, bank, first, rows):
-            dst = zT[g, vh][:, :, 32 * first : 32 * (first + rows), :]
-            src = bank.rearrange("v (p u e) -> v u p e", u=2, e=2)
-            if engine == "v":
-                nc.vector.tensor_copy(dst, src)
+        def pick_neighbours(r, d):
+            g, place = divmod(r, GROUP_ROWS)
+            if place == 0 and d == 0:
+                for half in range(HALVES):
+                    z_banks[g, half] = ps_z.tile([P, PASS], F32, name=f"z_bank{half}")
+            if d == D - 1 and r + AHEAD < ROWS:
+                picked = shared.tile([P, V], F32, name=f"third{r}", offset=(r + AHEAD) * SLOT + HALF_SLOT)
             else:
-                nc.scalar.activation(dst, src, COPY)
+                picked = picks.tile([P, V], F32, name=f"picked{d}")
+            nc.vector.tensor_tensor(picked[:], h_tiles[r][:].indirect(pos_t[d][:]), gate_t[:, d, :], MULT)
+            for half in range(HALVES):
+                add_turned(z_banks[g, half][:, place * P : place * P + P], picked[:, half * P : half * P + P], d)
 
-        def turn_back(dst, g, vh, u):
-            words = zT[g, vh][:].rearrange("v u p e -> v (u p e)").bitcast(F32)
+        def round_z(engine, g, half, sums, place, rows):
+            dst = zT[g, half][:, :, 32 * place : 32 * (place + rows), :]
+            copy_on(engine, dst, sums.rearrange("v (p u e) -> v u p e", u=2, e=2))
+
+        def turn_back(dst, g, half, u):
+            words = zT[g, half][:].rearrange("v u p e -> v (u p e)").bitcast(F32)
             nc.tensor.transpose(dst, words[:, u * P : u * P + P], ident[:])
 
-        def first_group_back():
-            zw = ps_1.tile([P, 2, 2, P], F32, name="zw")
-            for vh in range(2):
+        def first_pass_back():
+            turned = ps_back.tile([P, HALVES, 2, P], F32, name="turned")
+            for half in range(HALVES):
                 for u in range(2):
-                    turn_back(zw[:, vh, u, :], 0, vh, u)
-            zq_words = zq0[:].rearrange("p h v k -> p (h v k)").bitcast(F32)
+                    turn_back(turned[:, half, u, :], 0, half, u)
+            words = z0_rounded[:].rearrange("p h v j -> p (h v j)").bitcast(F32)
             nc.scalar.copy(
-                zq_words.rearrange("p (h v u) -> p h v u", h=2, u=2), zw[:].rearrange("p h u v -> p h v u")
+                words.rearrange("p (h v u) -> p h v u", h=HALVES, u=2), turned[:].rearrange("p h u v -> p h v u")
             )
 
-        def tail():
-            r = ROWS - 1
-            banks = [ps_h.tile([P, S], F32, name="acc") for vh in range(2)]
+        def last_row_and_second_product():
+            r, g_last = ROWS - 1, GROUPS - 1
+            copier = ("scalar", "vector")
+            sums = [ps_acc.tile([P, S], F32, name="acc") for half in range(HALVES)]
             for d, first, width in ((0, 0, V), (1, 0, V), (2, 0, P), (2, P, P)):
                 if first:
-                    g = share.tile([P, P], F32, name="last_half", offset=ROWS * REGION + 2048)
+                    picked = shared.tile([P, P], F32, name="last_picked", offset=LAST_SLOT + HALF_SLOT)
                 else:
-                    g = picks.tile([P, width], F32, name=f"picked{d}")
-                part = pos_t[d][:, first // 16 : (first + width) // 16]
-                nc.vector.tensor_tensor(g[:], h_tiles[r][:].indirect(part), gate_t[:, d, first : first + width], MULT)
-                for a in range(0, width, P):
-                    nc.tensor.matmul(
-                        banks[(first + a) // P][:, 0:P],
-                        g[:, a : a + P],
-                        ident[:],
-                        start=(d == 0),
-                        stop=(d == D - 1),
-                        is_transpose=True,
-                    )
-            for vh in range(2):
-                round_z("sv"[vh], 1, vh, banks[vh][:, 0:P], 3, 1)
-            zw = [ps_z.tile([P, 512], F32, name=f"zps{vh}") for vh in range(2)]
-            for vh in range(2):
-                for u in range(2):
-                    turn_back(zw[vh][:, u * P : u * P + P], 1, vh, u)
-            w2_c = share.tile([P, GROUPS, N], U32, name="w2_c", offset=ROWS * REGION, align_bytes=64)
-            nc.vector.quantize_mx(
-                out=w2_c[:].rearrange("p g n -> p (g n)").bitcast(FP8X4),
-                scales=w2_s[:].rearrange("p g n -> p (g n)"),
-                in_=w2_g[:].rearrange("p g n k -> p (g n k)"),
-            )
-            zc0 = share.tile([P, V], U32, name="zc0", offset=ROWS * REGION + 2048, align_bytes=64)
-            zs0 = keep.tile([P, V], U8, name="zs0", align_bytes=64)
-            nc.vector.quantize_mx(
-                out=zc0[:].bitcast(FP8X4), scales=zs0[:], in_=zq0[:].rearrange("p h v k -> p (h v k)")
-            )
-            res = keep.tile([N, V], F32, name="res")
-            for vh in range(2):
-                cols = slice(vh * P, vh * P + P)
-                zq = keep.tile([P, P, 4], BF16, name=f"zq_tail{vh}", align_bytes=64)
-                dst = zq[:].rearrange("p v k -> p (v k)").bitcast(F32).rearrange("p (v u) -> p v u", u=2)
-                src = zw[vh][:, 0 : 2 * P].rearrange("p (u v) -> p v u", u=2)
-                if vh == 0:
-                    nc.scalar.copy(dst, src)
-                else:
-                    nc.vector.tensor_copy(dst, src)
-                zc = keep.tile([P, P], U32, name=f"zc_tail{vh}", align_bytes=64)
-                zs = keep.tile([P, P], U8, name=f"zs_tail{vh}", align_bytes=64)
-                nc.vector.quantize_mx(
-                    out=zc[:].bitcast(FP8X4), scales=zs[:], in_=zq[:].rearrange("p v k -> p (v k)")
+                    picked = picks.tile([P, width], F32, name=f"picked{d}")
+                entries = entries_of(pos_t[d], first, first + width)
+                nc.vector.tensor_tensor(
+                    picked[:], h_tiles[r][:].indirect(entries), gate_t[:, d, first : first + width], MULT
                 )
-                acc_o = ps_h.tile([P, S], F32, name="acc")
-                for g, (codes, scales) in enumerate(((zc0[:, cols], zs0[:, cols]), (zc[:], zs[:]))):
+                for a in range(0, width, P):
+                    add_turned(sums[(first + a) // P][:, 0:P], picked[:, a : a + P], d)
+            for half in range(HALVES):
+                round_z(copier[half], g_last, half, sums[half][:, 0:P], GROUP_ROWS - 1, 1)
+            turned = [ps_z.tile([P, PASS], F32, name=f"z_bank{half}") for half in range(HALVES)]
+            for half in range(HALVES):
+                for u in range(2):
+                    turn_back(turned[half][:, u * P : u * P + P], g_last, half, u)
+            w2_codes = shared.tile([P, GROUPS, N], U32, name="w2_codes", offset=LAST_SLOT, align_bytes=64)
+            nc.vector.quantize_mx(
+                out=w2_codes[:].rearrange("p g n -> p (g n)").bitcast(FP8X4),
+                scales=w2_scales[:].rearrange("p g n -> p (g n)"),
+                in_=w2_rounded[:].rearrange("p g n j -> p (g n j)"),
+            )
+            z0_codes = shared.tile([P, V], U32, name="z0_codes", offset=LAST_SLOT + HALF_SLOT, align_bytes=64)
+            z0_scales = keep.tile([P, V], U8, name="z0_scales", align_bytes=64)
+            nc.vector.quantize_mx(
+                out=z0_codes[:].bitcast(FP8X4),
+                scales=z0_scales[:],
+                in_=z0_rounded[:].rearrange("p h v j -> p (h v j)"),
+            )
+            result = keep.tile([N, V], F32, name="result")
+            for half in range(HALVES):
+                cols = slice(half * P, half * P + P)
+                z1_rounded = keep.tile([P, P, 4], BF16, name=f"z1_bf16_{half}", align_bytes=64)
+                words = z1_rounded[:].rearrange("p v j -> p (v j)").bitcast(F32).rearrange("p (v u) -> p v u", u=2)
+                src = turned[half][:, 0 : 2 * P].rearrange("p (u v) -> p v u", u=2)
+                if copier[half] == "scalar":
+                    nc.scalar.copy(words, src)
+                else:
+                    nc.vector.tensor_copy(words, src)
+                z1_codes = keep.tile([P, P], U32, name=f"z1_codes{half}", align_bytes=64)
+                z1_scales = keep.tile([P, P], U8, name=f"z1_scales{half}", align_bytes=64)
+                nc.vector.quantize_mx(
+                    out=z1_codes[:].bitcast(FP8X4),
+                    scales=z1_scales[:],
+                    in_=z1_rounded[:].rearrange("p v j -> p (v j)"),
+                )
+                acc = ps_acc.tile([P, S], F32, name="acc")
+                operands = ((z0_codes[:, cols], z0_scales[:, cols]), (z1_codes[:], z1_scales[:]))
+                for g, (codes, scales) in enumerate(operands):
                     nc.tensor.matmul_mx(
-                        out=acc_o[:, 0:P],
-                        lhsT=w2_c[:, g, :].bitcast(FP8X4),
-                        lhsT_scale=w2_s[:, g, :],
+                        out=acc[:, 0:P],
+                        lhsT=w2_codes[:, g, :].bitcast(FP8X4),
+                        lhsT_scale=w2_scales[:, g, :],
                         rhs=codes.bitcast(FP8X4),
                         rhs_scale=scales,
                         start=(g == 0),
                         stop=(g == GROUPS - 1),
                     )
-                if vh == 0:
-                    nc.scalar.activation(res[:, cols], acc_o[:, 0:P], COPY)
-                else:
-                    nc.vector.tensor_copy(res[:, cols], acc_o[:, 0:P])
-                nc.sync.dma_start(out[:, cols], res[:, cols])
+                copy_on(copier[half], result[:, cols], acc[:, 0:P])
+                nc.sync.dma_start(out[:, cols], result[:, cols])
 
         for n in range(len(X_PIECES)):
             quantise_x(n)
-            if n == LAST0:
+            if n == pass0_pieces[-1]:
                 nc.vector.tensor_copy(codes0[:], all_codes[0][:].indirect(offs_t[:]))
-        for a, b in PARTS:
-            if a % HALF == 0:
-                pick_scales(a, a + HALF)
-            pick_codes(1, a, b)
+        for a, b in FIRST_ROW_PARTS:
+            if a % LIST_HALF == 0:
+                entries = entries_of(offs_t, a, a + LIST_HALF)
+                nc.vector.tensor_copy(x_scales[a // LIST_HALF][:], all_scales[:].indirect(entries))
+            nc.vector.tensor_copy(picked_x(1, a, b)[0], all_codes[1][:].indirect(entries_of(offs_t, a, b)))
             if a == 0:
                 quantise_w1(0)
+            h_banks[0] = ps_acc.tile([P, S], F32, name="acc")
             project(0, a, b)
-            fetch_h(0, a, b)
+            if a == 0:
+                h_tiles[0] = keep.tile([P, S], F32, name="h0")
+            nc.scalar.activation(h_tiles[0][:, a:b], h_banks[0][:, a:b], COPY)
+        project_row(1)
 
-        def weights1(r):
-            quantise_w1(r)
-            project(r, 0, HALF)
-            project(r, HALF, S)
-
-        weights1(1)
+        last_weights = ROWS - 1 - AHEAD
         for r in range(ROWS - 1):
-            pick_h(r, 0)
-            pick_h(r, 1)
-            if r + 2 < ROWS:
-                weights1(r + 2)
-            if r == 4:
-                cast4("s", w2_g[:, 0], w2_raw[:, 0])
-            if r == 5:
-                round_z("s", 0, 0, z_banks[0, 0][:], 0, 4)
-            fetch_h(r + 1, 0, S)
-            if r == 5:
-                round_z("s", 0, 1, z_banks[0, 1][:], 0, 4)
-                cast4("s", w2_g[:, 1], w2_raw[:, 1])
-            if r == 6:
-                first_group_back()
-            pick_h(r, 2)
-        for vh in range(2):
-            round_z("s", 1, vh, z_banks[1, vh][:, 0 : 3 * P], 0, 3)
-        tail()
+            pick_neighbours(r, 0)
+            pick_neighbours(r, 1)
+            if r <= last_weights:
+                project_row(r + AHEAD)
+            if r == last_weights - 1:
+                round_rows("scalar", w2_rounded[:, 0], w2_raw[:, 0])
+            if r == last_weights:
+                round_z("scalar", 0, 0, z_banks[0, 0][:], 0, GROUP_ROWS)
+            fetch_row(r + 1)
+            if r == last_weights:
+                round_z("scalar", 0, 1, z_banks[0, 1][:], 0, GROUP_ROWS)
+                round_rows("scalar", w2_rounded[:, 1], w2_raw[:, 1])
+            if r == last_weights + 1:
+                first_pass_back()
+            pick_neighbours(r, 2)
+        for half in range(HALVES):
+            round_z("scalar", 1, half, z_banks[1, half][:, 0 : (GROUP_ROWS - 1) * P], 0, GROUP_ROWS - 1)
+        last_row_and_second_product()

@@ -25,7 +25,7 @@ LIST_HALF = S // 2
 PER_COLUMN = 16
 
 X_PIECES = (
-    (0, 0, 512, 128),
+    (0, 0, 512, 320),
     (0, 512, 512, 320),
     (1, 0, 256, 0),
     (1, 256, 256, 0),
@@ -67,11 +67,6 @@ def tile_picked_sage_none_e_kernel(tc, xT, w1, w2, gate, offs, pos1, pos2, pos3,
         x_raw, w1_raw = {}, {}
         gate_t = keep.tile([P, D, V], F32, name="gate_t")
 
-        def load_x(n):
-            s, first, count = X_PIECES[n][:3]
-            x_raw[n] = keep.tile([P, 4, count], F32, name=f"x_raw{n}")
-            nc.sync.dma_start(x_raw[n][:], x_view[s][:, :, first : first + count])
-
         def load_w1(r):
             for s in range(PASSES):
                 place = r * SLOT + s * HALF_SLOT
@@ -79,10 +74,15 @@ def tile_picked_sage_none_e_kernel(tc, xT, w1, w2, gate, offs, pos1, pos2, pos3,
                 nc.sync.dma_start(w1_raw[r, s][:], w1_view[s][:, :, r * P : r * P + P])
 
         pass0_pieces = [n for n, piece in enumerate(X_PIECES) if piece[0] == 0]
-        for n in range(len(X_PIECES)):
-            load_x(n)
-            if n == pass0_pieces[-1]:
-                nc.sync.dma_start(offs_t[:], offs)
+        x_pass0 = keep.tile([P, 4, T], F32, name="x_pass0")
+        nc.sync.dma_start(x_pass0[:], x_view[0])
+        nc.sync.dma_start(offs_t[:], offs)
+        for n, (s, first, count, on_vector) in enumerate(X_PIECES):
+            if s == 0:
+                x_raw[n] = x_pass0[:, :, first : first + count]
+            else:
+                x_raw[n] = keep.tile([P, 4, count], F32, name=f"x_raw{n}")
+                nc.sync.dma_start(x_raw[n][:], x_view[s][:, :, first : first + count])
         load_w1(0)
         load_w1(1)
         nc.sync.dma_start(pos_t[0][:], pos1)

@@ -24,21 +24,16 @@ HALVES = V // P
 LIST_HALF = S // 2
 PER_COLUMN = 16
 
-X_PIECES = (
-    (0, 0, 512, 320),
-    (0, 512, 512, 320),
-    (1, 0, 256, 0),
-    (1, 256, 256, 0),
-    (1, 512, 256, 96),
-    (1, 768, 128, 32),
-    (1, 896, 128, 80),
-)
-FIRST_ROW_PARTS = ((0, 256), (256, 384), (384, 512))
+X1_PARTS = ((0, 256, "vector", None), (256, 384, "vector", 1), (384, 512, "scalar", 0))
+H0_PARTS = ((0, 256, "scalar"), (384, 512, "vector"), (256, 384, "scalar"))
+LAST_PLANE_PARTS = ((0, 256), (256, 512))
 AHEAD = 2
 
 HALF_SLOT = 4 * P * 4
 SLOT = 2 * HALF_SLOT
 LAST_SLOT = ROWS * SLOT
+PLANE_SLOT = LAST_SLOT + SLOT
+ROUNDED_SLOT = PLANE_SLOT + 4 * T
 
 FLOPS = 2 * K * H * S + 2 * H * N * V
 
@@ -58,13 +53,10 @@ def tile_picked_sage_none_e_kernel(tc, xT, w1, w2, gate, offs, pos1, pos2, pos3,
         pos_t = [lists.tile([P, V // PER_COLUMN], U16, name=f"pos_t{d}") for d in range(D)]
         ident = keep.tile([P, P], F32, name="ident")
         make_identity(nc, ident[:])
-        all_scales = keep.tile([P, T], U8, name="all_scales", align_bytes=64)
-        nc.vector.memset(all_scales[:].bitcast(I32), 0)
-
         x_view = xT.rearrange("(s p j) t -> s p j t", s=PASSES, p=P, j=4)
         w1_view = w1.rearrange("(s p j) c -> s p j c", s=PASSES, p=P, j=4)
         gate_view = gate.rearrange("d p v -> p d v")
-        x_raw, w1_raw = {}, {}
+        w1_raw = {}
         gate_t = keep.tile([P, D, V], F32, name="gate_t")
 
         def load_w1(r):
@@ -73,16 +65,15 @@ def tile_picked_sage_none_e_kernel(tc, xT, w1, w2, gate, offs, pos1, pos2, pos3,
                 w1_raw[r, s] = shared.tile([P, 4, P], F32, name=f"w1_raw{r}{s}", offset=place, align_bytes=64)
                 nc.sync.dma_start(w1_raw[r, s][:], w1_view[s][:, :, r * P : r * P + P])
 
-        pass0_pieces = [n for n, piece in enumerate(X_PIECES) if piece[0] == 0]
-        x_pass0 = keep.tile([P, 4, T], F32, name="x_pass0")
-        nc.sync.dma_start(x_pass0[:], x_view[0])
         nc.sync.dma_start(offs_t[:], offs)
-        for n, (s, first, count, on_vector) in enumerate(X_PIECES):
-            if s == 0:
-                x_raw[n] = x_pass0[:, :, first : first + count]
-            else:
-                x_raw[n] = keep.tile([P, 4, count], F32, name=f"x_raw{n}")
-                nc.sync.dma_start(x_raw[n][:], x_view[s][:, :, first : first + count])
+        planes = {}
+        for s in range(PASSES):
+            for j in range(4):
+                if (s, j) == (PASSES - 1, 3):
+                    planes[s, j] = shared.tile([P, T], F32, name="last_plane", offset=PLANE_SLOT)
+                else:
+                    planes[s, j] = keep.tile([P, T], F32, name=f"plane{s}{j}")
+                nc.sync.dma_start(planes[s, j][:], x_view[s][:, j, :])
         load_w1(0)
         load_w1(1)
         nc.sync.dma_start(pos_t[0][:], pos1)
@@ -106,70 +97,55 @@ def tile_picked_sage_none_e_kernel(tc, xT, w1, w2, gate, offs, pos1, pos2, pos3,
         def round_rows(engine, dst, src):
             copy_on(engine, dst.rearrange("p (q c) j -> p q j c", c=4), src.rearrange("p j (q c) -> p q j c", c=4))
 
-        all_codes = [keep.tile([P, T], U32, name=f"all_codes{s}", align_bytes=64) for s in range(PASSES)]
+        picked_planes = [keep.tile([P, 4, S], F32, name=f"picked_planes{s}") for s in range(PASSES)]
+        x_codes, x_scales = {}, {}
 
-        def quantise_x(n):
-            s, first, count, on_vector = X_PIECES[n]
-            rounded = keep.tile([P, count, 4], BF16, name=f"x_bf16_{n}", align_bytes=64)
-            round_rows("scalar", rounded[:, on_vector:count], x_raw[n][:, :, on_vector:count])
-            if on_vector:
-                round_rows("vector", rounded[:, 0:on_vector], x_raw[n][:, :, 0:on_vector])
+        def quantise_x(s, a, b, rounded):
             nc.vector.quantize_mx(
-                out=all_codes[s][:, first : first + count].bitcast(FP8X4),
-                scales=all_scales[4 * s : P, first : first + count],
-                in_=rounded[:].rearrange("p n j -> p (n j)"),
+                out=x_codes[s][:, a:b].bitcast(FP8X4),
+                scales=x_scales[s][:, a:b],
+                in_=rounded.rearrange("p n j -> p (n j)"),
             )
-
-        codes0 = keep.tile([P, S], U32, name="codes0", align_bytes=64)
-        codes1 = [
-            keep.tile([P, LIST_HALF], U32, name="codes1a", align_bytes=64),
-            shared.tile([P, LIST_HALF], U32, name="codes1b", offset=HALF_SLOT, align_bytes=64),
-        ]
-        x_scales = [
-            keep.tile([P, LIST_HALF], U8, name="scales_a", align_bytes=64),
-            shared.tile([P, LIST_HALF], U8, name="scales_b", offset=HALF_SLOT + 4 * LIST_HALF, align_bytes=64),
-        ]
-
-        def picked_x(s, a, b):
-            part, first = divmod(a, LIST_HALF)
-            codes = codes0[:, a:b] if s == 0 else codes1[part][:, first : first + b - a]
-            return codes, x_scales[part][:, first : first + b - a]
 
         def entries_of(tile, a, b):
             return tile[:, a // PER_COLUMN : b // PER_COLUMN]
 
-        w1_codes, w1_scales, h_banks, h_tiles = {}, {}, {}, {}
+        w1_rounded, w1_codes, w1_scales, h_banks, h_tiles = {}, {}, {}, {}, {}
+
+        def round_w1(r):
+            if r == 0:
+                w1_rounded[r] = shared.tile([P, PASSES, P, 4], BF16, name="w1_bf16_0", offset=ROUNDED_SLOT, align_bytes=64)
+            else:
+                w1_rounded[r] = keep.tile([P, PASSES, P, 4], BF16, name=f"w1_bf16_{r}", align_bytes=64)
+            for s in range(PASSES):
+                round_rows("scalar", w1_rounded[r][:, s], w1_raw[r, s][:])
 
         def quantise_w1(r):
-            rounded = keep.tile([P, PASSES, P, 4], BF16, name=f"w1_bf16_{r}", align_bytes=64)
             w1_codes[r] = keep.tile([P, PASSES, P], U32, name=f"w1_codes{r}", align_bytes=64)
             w1_scales[r] = keep.tile([P, PASSES, P], U8, name=f"w1_scales{r}", align_bytes=64)
-            for s in range(PASSES):
-                round_rows("scalar", rounded[:, s], w1_raw[r, s][:])
             nc.vector.quantize_mx(
                 out=w1_codes[r][:].rearrange("p s c -> p (s c)").bitcast(FP8X4),
                 scales=w1_scales[r][:].rearrange("p s c -> p (s c)"),
-                in_=rounded[:].rearrange("p s c j -> p (s c j)"),
+                in_=w1_rounded[r][:].rearrange("p s c j -> p (s c j)"),
             )
 
         def project(r, a, b):
             for s in range(PASSES):
-                codes, scales = picked_x(s, a, b)
                 nc.tensor.matmul_mx(
                     out=h_banks[r][:, a:b],
                     lhsT=w1_codes[r][:, s, :].bitcast(FP8X4),
                     lhsT_scale=w1_scales[r][:, s, :],
-                    rhs=codes.bitcast(FP8X4),
-                    rhs_scale=scales[4 * s : P, :],
+                    rhs=x_codes[s][:, a:b].bitcast(FP8X4),
+                    rhs_scale=x_scales[s][:, a:b],
                     start=(s == 0),
                     stop=(s == PASSES - 1),
                 )
 
         def project_row(r):
+            round_w1(r)
             quantise_w1(r)
             h_banks[r] = ps_acc.tile([P, S], F32, name="acc")
-            for a in range(0, S, LIST_HALF):
-                project(r, a, a + LIST_HALF)
+            project(r, 0, S)
 
         def fetch_row(r):
             h_tiles[r] = shared.tile([P, S], F32, name=f"h{r}", offset=(r + 1) * SLOT)
@@ -283,22 +259,36 @@ def tile_picked_sage_none_e_kernel(tc, xT, w1, w2, gate, offs, pos1, pos2, pos3,
                 copy_on(copier[half], result[:, cols], acc[:, 0:P])
                 nc.sync.dma_start(out[:, cols], result[:, cols])
 
-        for n in range(len(X_PIECES)):
-            quantise_x(n)
-            if n == pass0_pieces[-1]:
-                nc.vector.tensor_copy(codes0[:], all_codes[0][:].indirect(offs_t[:]))
-        for a, b in FIRST_ROW_PARTS:
-            if a % LIST_HALF == 0:
-                entries = entries_of(offs_t, a, a + LIST_HALF)
-                nc.vector.tensor_copy(x_scales[a // LIST_HALF][:], all_scales[:].indirect(entries))
-            nc.vector.tensor_copy(picked_x(1, a, b)[0], all_codes[1][:].indirect(entries_of(offs_t, a, b)))
+        for s in range(PASSES):
+            for j in range(4):
+                for a, b in LAST_PLANE_PARTS if (s, j) == (PASSES - 1, 3) else ((0, S),):
+                    nc.vector.tensor_copy(picked_planes[s][:, j, a:b], planes[s, j][:].indirect(entries_of(offs_t, a, b)))
+            if s == 0:
+                x0_rounded = keep.tile([P, S, 4], BF16, name="x0_bf16", align_bytes=64)
+                round_rows("scalar", x0_rounded[:], picked_planes[0][:])
+        x1_rounded = {}
+        for a, b, engine, behind in X1_PARTS:
+            if behind is None:
+                x1_rounded[a] = keep.tile([P, b - a, 4], BF16, name=f"x1_bf16_{a}", align_bytes=64)
+            else:
+                x1_rounded[a] = shared.tile([P, b - a, 4], BF16, name=f"x1_bf16_{a}", offset=behind * HALF_SLOT + 8 * (a % LIST_HALF), align_bytes=64)
+        x_codes[0] = shared.tile([P, S], U32, name="x_codes0", offset=PLANE_SLOT, align_bytes=64)
+        x_scales[0] = keep.tile([P, S], U8, name="x_scales0", align_bytes=64)
+        x_scales[1] = keep.tile([P, S], U8, name="x_scales1", align_bytes=64)
+        h_tiles[0] = keep.tile([P, S], F32, name="h0")
+        round_w1(0)
+        for a, b, engine, behind in X1_PARTS:
+            round_rows(engine, x1_rounded[a][:], picked_planes[1][:, :, a:b])
             if a == 0:
+                quantise_x(0, 0, S, x0_rounded[:])
                 quantise_w1(0)
+        x_codes[1] = shared.tile([P, S], U32, name="x_codes1", offset=ROUNDED_SLOT, align_bytes=64)
+        for a, b, engine, behind in sorted(X1_PARTS, key=lambda part: (part[3] or 0)):
+            quantise_x(1, a, b, x1_rounded[a][:])
+        for a, b, engine in H0_PARTS:
             h_banks[0] = ps_acc.tile([P, S], F32, name="acc")
             project(0, a, b)
-            if a == 0:
-                h_tiles[0] = keep.tile([P, S], F32, name="h0")
-            nc.scalar.activation(h_tiles[0][:, a:b], h_banks[0][:, a:b], COPY)
+            copy_on(engine, h_tiles[0][:, a:b], h_banks[0][:, a:b])
         project_row(1)
 
         last_weights = ROWS - 1 - AHEAD

@@ -1,7 +1,6 @@
 from contextlib import ExitStack
 
 import concourse.mybir as mybir
-from concourse.masks import make_identity
 
 F32 = mybir.dt.float32
 BF16 = mybir.dt.bfloat16
@@ -12,6 +11,8 @@ U8 = mybir.dt.uint8
 FP8X4 = mybir.dt.float8_e4m3fn_x4
 COPY = mybir.ActivationFunctionType.Copy
 MULT = mybir.AluOpType.mult
+ADD = mybir.AluOpType.add
+IS_EQUAL = mybir.AluOpType.is_equal
 
 P = 128
 K, T, D, S, V, H, N = 1024, 1024, 3, 512, 256, 1024, 128
@@ -22,10 +23,11 @@ ROWS = H // P
 GROUP_ROWS = PASS // P
 HALVES = V // P
 LIST_HALF = S // 2
+QUAD = 32
 PER_COLUMN = 16
 
 X1_PARTS = ((0, 256, "vector", None), (256, 384, "vector", 1), (384, 512, "scalar", 0))
-H0_PARTS = ((0, 256, "scalar"), (384, 512, "vector"), (256, 384, "scalar"))
+H0_PARTS = ((0, 256, "scalar"), (256, 512, "vector"))
 LAST_PLANE_PARTS = ((0, 256), (256, 512))
 AHEAD = 2
 
@@ -52,10 +54,19 @@ def tile_picked_sage_none_e_kernel(tc, xT, w1, w2, gate, offs, pos1, pos2, pos3,
         offs_t = lists.tile([P, S // PER_COLUMN], U16, name="offs_t")
         pos_t = [lists.tile([P, V // PER_COLUMN], U16, name=f"pos_t{d}") for d in range(D)]
         ident = keep.tile([P, P], F32, name="ident")
-        make_identity(nc, ident[:])
+        ones = keep.tile([P, QUAD], F32, name="ones")
+        column_count = keep.tile([P, QUAD], F32, name="column_count", align_bytes=64)
+        partition_count = keep.tile([P, QUAD], F32, name="partition_count", align_bytes=64)
+        nc.vector.memset(ones[:], 1.0)
+        nc.vector.memset(ident[:], 0.0)
+        nc.vector.tensor_tensor_scan(column_count[:], ones[:], ones[:], 0.0, MULT, ADD)
+        nc.vector.transpose(partition_count[:], column_count[:])
+        for first in range(0, P, QUAD):
+            rows = slice(first, first + QUAD)
+            nc.vector.tensor_tensor(ident[rows, rows], column_count[rows], partition_count[rows], IS_EQUAL)
+
         x_view = xT.rearrange("(s p j) t -> s p j t", s=PASSES, p=P, j=4)
         w1_view = w1.rearrange("(s p j) c -> s p j c", s=PASSES, p=P, j=4)
-        gate_view = gate.rearrange("d p v -> p d v")
         w1_raw = {}
         gate_t = keep.tile([P, D, V], F32, name="gate_t")
 
@@ -65,7 +76,7 @@ def tile_picked_sage_none_e_kernel(tc, xT, w1, w2, gate, offs, pos1, pos2, pos3,
                 w1_raw[r, s] = shared.tile([P, 4, P], F32, name=f"w1_raw{r}{s}", offset=place, align_bytes=64)
                 nc.sync.dma_start(w1_raw[r, s][:], w1_view[s][:, :, r * P : r * P + P])
 
-        nc.sync.dma_start(offs_t[:], offs)
+        gate_rows = keep.tile([P, D, P], F32, name="gate_rows")
         planes = {}
         for s in range(PASSES):
             for j in range(4):
@@ -74,13 +85,34 @@ def tile_picked_sage_none_e_kernel(tc, xT, w1, w2, gate, offs, pos1, pos2, pos3,
                 else:
                     planes[s, j] = keep.tile([P, T], F32, name=f"plane{s}{j}")
                 nc.sync.dma_start(planes[s, j][:], x_view[s][:, j, :])
+                if (s, j) == (0, 0):
+                    nc.sync.dma_start(offs_t[:], offs)
+                    nc.sync.dma_start(gate_rows[P - HALVES : P], gate[:, 0, :].rearrange("d (h v) -> h d v", h=HALVES))
+        nc.vector.memset(gate_rows[0 : P - HALVES], 0.0)
+        turned_gate = ps_acc.tile([P, S], F32, name="acc")
+        for d in range(D):
+            nc.tensor.transpose(turned_gate[:, d * P : d * P + P], gate_rows[:, d, :], ident[:])
+        gate_columns = keep.tile([P, D, HALVES], F32, name="gate_columns")
+        nc.scalar.activation(
+            gate_columns[:], turned_gate[:, 0 : D * P].rearrange("v (d q) -> v d q", d=D)[:, :, P - HALVES : P], COPY
+        )
+        for first in range(0, D, 2):
+            turns = range(first, min(first + 2, D))
+            spread = ps_acc.tile([P, S], F32, name="acc")
+            for d in turns:
+                for half in range(HALVES):
+                    place = (d - first) * V + half * P
+                    column = gate_columns[:, d, half : half + 1].to_broadcast([P, P])
+                    nc.tensor.transpose(spread[:, place : place + P], column, ident[:])
+            nc.scalar.activation(
+                gate_t[:, first : first + len(turns), :].rearrange("p d v -> p (d v)"), spread[:, 0 : len(turns) * V], COPY
+            )
+
         load_w1(0)
         load_w1(1)
         nc.sync.dma_start(pos_t[0][:], pos1)
-        nc.sync.dma_start(gate_t[:, 0:2], gate_view[:, 0:2])
         nc.sync.dma_start(pos_t[1][:], pos2)
         load_w1(2)
-        nc.sync.dma_start(gate_t[:, 2], gate_view[:, 2])
         nc.sync.dma_start(pos_t[2][:], pos3)
         for r in range(3, ROWS - 1):
             load_w1(r)
@@ -129,23 +161,24 @@ def tile_picked_sage_none_e_kernel(tc, xT, w1, w2, gate, offs, pos1, pos2, pos3,
                 in_=w1_rounded[r][:].rearrange("p s c j -> p (s c j)"),
             )
 
-        def project(r, a, b):
-            for s in range(PASSES):
-                nc.tensor.matmul_mx(
-                    out=h_banks[r][:, a:b],
-                    lhsT=w1_codes[r][:, s, :].bitcast(FP8X4),
-                    lhsT_scale=w1_scales[r][:, s, :],
-                    rhs=x_codes[s][:, a:b].bitcast(FP8X4),
-                    rhs_scale=x_scales[s][:, a:b],
-                    start=(s == 0),
-                    stop=(s == PASSES - 1),
-                )
+        def project(bank, r, s, a, b):
+            nc.tensor.matmul_mx(
+                out=bank[:, a:b],
+                lhsT=w1_codes[r][:, s, :].bitcast(FP8X4),
+                lhsT_scale=w1_scales[r][:, s, :],
+                rhs=x_codes[s][:, a:b].bitcast(FP8X4),
+                rhs_scale=x_scales[s][:, a:b],
+                start=(s == 0),
+                stop=(s == PASSES - 1),
+            )
 
         def project_row(r):
-            round_w1(r)
-            quantise_w1(r)
+            if r > 1:
+                round_w1(r)
+                quantise_w1(r)
             h_banks[r] = ps_acc.tile([P, S], F32, name="acc")
-            project(r, 0, S)
+            for s in range(PASSES):
+                project(h_banks[r], r, s, 0, S)
 
         def fetch_row(r):
             h_tiles[r] = shared.tile([P, S], F32, name=f"h{r}", offset=(r + 1) * SLOT)
@@ -275,7 +308,6 @@ def tile_picked_sage_none_e_kernel(tc, xT, w1, w2, gate, offs, pos1, pos2, pos3,
         x_codes[0] = shared.tile([P, S], U32, name="x_codes0", offset=PLANE_SLOT, align_bytes=64)
         x_scales[0] = keep.tile([P, S], U8, name="x_scales0", align_bytes=64)
         x_scales[1] = keep.tile([P, S], U8, name="x_scales1", align_bytes=64)
-        h_tiles[0] = keep.tile([P, S], F32, name="h0")
         round_w1(0)
         for a, b, engine, behind in X1_PARTS:
             round_rows(engine, x1_rounded[a][:], picked_planes[1][:, :, a:b])
@@ -285,10 +317,15 @@ def tile_picked_sage_none_e_kernel(tc, xT, w1, w2, gate, offs, pos1, pos2, pos3,
         x_codes[1] = shared.tile([P, S], U32, name="x_codes1", offset=ROUNDED_SLOT, align_bytes=64)
         for a, b, engine, behind in sorted(X1_PARTS, key=lambda part: (part[3] or 0)):
             quantise_x(1, a, b, x1_rounded[a][:])
-        for a, b, engine in H0_PARTS:
-            h_banks[0] = ps_acc.tile([P, S], F32, name="acc")
-            project(0, a, b)
-            copy_on(engine, h_tiles[0][:, a:b], h_banks[0][:, a:b])
+        part_banks = [ps_acc.tile([P, S], F32, name="acc") for part in H0_PARTS]
+        for s in range(PASSES):
+            for bank, (a, b, engine) in zip(part_banks, H0_PARTS):
+                project(bank, 0, s, a, b)
+        round_w1(1)
+        quantise_w1(1)
+        h_tiles[0] = shared.tile([P, S], F32, name="h0", offset=SLOT + HALF_SLOT)
+        for bank, (a, b, engine) in zip(part_banks, H0_PARTS):
+            copy_on(engine, h_tiles[0][:, a:b], bank[:, a:b])
         project_row(1)
 
         last_weights = ROWS - 1 - AHEAD

@@ -26,16 +26,17 @@ LIST_HALF = S // 2
 QUAD = 32
 PER_COLUMN = 16
 
-X1_PARTS = ((0, 256, "vector", None), (256, 384, "vector", 1), (384, 512, "scalar", 0))
+X1_PARTS = ((0, 256, "vector", None), (256, 384, "vector", 0), (384, 512, "scalar", 0))
+Q_ORDER = (0, 1, 2)
 H0_PARTS = ((0, 256, "scalar"), (256, 512, "vector"))
 LAST_PLANE_PARTS = ((0, 256), (256, 512))
+SCALAR_PLANE = (1, 1)
+X0_ON_VECTOR = 256
 AHEAD = 2
 
 HALF_SLOT = 4 * P * 4
 SLOT = 2 * HALF_SLOT
 LAST_SLOT = ROWS * SLOT
-PLANE_SLOT = LAST_SLOT + SLOT
-ROUNDED_SLOT = PLANE_SLOT + 4 * T
 
 FLOPS = 2 * K * H * S + 2 * H * N * V
 
@@ -47,9 +48,12 @@ def tile_picked_sage_none_e_kernel(tc, xT, w1, w2, gate, offs, pos1, pos2, pos3,
         keep = ctx.enter_context(tc.tile_pool(name="keep", bufs=1))
         shared = ctx.enter_context(tc.tile_pool(name="shared", bufs=1))
         picks = ctx.enter_context(tc.tile_pool(name="picks", bufs=3))
-        ps_acc = ctx.enter_context(tc.psum_pool(name="ps_acc", bufs=3))
+        ps_acc = ctx.enter_context(tc.psum_pool(name="ps_acc", bufs=1))
         ps_z = ctx.enter_context(tc.psum_pool(name="ps_z", bufs=2))
         ps_back = ctx.enter_context(tc.psum_pool(name="ps_back", bufs=1))
+
+        def product_bank(n):
+            return ps_acc.tile([P, S], F32, name=f"acc{n % 3}")
 
         offs_t = lists.tile([P, S // PER_COLUMN], U16, name="offs_t")
         pos_t = [lists.tile([P, V // PER_COLUMN], U16, name=f"pos_t{d}") for d in range(D)]
@@ -80,16 +84,13 @@ def tile_picked_sage_none_e_kernel(tc, xT, w1, w2, gate, offs, pos1, pos2, pos3,
         planes = {}
         for s in range(PASSES):
             for j in range(4):
-                if (s, j) == (PASSES - 1, 3):
-                    planes[s, j] = shared.tile([P, T], F32, name="last_plane", offset=PLANE_SLOT)
-                else:
-                    planes[s, j] = keep.tile([P, T], F32, name=f"plane{s}{j}")
+                planes[s, j] = keep.tile([P, T], F32, name=f"plane{s}{j}")
                 nc.sync.dma_start(planes[s, j][:], x_view[s][:, j, :])
                 if (s, j) == (0, 0):
                     nc.sync.dma_start(offs_t[:], offs)
                     nc.sync.dma_start(gate_rows[P - HALVES : P], gate[:, 0, :].rearrange("d (h v) -> h d v", h=HALVES))
         nc.vector.memset(gate_rows[0 : P - HALVES], 0.0)
-        turned_gate = ps_acc.tile([P, S], F32, name="acc")
+        turned_gate = product_bank(0)
         for d in range(D):
             nc.tensor.transpose(turned_gate[:, d * P : d * P + P], gate_rows[:, d, :], ident[:])
         gate_columns = keep.tile([P, D, HALVES], F32, name="gate_columns")
@@ -98,7 +99,7 @@ def tile_picked_sage_none_e_kernel(tc, xT, w1, w2, gate, offs, pos1, pos2, pos3,
         )
         for first in range(0, D, 2):
             turns = range(first, min(first + 2, D))
-            spread = ps_acc.tile([P, S], F32, name="acc")
+            spread = product_bank(1 + first // 2)
             for d in turns:
                 for half in range(HALVES):
                     place = (d - first) * V + half * P
@@ -129,7 +130,7 @@ def tile_picked_sage_none_e_kernel(tc, xT, w1, w2, gate, offs, pos1, pos2, pos3,
         def round_rows(engine, dst, src):
             copy_on(engine, dst.rearrange("p (q c) j -> p q j c", c=4), src.rearrange("p j (q c) -> p q j c", c=4))
 
-        picked_planes = [keep.tile([P, 4, S], F32, name=f"picked_planes{s}") for s in range(PASSES)]
+        picked_planes = [keep.tile([P, 4, S], BF16 if s else F32, name=f"picked_planes{s}") for s in range(PASSES)]
         x_codes, x_scales = {}, {}
 
         def quantise_x(s, a, b, rounded):
@@ -144,21 +145,20 @@ def tile_picked_sage_none_e_kernel(tc, xT, w1, w2, gate, offs, pos1, pos2, pos3,
 
         w1_rounded, w1_codes, w1_scales, h_banks, h_tiles = {}, {}, {}, {}, {}
 
-        def round_w1(r):
-            if r == 0:
-                w1_rounded[r] = shared.tile([P, PASSES, P, 4], BF16, name="w1_bf16_0", offset=ROUNDED_SLOT, align_bytes=64)
-            else:
-                w1_rounded[r] = keep.tile([P, PASSES, P, 4], BF16, name=f"w1_bf16_{r}", align_bytes=64)
+        def round_w1(r, engines=("scalar", "scalar")):
+            w1_rounded[r] = keep.tile([P, PASSES, P, 4], BF16, name=f"w1_bf16_{r}", align_bytes=64)
             for s in range(PASSES):
-                round_rows("scalar", w1_rounded[r][:, s], w1_raw[r, s][:])
+                round_rows(engines[s], w1_rounded[r][:, s], w1_raw[r, s][:])
 
-        def quantise_w1(r):
-            w1_codes[r] = keep.tile([P, PASSES, P], U32, name=f"w1_codes{r}", align_bytes=64)
-            w1_scales[r] = keep.tile([P, PASSES, P], U8, name=f"w1_scales{r}", align_bytes=64)
+        def quantise_w1(r, first, passes):
+            if first == 0:
+                w1_codes[r] = keep.tile([P, PASSES, P], U32, name=f"w1_codes{r}", align_bytes=64)
+                w1_scales[r] = keep.tile([P, PASSES, P], U8, name=f"w1_scales{r}", align_bytes=64)
+            part = slice(first, first + passes)
             nc.vector.quantize_mx(
-                out=w1_codes[r][:].rearrange("p s c -> p (s c)").bitcast(FP8X4),
-                scales=w1_scales[r][:].rearrange("p s c -> p (s c)"),
-                in_=w1_rounded[r][:].rearrange("p s c j -> p (s c j)"),
+                out=w1_codes[r][:, part].rearrange("p s c -> p (s c)").bitcast(FP8X4),
+                scales=w1_scales[r][:, part].rearrange("p s c -> p (s c)"),
+                in_=w1_rounded[r][:, part].rearrange("p s c j -> p (s c j)"),
             )
 
         def project(bank, r, s, a, b):
@@ -175,8 +175,8 @@ def tile_picked_sage_none_e_kernel(tc, xT, w1, w2, gate, offs, pos1, pos2, pos3,
         def project_row(r):
             if r > 1:
                 round_w1(r)
-                quantise_w1(r)
-            h_banks[r] = ps_acc.tile([P, S], F32, name="acc")
+                quantise_w1(r, 0, PASSES)
+            h_banks[r] = product_bank(r)
             for s in range(PASSES):
                 project(h_banks[r], r, s, 0, S)
 
@@ -216,11 +216,14 @@ def tile_picked_sage_none_e_kernel(tc, xT, w1, w2, gate, offs, pos1, pos2, pos3,
             words = zT[g, half][:].rearrange("v u p e -> v (u p e)").bitcast(F32)
             nc.tensor.transpose(dst, words[:, u * P : u * P + P], ident[:])
 
-        def first_pass_back():
+        def first_pass_turn():
             turned = ps_back.tile([P, HALVES, 2, P], F32, name="turned")
             for half in range(HALVES):
                 for u in range(2):
                     turn_back(turned[:, half, u, :], 0, half, u)
+            return turned
+
+        def first_pass_back(turned):
             words = z0_rounded[:].rearrange("p h v j -> p (h v j)").bitcast(F32)
             nc.scalar.copy(
                 words.rearrange("p (h v u) -> p h v u", h=HALVES, u=2), turned[:].rearrange("p h u v -> p h v u")
@@ -229,7 +232,7 @@ def tile_picked_sage_none_e_kernel(tc, xT, w1, w2, gate, offs, pos1, pos2, pos3,
         def last_row_and_second_product():
             r, g_last = ROWS - 1, GROUPS - 1
             copier = ("scalar", "vector")
-            sums = [ps_acc.tile([P, S], F32, name="acc") for half in range(HALVES)]
+            sums = [product_bank(r + 1 + half) for half in range(HALVES)]
             for d, first, width in ((0, 0, V), (1, 0, V), (2, 0, P), (2, P, P)):
                 if first:
                     picked = shared.tile([P, P], F32, name="last_picked", offset=LAST_SLOT + HALF_SLOT)
@@ -277,7 +280,7 @@ def tile_picked_sage_none_e_kernel(tc, xT, w1, w2, gate, offs, pos1, pos2, pos3,
                     scales=z1_scales[:],
                     in_=z1_rounded[:].rearrange("p v j -> p (v j)"),
                 )
-                acc = ps_acc.tile([P, S], F32, name="acc")
+                acc = product_bank(r + half)
                 operands = ((z0_codes[:, cols], z0_scales[:, cols]), (z1_codes[:], z1_scales[:]))
                 for g, (codes, scales) in enumerate(operands):
                     nc.tensor.matmul_mx(
@@ -292,38 +295,45 @@ def tile_picked_sage_none_e_kernel(tc, xT, w1, w2, gate, offs, pos1, pos2, pos3,
                 copy_on(copier[half], result[:, cols], acc[:, 0:P])
                 nc.sync.dma_start(out[:, cols], result[:, cols])
 
+        x_codes[0] = keep.tile([P, S], U32, name="x_codes0", align_bytes=64)
+        x_scales[0] = keep.tile([P, S], U8, name="x_scales0", align_bytes=64)
         for s in range(PASSES):
             for j in range(4):
-                for a, b in LAST_PLANE_PARTS if (s, j) == (PASSES - 1, 3) else ((0, S),):
+                if (s, j) == SCALAR_PLANE:
+                    plane_bf16 = keep.tile([P, T], BF16, name="plane_bf16")
+                    nc.scalar.activation(plane_bf16[:], planes[s, j][:], COPY)
+                    nc.scalar.activation(picked_planes[s][:, j, :], plane_bf16[:].indirect(offs_t[:]), COPY)
+                    continue
+                for a, b in LAST_PLANE_PARTS if j == 3 else ((0, S),):
                     nc.vector.tensor_copy(picked_planes[s][:, j, a:b], planes[s, j][:].indirect(entries_of(offs_t, a, b)))
             if s == 0:
                 x0_rounded = keep.tile([P, S, 4], BF16, name="x0_bf16", align_bytes=64)
-                round_rows("scalar", x0_rounded[:], picked_planes[0][:])
+                round_rows("vector", x0_rounded[:, 0:X0_ON_VECTOR], picked_planes[0][:, :, 0:X0_ON_VECTOR])
+                round_rows("scalar", x0_rounded[:, X0_ON_VECTOR:S], picked_planes[0][:, :, X0_ON_VECTOR:S])
+                quantise_x(0, 0, S, x0_rounded[:])
         x1_rounded = {}
         for a, b, engine, behind in X1_PARTS:
             if behind is None:
                 x1_rounded[a] = keep.tile([P, b - a, 4], BF16, name=f"x1_bf16_{a}", align_bytes=64)
             else:
                 x1_rounded[a] = shared.tile([P, b - a, 4], BF16, name=f"x1_bf16_{a}", offset=behind * HALF_SLOT + 8 * (a % LIST_HALF), align_bytes=64)
-        x_codes[0] = shared.tile([P, S], U32, name="x_codes0", offset=PLANE_SLOT, align_bytes=64)
-        x_scales[0] = keep.tile([P, S], U8, name="x_scales0", align_bytes=64)
         x_scales[1] = keep.tile([P, S], U8, name="x_scales1", align_bytes=64)
         round_w1(0)
         for a, b, engine, behind in X1_PARTS:
             round_rows(engine, x1_rounded[a][:], picked_planes[1][:, :, a:b])
             if a == 0:
-                quantise_x(0, 0, S, x0_rounded[:])
-                quantise_w1(0)
-        x_codes[1] = shared.tile([P, S], U32, name="x_codes1", offset=ROUNDED_SLOT, align_bytes=64)
-        for a, b, engine, behind in sorted(X1_PARTS, key=lambda part: (part[3] or 0)):
+                quantise_w1(0, 0, 1)
+        quantise_w1(0, 1, 1)
+        x_codes[1] = shared.tile([P, S], U32, name="x_codes1", offset=HALF_SLOT, align_bytes=64)
+        for a, b, engine, behind in [X1_PARTS[n] for n in Q_ORDER]:
             quantise_x(1, a, b, x1_rounded[a][:])
-        part_banks = [ps_acc.tile([P, S], F32, name="acc") for part in H0_PARTS]
+        part_banks = [product_bank(0), product_bank(2)]
         for s in range(PASSES):
             for bank, (a, b, engine) in zip(part_banks, H0_PARTS):
                 project(bank, 0, s, a, b)
-        round_w1(1)
-        quantise_w1(1)
-        h_tiles[0] = shared.tile([P, S], F32, name="h0", offset=SLOT + HALF_SLOT)
+        round_w1(1, ("scalar", "vector"))
+        quantise_w1(1, 0, PASSES)
+        h_tiles[0] = keep.tile([P, S], F32, name="h0")
         for bank, (a, b, engine) in zip(part_banks, H0_PARTS):
             copy_on(engine, h_tiles[0][:, a:b], bank[:, a:b])
         project_row(1)
@@ -341,9 +351,10 @@ def tile_picked_sage_none_e_kernel(tc, xT, w1, w2, gate, offs, pos1, pos2, pos3,
             fetch_row(r + 1)
             if r == last_weights:
                 round_z("scalar", 0, 1, z_banks[0, 1][:], 0, GROUP_ROWS)
+                turned0 = first_pass_turn()
                 round_rows("scalar", w2_rounded[:, 1], w2_raw[:, 1])
             if r == last_weights + 1:
-                first_pass_back()
+                first_pass_back(turned0)
             pick_neighbours(r, 2)
         for half in range(HALVES):
             round_z("scalar", 1, half, z_banks[1, half][:, 0 : (GROUP_ROWS - 1) * P], 0, GROUP_ROWS - 1)

@@ -28,10 +28,14 @@ PER_COLUMN = 16
 
 X1_PARTS = ((0, 256, "vector", None), (256, 384, "vector", 0), (384, 512, "scalar", 0))
 Q_ORDER = (0, 1, 2)
-H0_PARTS = ((0, 256, "scalar"), (256, 512, "vector"))
+H0_PARTS = ((0, 256, "scalar"), (256, 384, "vector"), (384, 512, "scalar"))
 LAST_PLANE_PARTS = ((0, 256), (256, 512))
 SCALAR_PLANE = (1, 1)
-X0_ON_VECTOR = 256
+X0_PARTS = ((0, 192, "scalar"), (192, 384, "vector"), (384, 512, "scalar"))
+SCALAR_PARTS = ((0, 512),)
+WARM = 16
+R1 = ("scalar", "scalar")
+R0 = ("scalar", "scalar")
 AHEAD = 2
 
 HALF_SLOT = 4 * P * 4
@@ -302,15 +306,27 @@ def tile_picked_sage_none_e_kernel(tc, xT, w1, w2, gate, offs, pos1, pos2, pos3,
                 if (s, j) == SCALAR_PLANE:
                     plane_bf16 = keep.tile([P, T], BF16, name="plane_bf16")
                     nc.scalar.activation(plane_bf16[:], planes[s, j][:], COPY)
-                    nc.scalar.activation(picked_planes[s][:, j, :], plane_bf16[:].indirect(offs_t[:]), COPY)
+                    for a, b in SCALAR_PARTS:
+                        nc.scalar.activation(picked_planes[s][:, j, a:b], plane_bf16[:].indirect(entries_of(offs_t, a, b)), COPY)
                     continue
-                for a, b in LAST_PLANE_PARTS if j == 3 else ((0, S),):
+                for a, b in ([part[:2] for part in X0_PARTS] if s == 0 else LAST_PLANE_PARTS) if j == 3 else ((0, S),):
                     nc.vector.tensor_copy(picked_planes[s][:, j, a:b], planes[s, j][:].indirect(entries_of(offs_t, a, b)))
             if s == 0:
                 x0_rounded = keep.tile([P, S, 4], BF16, name="x0_bf16", align_bytes=64)
-                round_rows("vector", x0_rounded[:, 0:X0_ON_VECTOR], picked_planes[0][:, :, 0:X0_ON_VECTOR])
-                round_rows("scalar", x0_rounded[:, X0_ON_VECTOR:S], picked_planes[0][:, :, X0_ON_VECTOR:S])
+                for a, b, engine in X0_PARTS:
+                    round_rows(engine, x0_rounded[:, a:b], picked_planes[0][:, :, a:b])
                 quantise_x(0, 0, S, x0_rounded[:])
+                warm_bank = ps_back.tile([P, HALVES, 2, P], F32, name="turned")
+                for n in range(WARM):
+                    nc.tensor.matmul_mx(
+                        out=warm_bank[:, 0, 0, :],
+                        lhsT=x_codes[0][:, 0:P].bitcast(FP8X4),
+                        lhsT_scale=x_scales[0][:, 0:P],
+                        rhs=x_codes[0][:, P : 2 * P].bitcast(FP8X4),
+                        rhs_scale=x_scales[0][:, P : 2 * P],
+                        start=True,
+                        stop=True,
+                    )
         x1_rounded = {}
         for a, b, engine, behind in X1_PARTS:
             if behind is None:
@@ -318,7 +334,7 @@ def tile_picked_sage_none_e_kernel(tc, xT, w1, w2, gate, offs, pos1, pos2, pos3,
             else:
                 x1_rounded[a] = shared.tile([P, b - a, 4], BF16, name=f"x1_bf16_{a}", offset=behind * HALF_SLOT + 8 * (a % LIST_HALF), align_bytes=64)
         x_scales[1] = keep.tile([P, S], U8, name="x_scales1", align_bytes=64)
-        round_w1(0)
+        round_w1(0, R0)
         for a, b, engine, behind in X1_PARTS:
             round_rows(engine, x1_rounded[a][:], picked_planes[1][:, :, a:b])
             if a == 0:
@@ -327,11 +343,11 @@ def tile_picked_sage_none_e_kernel(tc, xT, w1, w2, gate, offs, pos1, pos2, pos3,
         x_codes[1] = shared.tile([P, S], U32, name="x_codes1", offset=HALF_SLOT, align_bytes=64)
         for a, b, engine, behind in [X1_PARTS[n] for n in Q_ORDER]:
             quantise_x(1, a, b, x1_rounded[a][:])
-        part_banks = [product_bank(0), product_bank(2)]
+        part_banks = [product_bank(0), product_bank(2), ps_z.tile([P, PASS], F32, name="z_bank0")]
         for s in range(PASSES):
             for bank, (a, b, engine) in zip(part_banks, H0_PARTS):
                 project(bank, 0, s, a, b)
-        round_w1(1, ("scalar", "vector"))
+        round_w1(1, R1)
         quantise_w1(1, 0, PASSES)
         h_tiles[0] = keep.tile([P, S], F32, name="h0")
         for bank, (a, b, engine) in zip(part_banks, H0_PARTS):

@@ -134,7 +134,7 @@ def tile_picked_sage_none_e_kernel(tc, xT, w1, w2, gate, offs, pos1, pos2, pos3,
         def round_rows(engine, dst, src):
             copy_on(engine, dst.rearrange("p (q c) j -> p q j c", c=4), src.rearrange("p j (q c) -> p q j c", c=4))
 
-        picked_planes = [keep.tile([P, 4, S], BF16 if s else F32, name=f"picked_planes{s}") for s in range(PASSES)]
+        picked_planes = [keep.tile([P, 4, S], BF16, name=f"picked_planes{s}") for s in range(PASSES)]
         x_codes, x_scales = {}, {}
 
         def quantise_x(s, a, b, rounded):

@@ -4,7 +4,6 @@ import concourse.mybir as mybir
 
 F32 = mybir.dt.float32
 BF16 = mybir.dt.bfloat16
-I32 = mybir.dt.int32
 U32 = mybir.dt.uint32
 U16 = mybir.dt.uint16
 U8 = mybir.dt.uint8
@@ -23,23 +22,22 @@ ROWS = H // P
 GROUP_ROWS = PASS // P
 HALVES = V // P
 LIST_HALF = S // 2
+LIST_QUARTER = S // 4
 QUAD = 32
 PER_COLUMN = 16
 
-X1_PARTS = ((0, 256, "vector", None), (256, 384, "vector", 0), (384, 512, "scalar", 0))
-Q_ORDER = (0, 1, 2)
-H0_PARTS = ((0, 256, "scalar"), (256, 384, "vector"), (384, 512, "scalar"))
-LAST_PLANE_PARTS = ((0, 256), (256, 512))
 SCALAR_PLANE = (1, 1)
-X0_PARTS = ((0, 192, "scalar"), (192, 384, "vector"), (384, 512, "scalar"))
-SCALAR_PARTS = ((0, 512),)
-WARM = 16
-R1 = ("scalar", "scalar")
-R0 = ("scalar", "scalar")
+PASS0_PARTS = ((0, 192, "scalar"), (192, 384, "vector"), (384, S, "scalar"))
+PASS1_PARTS = (
+    (0, LIST_HALF, "vector", "scalar"),
+    (LIST_HALF, LIST_HALF + LIST_QUARTER, "vector", "vector"),
+    (LIST_HALF + LIST_QUARTER, S, "scalar", "scalar"),
+)
 AHEAD = 2
 
 HALF_SLOT = 4 * P * 4
 SLOT = 2 * HALF_SLOT
+NODE_BYTES = 4 * 2
 LAST_SLOT = ROWS * SLOT
 
 FLOPS = 2 * K * H * S + 2 * H * N * V
@@ -131,17 +129,17 @@ def tile_picked_sage_none_e_kernel(tc, xT, w1, w2, gate, offs, pos1, pos2, pos3,
             else:
                 nc.scalar.activation(dst, src, COPY)
 
-        def round_rows(engine, dst, src):
+        def interleave(engine, dst, src):
             copy_on(engine, dst.rearrange("p (q c) j -> p q j c", c=4), src.rearrange("p j (q c) -> p q j c", c=4))
 
         picked_planes = [keep.tile([P, 4, S], BF16, name=f"picked_planes{s}") for s in range(PASSES)]
         x_codes, x_scales = {}, {}
 
-        def quantise_x(s, a, b, rounded):
+        def quantise_x(s, a, b, interleaved):
             nc.vector.quantize_mx(
                 out=x_codes[s][:, a:b].bitcast(FP8X4),
                 scales=x_scales[s][:, a:b],
-                in_=rounded.rearrange("p n j -> p (n j)"),
+                in_=interleaved.rearrange("p n j -> p (n j)"),
             )
 
         def entries_of(tile, a, b):
@@ -149,10 +147,10 @@ def tile_picked_sage_none_e_kernel(tc, xT, w1, w2, gate, offs, pos1, pos2, pos3,
 
         w1_rounded, w1_codes, w1_scales, h_banks, h_tiles = {}, {}, {}, {}, {}
 
-        def round_w1(r, engines=("scalar", "scalar")):
+        def round_w1(r):
             w1_rounded[r] = keep.tile([P, PASSES, P, 4], BF16, name=f"w1_bf16_{r}", align_bytes=64)
             for s in range(PASSES):
-                round_rows(engines[s], w1_rounded[r][:, s], w1_raw[r, s][:])
+                interleave("scalar", w1_rounded[r][:, s], w1_raw[r, s][:])
 
         def quantise_w1(r, first, passes):
             if first == 0:
@@ -177,9 +175,6 @@ def tile_picked_sage_none_e_kernel(tc, xT, w1, w2, gate, offs, pos1, pos2, pos3,
             )
 
         def project_row(r):
-            if r > 1:
-                round_w1(r)
-                quantise_w1(r, 0, PASSES)
             h_banks[r] = product_bank(r)
             for s in range(PASSES):
                 project(h_banks[r], r, s, 0, S)
@@ -299,59 +294,56 @@ def tile_picked_sage_none_e_kernel(tc, xT, w1, w2, gate, offs, pos1, pos2, pos3,
                 copy_on(copier[half], result[:, cols], acc[:, 0:P])
                 nc.sync.dma_start(out[:, cols], result[:, cols])
 
+        def pick_plane(s, j, parts):
+            if (s, j) == SCALAR_PLANE:
+                plane_bf16 = keep.tile([P, T], BF16, name="plane_bf16")
+                nc.scalar.activation(plane_bf16[:], planes[s, j][:], COPY)
+                nc.scalar.activation(picked_planes[s][:, j, :], plane_bf16[:].indirect(offs_t[:]), COPY)
+                return
+            for a, b in parts:
+                nc.vector.tensor_copy(picked_planes[s][:, j, a:b], planes[s, j][:].indirect(entries_of(offs_t, a, b)))
+
+        whole_list = ((0, S),)
         x_codes[0] = keep.tile([P, S], U32, name="x_codes0", align_bytes=64)
         x_scales[0] = keep.tile([P, S], U8, name="x_scales0", align_bytes=64)
-        for s in range(PASSES):
-            for j in range(4):
-                if (s, j) == SCALAR_PLANE:
-                    plane_bf16 = keep.tile([P, T], BF16, name="plane_bf16")
-                    nc.scalar.activation(plane_bf16[:], planes[s, j][:], COPY)
-                    for a, b in SCALAR_PARTS:
-                        nc.scalar.activation(picked_planes[s][:, j, a:b], plane_bf16[:].indirect(entries_of(offs_t, a, b)), COPY)
-                    continue
-                for a, b in ([part[:2] for part in X0_PARTS] if s == 0 else LAST_PLANE_PARTS) if j == 3 else ((0, S),):
-                    nc.vector.tensor_copy(picked_planes[s][:, j, a:b], planes[s, j][:].indirect(entries_of(offs_t, a, b)))
-            if s == 0:
-                x0_rounded = keep.tile([P, S, 4], BF16, name="x0_bf16", align_bytes=64)
-                for a, b, engine in X0_PARTS:
-                    round_rows(engine, x0_rounded[:, a:b], picked_planes[0][:, :, a:b])
-                quantise_x(0, 0, S, x0_rounded[:])
-                warm_bank = ps_back.tile([P, HALVES, 2, P], F32, name="turned")
-                for n in range(WARM):
-                    nc.tensor.matmul_mx(
-                        out=warm_bank[:, 0, 0, :],
-                        lhsT=x_codes[0][:, 0:P].bitcast(FP8X4),
-                        lhsT_scale=x_scales[0][:, 0:P],
-                        rhs=x_codes[0][:, P : 2 * P].bitcast(FP8X4),
-                        rhs_scale=x_scales[0][:, P : 2 * P],
-                        start=True,
-                        stop=True,
-                    )
-        x1_rounded = {}
-        for a, b, engine, behind in X1_PARTS:
-            if behind is None:
-                x1_rounded[a] = keep.tile([P, b - a, 4], BF16, name=f"x1_bf16_{a}", align_bytes=64)
+        for j in range(3):
+            pick_plane(0, j, whole_list)
+        pick_plane(0, 3, [(a, b) for a, b, engine in PASS0_PARTS])
+        x0_interleaved = keep.tile([P, S, 4], BF16, name="x0_bf16", align_bytes=64)
+        for a, b, engine in PASS0_PARTS:
+            interleave(engine, x0_interleaved[:, a:b], picked_planes[0][:, :, a:b])
+        quantise_x(0, 0, S, x0_interleaved[:])
+
+        for j in range(3):
+            pick_plane(1, j, whole_list)
+        pick_plane(1, 3, ((0, LIST_HALF), (LIST_HALF, S)))
+        x1_interleaved = {}
+        for a, b, interleaver, copier in PASS1_PARTS:
+            shape, name = [P, b - a, 4], f"x1_bf16_{a}"
+            if a < LIST_HALF:
+                x1_interleaved[a] = keep.tile(shape, BF16, name=name, align_bytes=64)
             else:
-                x1_rounded[a] = shared.tile([P, b - a, 4], BF16, name=f"x1_bf16_{a}", offset=behind * HALF_SLOT + 8 * (a % LIST_HALF), align_bytes=64)
+                place = NODE_BYTES * (a - LIST_HALF)
+                x1_interleaved[a] = shared.tile(shape, BF16, name=name, offset=place, align_bytes=64)
         x_scales[1] = keep.tile([P, S], U8, name="x_scales1", align_bytes=64)
-        round_w1(0, R0)
-        for a, b, engine, behind in X1_PARTS:
-            round_rows(engine, x1_rounded[a][:], picked_planes[1][:, :, a:b])
+        round_w1(0)
+        for a, b, interleaver, copier in PASS1_PARTS:
+            interleave(interleaver, x1_interleaved[a][:], picked_planes[1][:, :, a:b])
             if a == 0:
                 quantise_w1(0, 0, 1)
         quantise_w1(0, 1, 1)
         x_codes[1] = shared.tile([P, S], U32, name="x_codes1", offset=HALF_SLOT, align_bytes=64)
-        for a, b, engine, behind in [X1_PARTS[n] for n in Q_ORDER]:
-            quantise_x(1, a, b, x1_rounded[a][:])
+        for a, b, interleaver, copier in PASS1_PARTS:
+            quantise_x(1, a, b, x1_interleaved[a][:])
         part_banks = [product_bank(0), product_bank(2), ps_z.tile([P, PASS], F32, name="z_bank0")]
         for s in range(PASSES):
-            for bank, (a, b, engine) in zip(part_banks, H0_PARTS):
+            for bank, (a, b, interleaver, copier) in zip(part_banks, PASS1_PARTS):
                 project(bank, 0, s, a, b)
-        round_w1(1, R1)
+        round_w1(1)
         quantise_w1(1, 0, PASSES)
         h_tiles[0] = keep.tile([P, S], F32, name="h0")
-        for bank, (a, b, engine) in zip(part_banks, H0_PARTS):
-            copy_on(engine, h_tiles[0][:, a:b], bank[:, a:b])
+        for bank, (a, b, interleaver, copier) in zip(part_banks, PASS1_PARTS):
+            copy_on(copier, h_tiles[0][:, a:b], bank[:, a:b])
         project_row(1)
 
         last_weights = ROWS - 1 - AHEAD
@@ -359,16 +351,18 @@ def tile_picked_sage_none_e_kernel(tc, xT, w1, w2, gate, offs, pos1, pos2, pos3,
             pick_neighbours(r, 0)
             pick_neighbours(r, 1)
             if r <= last_weights:
+                round_w1(r + AHEAD)
+                quantise_w1(r + AHEAD, 0, PASSES)
                 project_row(r + AHEAD)
             if r == last_weights - 1:
-                round_rows("scalar", w2_rounded[:, 0], w2_raw[:, 0])
+                interleave("scalar", w2_rounded[:, 0], w2_raw[:, 0])
             if r == last_weights:
                 round_z("scalar", 0, 0, z_banks[0, 0][:], 0, GROUP_ROWS)
             fetch_row(r + 1)
             if r == last_weights:
                 round_z("scalar", 0, 1, z_banks[0, 1][:], 0, GROUP_ROWS)
                 turned0 = first_pass_turn()
-                round_rows("scalar", w2_rounded[:, 1], w2_raw[:, 1])
+                interleave("scalar", w2_rounded[:, 1], w2_raw[:, 1])
             if r == last_weights + 1:
                 first_pass_back(turned0)
             pick_neighbours(r, 2)

@@ -33,12 +33,19 @@ PASS1_PARTS = (
     (LIST_HALF, LIST_HALF + LIST_QUARTER, "vector", "vector"),
     (LIST_HALF + LIST_QUARTER, S, "scalar", "scalar"),
 )
+HELD_BY_WIDE = {2: 1, 3: 3, 4: 2}
 AHEAD = 2
 
 HALF_SLOT = 4 * P * 4
 SLOT = 2 * HALF_SLOT
 NODE_BYTES = 4 * 2
-LAST_SLOT = ROWS * SLOT
+PLAIN_ROWS = GROUP_ROWS
+WIDE_SLOTS = PLAIN_ROWS * SLOT
+QUARTER_SLOT = SLOT // 4
+LAST_SLOT = WIDE_SLOTS + 4 * SLOT + QUARTER_SLOT
+BLOCK = 32
+RUN = 8
+WIDE = 2 * P
 
 FLOPS = 2 * K * H * S + 2 * H * N * V
 
@@ -51,7 +58,7 @@ def tile_picked_sage_none_e_kernel(tc, xT, w1, w2, gate, offs, pos1, pos2, pos3,
         shared = ctx.enter_context(tc.tile_pool(name="shared", bufs=1))
         picks = ctx.enter_context(tc.tile_pool(name="picks", bufs=3))
         ps_acc = ctx.enter_context(tc.psum_pool(name="ps_acc", bufs=1))
-        ps_z = ctx.enter_context(tc.psum_pool(name="ps_z", bufs=2))
+        ps_z = ctx.enter_context(tc.psum_pool(name="ps_z", bufs=1))
         ps_back = ctx.enter_context(tc.psum_pool(name="ps_back", bufs=1))
 
         def product_bank(n):
@@ -117,11 +124,18 @@ def tile_picked_sage_none_e_kernel(tc, xT, w1, w2, gate, offs, pos1, pos2, pos3,
         nc.sync.dma_start(pos_t[1][:], pos2)
         load_w1(2)
         nc.sync.dma_start(pos_t[2][:], pos3)
-        for r in range(3, ROWS - 1):
-            load_w1(r)
-        w2_raw = keep.tile([P, GROUPS, 4, N], F32, name="w2_raw")
-        nc.sync.dma_start(w2_raw[:], w2.rearrange("(g p j) n -> p g j n", g=GROUPS, j=4))
-        load_w1(ROWS - 1)
+        load_w1(3)
+        w1_wide = {}
+        for c in range(2):
+            for s in range(PASSES):
+                place = WIDE_SLOTS + (2 * c + s) * SLOT
+                w1_wide[c, s] = shared.tile([P, 4, WIDE], F32, name=f"w1_wide{c}{s}", offset=place, align_bytes=64)
+                nc.sync.dma_start(w1_wide[c, s][:], w1_view[s][:, :, PASS + c * WIDE : PASS + (c + 1) * WIDE])
+        w2_raw = [keep.tile([P, 4, N], F32, name=f"w2_raw{g}") for g in range(GROUPS)]
+        nc.sync.dma_start(w2_raw[0][:], w2[0:PASS].rearrange("(p j) n -> p j n", j=4))
+        w2_dealt = w2[PASS:H].rearrange("(b j a) n -> j b a n", j=4, a=RUN)
+        for j in range(4):
+            nc.sync.dma_start(w2_raw[1][:, j, :], w2_dealt[j])
 
         def copy_on(engine, dst, src):
             if engine == "vector":
@@ -146,11 +160,40 @@ def tile_picked_sage_none_e_kernel(tc, xT, w1, w2, gate, offs, pos1, pos2, pos3,
             return tile[:, a // PER_COLUMN : b // PER_COLUMN]
 
         w1_rounded, w1_codes, w1_scales, h_banks, h_tiles = {}, {}, {}, {}, {}
+        high_codes, high_scales = {}, {}
+
+        def deal(dst, raw, first, width):
+            runs = raw[:].rearrange("p j (b w) -> p b j w", w=BLOCK)[:, :, :, first : first + width]
+            nc.scalar.copy(
+                dst.rearrange("p (b q c) j -> p b q j c", q=width // 4, c=4), runs.rearrange("p b j (q c) -> p b q j c", c=4)
+            )
 
         def round_w1(r):
             w1_rounded[r] = keep.tile([P, PASSES, P, 4], BF16, name=f"w1_bf16_{r}", align_bytes=64)
             for s in range(PASSES):
-                interleave("scalar", w1_rounded[r][:, s], w1_raw[r, s][:])
+                if r < PLAIN_ROWS:
+                    interleave("scalar", w1_rounded[r][:, s], w1_raw[r, s][:])
+                else:
+                    deal(w1_rounded[r][:, s], w1_wide[r - PLAIN_ROWS, s], 0, 2 * RUN)
+
+        high_rounded = {}
+
+        def round_high(c, s):
+            if c == 0 and s == 0:
+                high_rounded[s] = shared.tile([P, 2, P, 4], BF16, name="w1_high0", offset=LAST_SLOT - HALF_SLOT, align_bytes=64)
+            elif c == 0:
+                high_rounded[s] = keep.tile([P, 2, P, 4], BF16, name="w1_high1", align_bytes=64)
+            for e in range(2):
+                deal(high_rounded[s][:, e, c * P // 2 : (c + 1) * P // 2], w1_wide[c, s], (2 + e) * RUN, RUN)
+
+        def quantise_high(s):
+            high_codes[s] = keep.tile([P, 2, P], U32, name=f"high_codes{s}", align_bytes=64)
+            high_scales[s] = keep.tile([P, 2, P], U8, name=f"high_scales{s}", align_bytes=64)
+            nc.vector.quantize_mx(
+                out=high_codes[s][:].rearrange("p e c -> p (e c)").bitcast(FP8X4),
+                scales=high_scales[s][:].rearrange("p e c -> p (e c)"),
+                in_=high_rounded[s][:].rearrange("p e c j -> p (e c j)"),
+            )
 
         def quantise_w1(r, first, passes):
             if first == 0:
@@ -164,10 +207,14 @@ def tile_picked_sage_none_e_kernel(tc, xT, w1, w2, gate, offs, pos1, pos2, pos3,
             )
 
         def project(bank, r, s, a, b):
+            if r < ROWS - 2:
+                codes, scales = w1_codes[r][:, s, :], w1_scales[r][:, s, :]
+            else:
+                codes, scales = high_codes[s][:, r - ROWS + 2, :], high_scales[s][:, r - ROWS + 2, :]
             nc.tensor.matmul_mx(
                 out=bank[:, a:b],
-                lhsT=w1_codes[r][:, s, :].bitcast(FP8X4),
-                lhsT_scale=w1_scales[r][:, s, :],
+                lhsT=codes.bitcast(FP8X4),
+                lhsT_scale=scales,
                 rhs=x_codes[s][:, a:b].bitcast(FP8X4),
                 rhs_scale=x_scales[s][:, a:b],
                 start=(s == 0),
@@ -180,12 +227,17 @@ def tile_picked_sage_none_e_kernel(tc, xT, w1, w2, gate, offs, pos1, pos2, pos3,
                 project(h_banks[r], r, s, 0, S)
 
         def fetch_row(r):
-            h_tiles[r] = shared.tile([P, S], F32, name=f"h{r}", offset=(r + 1) * SLOT)
+            if r + 1 < PLAIN_ROWS:
+                h_tiles[r] = shared.tile([P, S], F32, name=f"h{r}", offset=(r + 1) * SLOT)
+            elif r < ROWS - 2:
+                place = WIDE_SLOTS + HELD_BY_WIDE[r - 1] * SLOT + QUARTER_SLOT
+                h_tiles[r] = shared.tile([P, S], F32, name=f"h{r}", offset=place)
+            else:
+                h_tiles[r] = shared.tile([P, S], F32, name=f"h{r}", offset=LAST_SLOT + (r - ROWS + 2) * HALF_SLOT)
             nc.scalar.activation(h_tiles[r][:], h_banks[r][:], COPY)
 
-        zT = {
-            (g, half): keep.tile([P, 2, P, 2], BF16, name=f"zT{g}{half}") for g in range(GROUPS) for half in range(HALVES)
-        }
+        zT = {(0, half): keep.tile([P, 2, P, 2], BF16, name=f"zT0{half}") for half in range(HALVES)}
+        z1_rounded = [keep.tile([P, P, 4], BF16, name=f"z1_bf16_{half}", align_bytes=64) for half in range(HALVES)]
         w2_scales = keep.tile([P, GROUPS, N], U8, name="w2_scales", align_bytes=64)
         w2_rounded = keep.tile([P, GROUPS, N, 4], BF16, name="w2_bf16", align_bytes=64)
         z0_rounded = keep.tile([P, HALVES, P, 4], BF16, name="z0_bf16", align_bytes=64)
@@ -198,9 +250,11 @@ def tile_picked_sage_none_e_kernel(tc, xT, w1, w2, gate, offs, pos1, pos2, pos3,
             g, place = divmod(r, GROUP_ROWS)
             if place == 0 and d == 0:
                 for half in range(HALVES):
-                    z_banks[g, half] = ps_z.tile([P, PASS], F32, name=f"z_bank{half}")
-            if d == D - 1 and r + AHEAD < ROWS:
+                    z_banks[g, half] = ps_z.tile([P, PASS], F32, name=f"z_bank{g}{half}")
+            if d == D - 1 and r + AHEAD < PLAIN_ROWS:
                 picked = shared.tile([P, V], F32, name=f"third{r}", offset=(r + AHEAD) * SLOT + HALF_SLOT)
+            elif d == D - 1 and r in HELD_BY_WIDE:
+                picked = shared.tile([P, V], F32, name=f"third{r}", offset=WIDE_SLOTS + HELD_BY_WIDE[r] * SLOT)
             else:
                 picked = picks.tile([P, V], F32, name=f"picked{d}")
             nc.vector.tensor_tensor(picked[:], h_tiles[r][:].indirect(pos_t[d][:]), gate_t[:, d, :], MULT)
@@ -228,27 +282,49 @@ def tile_picked_sage_none_e_kernel(tc, xT, w1, w2, gate, offs, pos1, pos2, pos3,
                 words.rearrange("p (h v u) -> p h v u", h=HALVES, u=2), turned[:].rearrange("p h u v -> p h v u")
             )
 
-        def last_row_and_second_product():
-            r, g_last = ROWS - 1, GROUPS - 1
-            copier = ("scalar", "vector")
-            sums = [product_bank(r + 1 + half) for half in range(HALVES)]
-            for d, first, width in ((0, 0, V), (1, 0, V), (2, 0, P), (2, P, P)):
-                if first:
-                    picked = shared.tile([P, P], F32, name="last_picked", offset=LAST_SLOT + HALF_SLOT)
-                else:
-                    picked = picks.tile([P, width], F32, name=f"picked{d}")
-                entries = entries_of(pos_t[d], first, first + width)
-                nc.vector.tensor_tensor(
-                    picked[:], h_tiles[r][:].indirect(entries), gate_t[:, d, first : first + width], MULT
-                )
-                for a in range(0, width, P):
-                    add_turned(sums[(first + a) // P][:, 0:P], picked[:, a : a + P], d)
+        def low_slots_turn():
+            turned = product_bank(ROWS)[:, 0 : HALVES * P].rearrange("p (h v) -> p h v", h=HALVES)
             for half in range(HALVES):
-                round_z(copier[half], g_last, half, sums[half][:, 0:P], GROUP_ROWS - 1, 1)
-            turned = [ps_z.tile([P, PASS], F32, name=f"z_bank{half}") for half in range(HALVES)]
+                pairs = keep.tile([P, P, 2], BF16, name=f"zT1{half}")
+                sums = z_banks[1, half][:, 0 : 2 * P].rearrange("v (b e a) -> v b a e", e=2, a=RUN)
+                copy_on("scalar", pairs[:].rearrange("v (b a) e -> v b a e", a=RUN), sums)
+                nc.tensor.transpose(turned[:, half, :], pairs[:].rearrange("v p e -> v (p e)").bitcast(F32), ident[:])
+            return turned
+
+        def low_slots_back(turned):
             for half in range(HALVES):
-                for u in range(2):
-                    turn_back(turned[half][:, u * P : u * P + P], g_last, half, u)
+                words = z1_rounded[half][:].rearrange("p v j -> p (v j)").bitcast(F32).rearrange("p (v u) -> p v u", u=2)
+                nc.scalar.copy(words[:, :, 0], turned[:, half, :])
+
+        def last_rows_and_second_product():
+            rows = (ROWS - 2, ROWS - 1)
+            sums = [ps_z.tile([P, PASS], F32, name=f"z_bank0{half}") for half in range(HALVES)]
+            for e, r in enumerate(rows):
+                for d in range(D - 1):
+                    if (e, d) == (0, 1):
+                        picked = shared.tile([P, V], F32, name="held_picked", offset=LAST_SLOT + SLOT)
+                    else:
+                        picked = picks.tile([P, V], F32, name=f"picked{d}")
+                    nc.vector.tensor_tensor(picked[:], h_tiles[r][:].indirect(pos_t[d][:]), gate_t[:, d, :], MULT)
+                    for half in range(HALVES):
+                        nc.tensor.matmul(
+                            sums[half][:, e * P : e * P + P],
+                            picked[:, half * P : half * P + P],
+                            ident[:],
+                            start=(d == 0),
+                            stop=(d == D - 2),
+                            is_transpose=True,
+                        )
+            thirds = shared.tile([P, 2, V], F32, name="thirds", offset=LAST_SLOT + SLOT)
+            for e, r in enumerate(rows):
+                nc.vector.tensor_tensor(thirds[:, e, :], h_tiles[r][:].indirect(pos_t[D - 1][:]), gate_t[:, D - 1, :], MULT)
+            partial = []
+            for half in range(HALVES):
+                staged = keep.tile([P, 2 * P], F32, name=f"staged{half}")
+                copy_on("scalar", staged[:], sums[half][:, 0 : 2 * P])
+                partial.append(product_bank(ROWS + half))
+                for e in range(2):
+                    nc.tensor.transpose(partial[half][:, e * P : e * P + P], staged[:, e * P : e * P + P], ident[:])
             w2_codes = shared.tile([P, GROUPS, N], U32, name="w2_codes", offset=LAST_SLOT, align_bytes=64)
             nc.vector.quantize_mx(
                 out=w2_codes[:].rearrange("p g n -> p (g n)").bitcast(FP8X4),
@@ -262,24 +338,25 @@ def tile_picked_sage_none_e_kernel(tc, xT, w1, w2, gate, offs, pos1, pos2, pos3,
                 scales=z0_scales[:],
                 in_=z0_rounded[:].rearrange("p h v j -> p (h v j)"),
             )
+            for half in range(HALVES):
+                nc.vector.tensor_tensor(
+                    z1_rounded[half][:, :, 2:4],
+                    partial[half][:, 0 : 2 * P].rearrange("p (e v) -> p v e", e=2),
+                    thirds[:, :, half * P : half * P + P].rearrange("p e v -> p v e"),
+                    ADD,
+                )
             result = keep.tile([N, V], F32, name="result")
+            copier = ("scalar", "vector")
             for half in range(HALVES):
                 cols = slice(half * P, half * P + P)
-                z1_rounded = keep.tile([P, P, 4], BF16, name=f"z1_bf16_{half}", align_bytes=64)
-                words = z1_rounded[:].rearrange("p v j -> p (v j)").bitcast(F32).rearrange("p (v u) -> p v u", u=2)
-                src = turned[half][:, 0 : 2 * P].rearrange("p (u v) -> p v u", u=2)
-                if copier[half] == "scalar":
-                    nc.scalar.copy(words, src)
-                else:
-                    nc.vector.tensor_copy(words, src)
                 z1_codes = keep.tile([P, P], U32, name=f"z1_codes{half}", align_bytes=64)
                 z1_scales = keep.tile([P, P], U8, name=f"z1_scales{half}", align_bytes=64)
                 nc.vector.quantize_mx(
                     out=z1_codes[:].bitcast(FP8X4),
                     scales=z1_scales[:],
-                    in_=z1_rounded[:].rearrange("p v j -> p (v j)"),
+                    in_=z1_rounded[half][:].rearrange("p v j -> p (v j)"),
                 )
-                acc = product_bank(r + half)
+                acc = product_bank(ROWS) if half else ps_z.tile([P, PASS], F32, name="z_bank01")
                 operands = ((z0_codes[:, cols], z0_scales[:, cols]), (z1_codes[:], z1_scales[:]))
                 for g, (codes, scales) in enumerate(operands):
                     nc.tensor.matmul_mx(
@@ -335,7 +412,7 @@ def tile_picked_sage_none_e_kernel(tc, xT, w1, w2, gate, offs, pos1, pos2, pos3,
         x_codes[1] = shared.tile([P, S], U32, name="x_codes1", offset=HALF_SLOT, align_bytes=64)
         for a, b, interleaver, copier in PASS1_PARTS:
             quantise_x(1, a, b, x1_interleaved[a][:])
-        part_banks = [product_bank(0), product_bank(2), ps_z.tile([P, PASS], F32, name="z_bank0")]
+        part_banks = [product_bank(0), product_bank(2), ps_z.tile([P, PASS], F32, name="z_bank10")]
         for s in range(PASSES):
             for bank, (a, b, interleaver, copier) in zip(part_banks, PASS1_PARTS):
                 project(bank, 0, s, a, b)
@@ -346,26 +423,36 @@ def tile_picked_sage_none_e_kernel(tc, xT, w1, w2, gate, offs, pos1, pos2, pos3,
             copy_on(copier, h_tiles[0][:, a:b], bank[:, a:b])
         project_row(1)
 
-        last_weights = ROWS - 1 - AHEAD
-        for r in range(ROWS - 1):
+        for r in range(PLAIN_ROWS):
             pick_neighbours(r, 0)
             pick_neighbours(r, 1)
-            if r <= last_weights:
-                round_w1(r + AHEAD)
-                quantise_w1(r + AHEAD, 0, PASSES)
-                project_row(r + AHEAD)
-            if r == last_weights - 1:
-                interleave("scalar", w2_rounded[:, 0], w2_raw[:, 0])
-            if r == last_weights:
-                round_z("scalar", 0, 0, z_banks[0, 0][:], 0, GROUP_ROWS)
+            round_w1(r + AHEAD)
+            if r + AHEAD >= PLAIN_ROWS:
+                round_high(r + AHEAD - PLAIN_ROWS, 1)
+            quantise_w1(r + AHEAD, 0, PASSES)
+            project_row(r + AHEAD)
             fetch_row(r + 1)
-            if r == last_weights:
-                round_z("scalar", 0, 1, z_banks[0, 1][:], 0, GROUP_ROWS)
-                turned0 = first_pass_turn()
-                interleave("scalar", w2_rounded[:, 1], w2_raw[:, 1])
-            if r == last_weights + 1:
-                first_pass_back(turned0)
             pick_neighbours(r, 2)
+        for g in range(GROUPS):
+            interleave("scalar", w2_rounded[:, g], w2_raw[g][:])
+        pick_neighbours(4, 0)
+        quantise_high(1)
+        pick_neighbours(4, 1)
+        for c in range(2):
+            round_high(c, 0)
+        quantise_high(0)
+        project_row(6)
+        fetch_row(5)
+        project_row(7)
         for half in range(HALVES):
-            round_z("scalar", 1, half, z_banks[1, half][:, 0 : (GROUP_ROWS - 1) * P], 0, GROUP_ROWS - 1)
-        last_row_and_second_product()
+            round_z("scalar", 0, half, z_banks[0, half][:], 0, GROUP_ROWS)
+        turned0 = first_pass_turn()
+        pick_neighbours(4, 2)
+        fetch_row(6)
+        fetch_row(7)
+        for d in range(D):
+            pick_neighbours(5, d)
+        turned1 = low_slots_turn()
+        first_pass_back(turned0)
+        low_slots_back(turned1)
+        last_rows_and_second_product()

@@ -5,6 +5,7 @@ import concourse.mybir as mybir
 F32 = mybir.dt.float32
 BF16 = mybir.dt.bfloat16
 U32 = mybir.dt.uint32
+I32 = mybir.dt.int32
 U16 = mybir.dt.uint16
 U8 = mybir.dt.uint8
 FP8X4 = mybir.dt.float8_e4m3fn_x4
@@ -42,7 +43,8 @@ NODE_BYTES = 4 * 2
 PLAIN_ROWS = GROUP_ROWS
 WIDE_SLOTS = PLAIN_ROWS * SLOT
 QUARTER_SLOT = SLOT // 4
-LAST_SLOT = WIDE_SLOTS + 4 * SLOT + QUARTER_SLOT
+WIDE_SLOT = SLOT + QUARTER_SLOT
+LAST_SLOT = WIDE_SLOTS + 4 * WIDE_SLOT
 BLOCK = 32
 RUN = 8
 WIDE = 2 * P
@@ -128,7 +130,7 @@ def tile_picked_sage_none_e_kernel(tc, xT, w1, w2, gate, offs, pos1, pos2, pos3,
         w1_wide = {}
         for c in range(2):
             for s in range(PASSES):
-                place = WIDE_SLOTS + (2 * c + s) * SLOT
+                place = WIDE_SLOTS + (2 * c + s) * WIDE_SLOT
                 w1_wide[c, s] = shared.tile([P, 4, WIDE], F32, name=f"w1_wide{c}{s}", offset=place, align_bytes=64)
                 nc.sync.dma_start(w1_wide[c, s][:], w1_view[s][:, :, PASS + c * WIDE : PASS + (c + 1) * WIDE])
         w2_raw = [keep.tile([P, 4, N], F32, name=f"w2_raw{g}") for g in range(GROUPS)]
@@ -169,7 +171,11 @@ def tile_picked_sage_none_e_kernel(tc, xT, w1, w2, gate, offs, pos1, pos2, pos3,
             )
 
         def round_w1(r):
-            w1_rounded[r] = keep.tile([P, PASSES, P, 4], BF16, name=f"w1_bf16_{r}", align_bytes=64)
+            if r == PLAIN_ROWS + 1:
+                place = WIDE_SLOTS + 2 * WIDE_SLOT - HALF_SLOT
+                w1_rounded[r] = shared.tile([P, PASSES, P, 4], BF16, name=f"w1_bf16_{r}", offset=place, align_bytes=64)
+            else:
+                w1_rounded[r] = keep.tile([P, PASSES, P, 4], BF16, name=f"w1_bf16_{r}", align_bytes=64)
             for s in range(PASSES):
                 if r < PLAIN_ROWS:
                     interleave("scalar", w1_rounded[r][:, s], w1_raw[r, s][:])
@@ -230,7 +236,7 @@ def tile_picked_sage_none_e_kernel(tc, xT, w1, w2, gate, offs, pos1, pos2, pos3,
             if r + 1 < PLAIN_ROWS:
                 h_tiles[r] = shared.tile([P, S], F32, name=f"h{r}", offset=(r + 1) * SLOT)
             elif r < ROWS - 2:
-                place = WIDE_SLOTS + HELD_BY_WIDE[r - 1] * SLOT + QUARTER_SLOT
+                place = WIDE_SLOTS + HELD_BY_WIDE[r - 1] * WIDE_SLOT + QUARTER_SLOT
                 h_tiles[r] = shared.tile([P, S], F32, name=f"h{r}", offset=place)
             else:
                 h_tiles[r] = shared.tile([P, S], F32, name=f"h{r}", offset=LAST_SLOT + (r - ROWS + 2) * HALF_SLOT)
@@ -239,7 +245,8 @@ def tile_picked_sage_none_e_kernel(tc, xT, w1, w2, gate, offs, pos1, pos2, pos3,
         zT = {(0, half): keep.tile([P, 2, P, 2], BF16, name=f"zT0{half}") for half in range(HALVES)}
         z1_rounded = [keep.tile([P, P, 4], BF16, name=f"z1_bf16_{half}", align_bytes=64) for half in range(HALVES)]
         w2_scales = keep.tile([P, GROUPS, N], U8, name="w2_scales", align_bytes=64)
-        w2_rounded = keep.tile([P, GROUPS, N, 4], BF16, name="w2_bf16", align_bytes=64)
+        w2_place = WIDE_SLOTS + HELD_BY_WIDE[4] * WIDE_SLOT + QUARTER_SLOT
+        w2_rounded = shared.tile([P, GROUPS, N, 4], BF16, name="w2_bf16", offset=w2_place, align_bytes=64)
         z0_rounded = keep.tile([P, HALVES, P, 4], BF16, name="z0_bf16", align_bytes=64)
         z_banks = {}
 
@@ -254,7 +261,7 @@ def tile_picked_sage_none_e_kernel(tc, xT, w1, w2, gate, offs, pos1, pos2, pos3,
             if d == D - 1 and r + AHEAD < PLAIN_ROWS:
                 picked = shared.tile([P, V], F32, name=f"third{r}", offset=(r + AHEAD) * SLOT + HALF_SLOT)
             elif d == D - 1 and r in HELD_BY_WIDE:
-                picked = shared.tile([P, V], F32, name=f"third{r}", offset=WIDE_SLOTS + HELD_BY_WIDE[r] * SLOT)
+                picked = shared.tile([P, V], F32, name=f"third{r}", offset=WIDE_SLOTS + HELD_BY_WIDE[r] * WIDE_SLOT)
             else:
                 picked = picks.tile([P, V], F32, name=f"picked{d}")
             nc.vector.tensor_tensor(picked[:], h_tiles[r][:].indirect(pos_t[d][:]), gate_t[:, d, :], MULT)
@@ -283,68 +290,82 @@ def tile_picked_sage_none_e_kernel(tc, xT, w1, w2, gate, offs, pos1, pos2, pos3,
             )
 
         def low_slots_turn():
-            turned = product_bank(ROWS)[:, 0 : HALVES * P].rearrange("p (h v) -> p h v", h=HALVES)
+            turned = []
             for half in range(HALVES):
                 pairs = keep.tile([P, P, 2], BF16, name=f"zT1{half}")
                 sums = z_banks[1, half][:, 0 : 2 * P].rearrange("v (b e a) -> v b a e", e=2, a=RUN)
                 copy_on("scalar", pairs[:].rearrange("v (b a) e -> v b a e", a=RUN), sums)
-                nc.tensor.transpose(turned[:, half, :], pairs[:].rearrange("v p e -> v (p e)").bitcast(F32), ident[:])
+                turned.append(product_bank(ROWS + half))
+                nc.tensor.transpose(turned[half][:, 0:P], pairs[:].rearrange("v p e -> v (p e)").bitcast(F32), ident[:])
             return turned
 
-        def low_slots_back(turned):
-            for half in range(HALVES):
-                words = z1_rounded[half][:].rearrange("p v j -> p (v j)").bitcast(F32).rearrange("p (v u) -> p v u", u=2)
-                nc.scalar.copy(words[:, :, 0], turned[:, half, :])
-
-        def last_rows_and_second_product():
+        def last_rows_and_second_product(turned):
             rows = (ROWS - 2, ROWS - 1)
-            sums = [ps_z.tile([P, PASS], F32, name=f"z_bank0{half}") for half in range(HALVES)]
+            last = D - 1
+            first_sums = [ps_z.tile([P, PASS], F32, name="z_bank00"), ps_back.tile([P, PASS], F32, name="turned")]
+            second_sums = ps_z.tile([P, PASS], F32, name="z_bank01")
+            z1_pairs = keep.tile([P, 2, P], F32, name="z1_pairs")
+
+            def add_turn(half, e, d, picked, stop):
+                dst = second_sums[:, e * P : e * P + P] if half else first_sums[e][:, 0:P]
+                nc.tensor.matmul(dst, picked, ident[:], start=(d == 0), stop=stop, is_transpose=True)
+
+            def third_turn(dst, r, half):
+                entries = entries_of(pos_t[last], half * P, half * P + P)
+                nc.vector.tensor_tensor(dst, h_tiles[r][:].indirect(entries), gate_t[:, last, half * P : half * P + P], MULT)
+
+            early = {}
             for e, r in enumerate(rows):
-                for d in range(D - 1):
+                for d in range(last):
                     if (e, d) == (0, 1):
-                        picked = shared.tile([P, V], F32, name="held_picked", offset=LAST_SLOT + SLOT)
+                        early[e, d] = shared.tile([P, V], F32, name="held_picked", offset=LAST_SLOT + SLOT + QUARTER_SLOT // 2)
                     else:
-                        picked = picks.tile([P, V], F32, name=f"picked{d}")
-                    nc.vector.tensor_tensor(picked[:], h_tiles[r][:].indirect(pos_t[d][:]), gate_t[:, d, :], MULT)
-                    for half in range(HALVES):
-                        nc.tensor.matmul(
-                            sums[half][:, e * P : e * P + P],
-                            picked[:, half * P : half * P + P],
-                            ident[:],
-                            start=(d == 0),
-                            stop=(d == D - 2),
-                            is_transpose=True,
-                        )
-            thirds = shared.tile([P, 2, V], F32, name="thirds", offset=LAST_SLOT + SLOT)
+                        early[e, d] = picks.tile([P, V], F32, name=f"picked{d}")
+                    nc.vector.tensor_tensor(early[e, d][:], h_tiles[r][:].indirect(pos_t[d][:]), gate_t[:, d, :], MULT)
+                    add_turn(1, e, d, early[e, d][:, P:V], d == last - 1)
+                    add_turn(0, e, d, early[e, d][:, 0:P], False)
+            first_thirds = shared.tile([P, 2, P], F32, name="first_thirds", offset=LAST_SLOT + SLOT)
             for e, r in enumerate(rows):
-                nc.vector.tensor_tensor(thirds[:, e, :], h_tiles[r][:].indirect(pos_t[D - 1][:]), gate_t[:, D - 1, :], MULT)
-            partial = []
-            for half in range(HALVES):
-                staged = keep.tile([P, 2 * P], F32, name=f"staged{half}")
-                copy_on("scalar", staged[:], sums[half][:, 0 : 2 * P])
-                partial.append(product_bank(ROWS + half))
-                for e in range(2):
-                    nc.tensor.transpose(partial[half][:, e * P : e * P + P], staged[:, e * P : e * P + P], ident[:])
+                third_turn(first_thirds[:, e, :], r, 0)
+                add_turn(0, e, last, first_thirds[:, e, :], True)
+            thirds = shared.tile([P, 2, P], F32, name="thirds", offset=LAST_SLOT + SLOT + QUARTER_SLOT)
+            for e, r in enumerate(rows):
+                third_turn(thirds[:, e, :], r, 1)
+            staged = shared.tile([P, 2 * P], F32, name="staged", offset=LAST_SLOT + SLOT + HALF_SLOT)
+            copy_on("scalar", staged[:], second_sums[:, 0 : 2 * P])
+            nc.scalar.copy(z1_pairs[:, 0, :], turned[1][:, 0:P])
+            partial = product_bank(ROWS + 2)
+            for e in range(2):
+                nc.tensor.transpose(partial[:, e * P : e * P + P], staged[:, e * P : e * P + P], ident[:])
+            high_pairs = keep.tile([P, P, 2], BF16, name="high_pairs")
+            for e in range(2):
+                copy_on("scalar", high_pairs[:, :, e], first_sums[e][:, 0:P])
+            nc.tensor.transpose(turned[0][:, P : 2 * P], high_pairs[:].rearrange("v p e -> v (p e)").bitcast(F32), ident[:])
+            words = [
+                z1_rounded[half][:].rearrange("p v j -> p (v j)").bitcast(dtype).rearrange("p (v u) -> p v u", u=2)
+                for half, dtype in enumerate((F32, I32))
+            ]
+            nc.scalar.copy(words[0], turned[0][:, 0 : 2 * P].rearrange("p (u v) -> p v u", u=2))
             w2_codes = shared.tile([P, GROUPS, N], U32, name="w2_codes", offset=LAST_SLOT, align_bytes=64)
             nc.vector.quantize_mx(
                 out=w2_codes[:].rearrange("p g n -> p (g n)").bitcast(FP8X4),
                 scales=w2_scales[:].rearrange("p g n -> p (g n)"),
                 in_=w2_rounded[:].rearrange("p g n j -> p (g n j)"),
             )
-            z0_codes = shared.tile([P, V], U32, name="z0_codes", offset=LAST_SLOT + HALF_SLOT, align_bytes=64)
+            nc.vector.tensor_tensor(
+                z1_pairs[:, 1, :].bitcast(BF16).rearrange("p (v e) -> p v e", e=2),
+                partial[:, 0 : 2 * P].rearrange("p (e v) -> p v e", e=2),
+                thirds[:].rearrange("p e v -> p v e"),
+                ADD,
+            )
+            z0_codes = shared.tile([P, V], U32, name="z0_codes", offset=LAST_SLOT + SLOT + HALF_SLOT, align_bytes=64)
             z0_scales = keep.tile([P, V], U8, name="z0_scales", align_bytes=64)
             nc.vector.quantize_mx(
                 out=z0_codes[:].bitcast(FP8X4),
                 scales=z0_scales[:],
                 in_=z0_rounded[:].rearrange("p h v j -> p (h v j)"),
             )
-            for half in range(HALVES):
-                nc.vector.tensor_tensor(
-                    z1_rounded[half][:, :, 2:4],
-                    partial[half][:, 0 : 2 * P].rearrange("p (e v) -> p v e", e=2),
-                    thirds[:, :, half * P : half * P + P].rearrange("p e v -> p v e"),
-                    ADD,
-                )
+            nc.vector.tensor_copy(words[1], z1_pairs[:].bitcast(I32).rearrange("p u v -> p v u"))
             result = keep.tile([N, V], F32, name="result")
             copier = ("scalar", "vector")
             for half in range(HALVES):
@@ -356,7 +377,7 @@ def tile_picked_sage_none_e_kernel(tc, xT, w1, w2, gate, offs, pos1, pos2, pos3,
                     scales=z1_scales[:],
                     in_=z1_rounded[half][:].rearrange("p v j -> p (v j)"),
                 )
-                acc = product_bank(ROWS) if half else ps_z.tile([P, PASS], F32, name="z_bank01")
+                acc = product_bank(ROWS + 2) if half else ps_back.tile([P, PASS], F32, name="turned")
                 operands = ((z0_codes[:, cols], z0_scales[:, cols]), (z1_codes[:], z1_scales[:]))
                 for g, (codes, scales) in enumerate(operands):
                     nc.tensor.matmul_mx(
@@ -416,11 +437,24 @@ def tile_picked_sage_none_e_kernel(tc, xT, w1, w2, gate, offs, pos1, pos2, pos3,
         for s in range(PASSES):
             for bank, (a, b, interleaver, copier) in zip(part_banks, PASS1_PARTS):
                 project(bank, 0, s, a, b)
-        round_w1(1)
-        quantise_w1(1, 0, PASSES)
+        w1_codes[1] = keep.tile([P, PASSES, P], U32, name="w1_codes1", align_bytes=64)
+        w1_scales[1] = keep.tile([P, PASSES, P], U8, name="w1_scales1", align_bytes=64)
+        second_rounded = [
+            keep.tile([P, P, 4], BF16, name="w1_bf16_10", align_bytes=64),
+            shared.tile([P, P, 4], BF16, name="w1_bf16_11", offset=0, align_bytes=64),
+        ]
+        for s, engine in enumerate(("scalar", "vector")):
+            interleave(engine, second_rounded[s][:], w1_raw[1, s][:])
         h_tiles[0] = keep.tile([P, S], F32, name="h0")
-        for bank, (a, b, interleaver, copier) in zip(part_banks, PASS1_PARTS):
-            copy_on(copier, h_tiles[0][:, a:b], bank[:, a:b])
+        for s in range(PASSES):
+            nc.vector.quantize_mx(
+                out=w1_codes[1][:, s].bitcast(FP8X4),
+                scales=w1_scales[1][:, s],
+                in_=second_rounded[s][:].rearrange("p c j -> p (c j)"),
+            )
+            if s == 0:
+                for bank, (a, b, interleaver, copier) in zip(part_banks, PASS1_PARTS):
+                    copy_on(copier, h_tiles[0][:, a:b], bank[:, a:b])
         project_row(1)
 
         for r in range(PLAIN_ROWS):
@@ -433,8 +467,6 @@ def tile_picked_sage_none_e_kernel(tc, xT, w1, w2, gate, offs, pos1, pos2, pos3,
             project_row(r + AHEAD)
             fetch_row(r + 1)
             pick_neighbours(r, 2)
-        for g in range(GROUPS):
-            interleave("scalar", w2_rounded[:, g], w2_raw[g][:])
         pick_neighbours(4, 0)
         quantise_high(1)
         pick_neighbours(4, 1)
@@ -454,5 +486,6 @@ def tile_picked_sage_none_e_kernel(tc, xT, w1, w2, gate, offs, pos1, pos2, pos3,
             pick_neighbours(5, d)
         turned1 = low_slots_turn()
         first_pass_back(turned0)
-        low_slots_back(turned1)
-        last_rows_and_second_product()
+        for g in range(GROUPS):
+            interleave("scalar", w2_rounded[:, g], w2_raw[g][:])
+        last_rows_and_second_product(turned1)

@@ -172,7 +172,7 @@ def tile_picked_sage_none_e_kernel(tc, xT, w1, w2, gate, offs, pos1, pos2, pos3,
 
         def round_w1(r):
             if r == PLAIN_ROWS + 1:
-                place = WIDE_SLOTS + 2 * WIDE_SLOT - HALF_SLOT
+                place = WIDE_SLOTS + WIDE_SLOT + HALF_SLOT + QUARTER_SLOT // 2
                 w1_rounded[r] = shared.tile([P, PASSES, P, 4], BF16, name=f"w1_bf16_{r}", offset=place, align_bytes=64)
             else:
                 w1_rounded[r] = keep.tile([P, PASSES, P, 4], BF16, name=f"w1_bf16_{r}", align_bytes=64)
@@ -186,7 +186,7 @@ def tile_picked_sage_none_e_kernel(tc, xT, w1, w2, gate, offs, pos1, pos2, pos3,
 
         def round_high(c, s):
             if c == 0 and s == 0:
-                high_rounded[s] = shared.tile([P, 2, P, 4], BF16, name="w1_high0", offset=LAST_SLOT - HALF_SLOT, align_bytes=64)
+                high_rounded[s] = shared.tile([P, 2, P, 4], BF16, name="w1_high0", offset=LAST_SLOT - HALF_SLOT - QUARTER_SLOT // 2, align_bytes=64)
             elif c == 0:
                 high_rounded[s] = keep.tile([P, 2, P, 4], BF16, name="w1_high1", align_bytes=64)
             for e in range(2):
@@ -212,7 +212,7 @@ def tile_picked_sage_none_e_kernel(tc, xT, w1, w2, gate, offs, pos1, pos2, pos3,
                 in_=w1_rounded[r][:, part].rearrange("p s c j -> p (s c j)"),
             )
 
-        def project(bank, r, s, a, b):
+        def project(bank, r, s, a, b, first=0):
             if r < ROWS - 2:
                 codes, scales = w1_codes[r][:, s, :], w1_scales[r][:, s, :]
             else:
@@ -223,8 +223,8 @@ def tile_picked_sage_none_e_kernel(tc, xT, w1, w2, gate, offs, pos1, pos2, pos3,
                 lhsT_scale=scales,
                 rhs=x_codes[s][:, a:b].bitcast(FP8X4),
                 rhs_scale=x_scales[s][:, a:b],
-                start=(s == 0),
-                stop=(s == PASSES - 1),
+                start=(s == first),
+                stop=(s != first),
             )
 
         def project_row(r):
@@ -236,16 +236,20 @@ def tile_picked_sage_none_e_kernel(tc, xT, w1, w2, gate, offs, pos1, pos2, pos3,
             if r + 1 < PLAIN_ROWS:
                 h_tiles[r] = shared.tile([P, S], F32, name=f"h{r}", offset=(r + 1) * SLOT)
             elif r < ROWS - 2:
-                place = WIDE_SLOTS + HELD_BY_WIDE[r - 1] * WIDE_SLOT + QUARTER_SLOT
+                place = WIDE_SLOTS + HELD_BY_WIDE[r - 1] * WIDE_SLOT + QUARTER_SLOT // 2
                 h_tiles[r] = shared.tile([P, S], F32, name=f"h{r}", offset=place)
             else:
                 h_tiles[r] = shared.tile([P, S], F32, name=f"h{r}", offset=LAST_SLOT + (r - ROWS + 2) * HALF_SLOT)
             nc.scalar.activation(h_tiles[r][:], h_banks[r][:], COPY)
 
-        zT = {(0, half): keep.tile([P, 2, P, 2], BF16, name=f"zT0{half}") for half in range(HALVES)}
+        zT_place = WIDE_SLOTS + HELD_BY_WIDE[4] * WIDE_SLOT + HALF_SLOT + QUARTER_SLOT // 2
+        zT = {
+            (0, half): shared.tile([P, 2, P, 2], BF16, name=f"zT0{half}", offset=zT_place + half * QUARTER_SLOT)
+            for half in range(HALVES)
+        }
         z1_rounded = [keep.tile([P, P, 4], BF16, name=f"z1_bf16_{half}", align_bytes=64) for half in range(HALVES)]
         w2_scales = keep.tile([P, GROUPS, N], U8, name="w2_scales", align_bytes=64)
-        w2_place = WIDE_SLOTS + HELD_BY_WIDE[4] * WIDE_SLOT + QUARTER_SLOT
+        w2_place = WIDE_SLOTS + HELD_BY_WIDE[3] * WIDE_SLOT + QUARTER_SLOT // 2
         w2_rounded = shared.tile([P, GROUPS, N, 4], BF16, name="w2_bf16", offset=w2_place, align_bytes=64)
         z0_rounded = keep.tile([P, HALVES, P, 4], BF16, name="z0_bf16", align_bytes=64)
         z_banks = {}
@@ -261,7 +265,7 @@ def tile_picked_sage_none_e_kernel(tc, xT, w1, w2, gate, offs, pos1, pos2, pos3,
             if d == D - 1 and r + AHEAD < PLAIN_ROWS:
                 picked = shared.tile([P, V], F32, name=f"third{r}", offset=(r + AHEAD) * SLOT + HALF_SLOT)
             elif d == D - 1 and r in HELD_BY_WIDE:
-                picked = shared.tile([P, V], F32, name=f"third{r}", offset=WIDE_SLOTS + HELD_BY_WIDE[r] * WIDE_SLOT)
+                picked = shared.tile([P, V], F32, name=f"third{r}", offset=WIDE_SLOTS + HELD_BY_WIDE[r] * WIDE_SLOT - QUARTER_SLOT // 2)
             else:
                 picked = picks.tile([P, V], F32, name=f"picked{d}")
             nc.vector.tensor_tensor(picked[:], h_tiles[r][:].indirect(pos_t[d][:]), gate_t[:, d, :], MULT)
@@ -469,23 +473,26 @@ def tile_picked_sage_none_e_kernel(tc, xT, w1, w2, gate, offs, pos1, pos2, pos3,
             pick_neighbours(r, 2)
         pick_neighbours(4, 0)
         quantise_high(1)
+        for r in (6, 7):
+            h_banks[r] = product_bank(r)
+            project(h_banks[r], r, 1, 0, S, first=1)
         pick_neighbours(4, 1)
         for c in range(2):
             round_high(c, 0)
         quantise_high(0)
-        project_row(6)
+        for r in (6, 7):
+            project(h_banks[r], r, 0, 0, S, first=1)
         fetch_row(5)
-        project_row(7)
         for half in range(HALVES):
             round_z("scalar", 0, half, z_banks[0, half][:], 0, GROUP_ROWS)
         turned0 = first_pass_turn()
         pick_neighbours(4, 2)
         fetch_row(6)
         fetch_row(7)
+        first_pass_back(turned0)
         for d in range(D):
             pick_neighbours(5, d)
         turned1 = low_slots_turn()
-        first_pass_back(turned0)
         for g in range(GROUPS):
             interleave("scalar", w2_rounded[:, g], w2_raw[g][:])
         last_rows_and_second_product(turned1)

@@ -145,8 +145,8 @@ def tile_picked_sage_none_e_kernel(tc, xT, w1, w2, gate, offs, pos1, pos2, pos3,
             else:
                 nc.scalar.activation(dst, src, COPY)
 
-        def interleave(engine, dst, src):
-            copy_on(engine, dst.rearrange("p (q c) j -> p q j c", c=4), src.rearrange("p j (q c) -> p q j c", c=4))
+        def interleave(engine, dst, src, run=4):
+            copy_on(engine, dst.rearrange("p (q c) j -> p q j c", c=run), src.rearrange("p j (q c) -> p q j c", c=run))
 
         picked_planes = [keep.tile([P, 4, S], BF16, name=f"picked_planes{s}") for s in range(PASSES)]
         x_codes, x_scales = {}, {}
@@ -167,7 +167,7 @@ def tile_picked_sage_none_e_kernel(tc, xT, w1, w2, gate, offs, pos1, pos2, pos3,
         def deal(dst, raw, first, width):
             runs = raw[:].rearrange("p j (b w) -> p b j w", w=BLOCK)[:, :, :, first : first + width]
             nc.scalar.copy(
-                dst.rearrange("p (b q c) j -> p b q j c", q=width // 4, c=4), runs.rearrange("p b j (q c) -> p b q j c", c=4)
+                dst.rearrange("p (b q c) j -> p b q j c", q=width // 2, c=2), runs.rearrange("p b j (q c) -> p b q j c", c=2)
             )
 
         def round_w1(r):
@@ -178,7 +178,7 @@ def tile_picked_sage_none_e_kernel(tc, xT, w1, w2, gate, offs, pos1, pos2, pos3,
                 w1_rounded[r] = keep.tile([P, PASSES, P, 4], BF16, name=f"w1_bf16_{r}", align_bytes=64)
             for s in range(PASSES):
                 if r < PLAIN_ROWS:
-                    interleave("scalar", w1_rounded[r][:, s], w1_raw[r, s][:])
+                    interleave("scalar", w1_rounded[r][:, s], w1_raw[r, s][:], 2)
                 else:
                     deal(w1_rounded[r][:, s], w1_wide[r - PLAIN_ROWS, s], 0, 2 * RUN)
 
@@ -448,7 +448,7 @@ def tile_picked_sage_none_e_kernel(tc, xT, w1, w2, gate, offs, pos1, pos2, pos3,
             shared.tile([P, P, 4], BF16, name="w1_bf16_11", offset=0, align_bytes=64),
         ]
         for s, engine in enumerate(("scalar", "vector")):
-            interleave(engine, second_rounded[s][:], w1_raw[1, s][:])
+            interleave(engine, second_rounded[s][:], w1_raw[1, s][:], 4 if s else 2)
         h_tiles[0] = keep.tile([P, S], F32, name="h0")
         for s in range(PASSES):
             nc.vector.quantize_mx(
@@ -494,5 +494,5 @@ def tile_picked_sage_none_e_kernel(tc, xT, w1, w2, gate, offs, pos1, pos2, pos3,
             pick_neighbours(5, d)
         turned1 = low_slots_turn()
         for g in range(GROUPS):
-            interleave("scalar", w2_rounded[:, g], w2_raw[g][:])
+            interleave("scalar", w2_rounded[:, g], w2_raw[g][:], 2)
         last_rows_and_second_product(turned1)

@@ -28,13 +28,14 @@ QUAD = 32
 PER_COLUMN = 16
 
 SCALAR_PLANE = (1, 1)
-PASS0_PARTS = ((0, 192, "scalar"), (192, 384, "vector"), (384, S, "scalar"))
+PASS0_PARTS = ((0, 192, "scalar"), (192, 384, "gpsimd"), (384, S, "scalar"))
 PASS1_PARTS = (
     (0, LIST_HALF, "vector", "scalar"),
     (LIST_HALF, LIST_HALF + LIST_QUARTER, "vector", "vector"),
     (LIST_HALF + LIST_QUARTER, S, "scalar", "scalar"),
 )
 HELD_BY_WIDE = {2: 1, 3: 3, 4: 2}
+THIRD_HELD = (2, 4)
 AHEAD = 2
 
 HALF_SLOT = 4 * P * 4
@@ -142,10 +143,15 @@ def tile_picked_sage_none_e_kernel(tc, xT, w1, w2, gate, offs, pos1, pos2, pos3,
         def copy_on(engine, dst, src):
             if engine == "vector":
                 nc.vector.tensor_copy(dst, src)
+            elif engine == "gpsimd":
+                nc.gpsimd.tensor_scalar(dst, src, 1.0, 0.0, MULT, ADD)
             else:
                 nc.scalar.activation(dst, src, COPY)
 
         def interleave(engine, dst, src, run=4):
+            if engine == "gpsimd":
+                copy_on(engine, dst, src.rearrange("p j c -> p c j"))
+                return
             copy_on(engine, dst.rearrange("p (q c) j -> p q j c", c=run), src.rearrange("p j (q c) -> p q j c", c=run))
 
         picked_planes = [keep.tile([P, 4, S], BF16, name=f"picked_planes{s}") for s in range(PASSES)]
@@ -264,7 +270,7 @@ def tile_picked_sage_none_e_kernel(tc, xT, w1, w2, gate, offs, pos1, pos2, pos3,
                     z_banks[g, half] = ps_z.tile([P, PASS], F32, name=f"z_bank{g}{half}")
             if d == D - 1 and r + AHEAD < PLAIN_ROWS:
                 picked = shared.tile([P, V], F32, name=f"third{r}", offset=(r + AHEAD) * SLOT + HALF_SLOT)
-            elif d == D - 1 and r in HELD_BY_WIDE:
+            elif d == D - 1 and r in THIRD_HELD:
                 picked = shared.tile([P, V], F32, name=f"third{r}", offset=WIDE_SLOTS + HELD_BY_WIDE[r] * WIDE_SLOT - QUARTER_SLOT // 2)
             else:
                 picked = picks.tile([P, V], F32, name=f"picked{d}")
@@ -467,10 +473,17 @@ def tile_picked_sage_none_e_kernel(tc, xT, w1, w2, gate, offs, pos1, pos2, pos3,
             round_w1(r + AHEAD)
             if r + AHEAD >= PLAIN_ROWS:
                 round_high(r + AHEAD - PLAIN_ROWS, 1)
-            quantise_w1(r + AHEAD, 0, PASSES)
-            project_row(r + AHEAD)
-            fetch_row(r + 1)
-            pick_neighbours(r, 2)
+            if r + 1 < PLAIN_ROWS:
+                quantise_w1(r + AHEAD, 0, PASSES)
+                project_row(r + AHEAD)
+                fetch_row(r + 1)
+                pick_neighbours(r, 2)
+            else:
+                quantise_w1(r + AHEAD, 0, 1)
+                pick_neighbours(r, 2)
+                quantise_w1(r + AHEAD, 1, 1)
+                project_row(r + AHEAD)
+                fetch_row(r + 1)
         pick_neighbours(4, 0)
         quantise_high(1)
         for r in (6, 7):

@@ -34,8 +34,6 @@ PASS1_PARTS = (
     (LIST_HALF, LIST_HALF + LIST_QUARTER, "vector", "vector"),
     (LIST_HALF + LIST_QUARTER, S, "scalar", "scalar"),
 )
-HELD_BY_WIDE = {2: 1, 3: 3, 4: 2}
-THIRD_HELD = (2, 4)
 AHEAD = 2
 
 HALF_SLOT = 4 * P * 4
@@ -44,8 +42,8 @@ NODE_BYTES = 4 * 2
 PLAIN_ROWS = GROUP_ROWS
 WIDE_SLOTS = PLAIN_ROWS * SLOT
 QUARTER_SLOT = SLOT // 4
-WIDE_SLOT = SLOT + QUARTER_SLOT
-LAST_SLOT = WIDE_SLOTS + 4 * WIDE_SLOT
+CUT_SLOTS = WIDE_SLOTS + 2 * SLOT
+LAST_SLOT = CUT_SLOTS + 4 * SLOT
 BLOCK = 32
 RUN = 8
 WIDE = 2 * P
@@ -128,17 +126,20 @@ def tile_picked_sage_none_e_kernel(tc, xT, w1, w2, gate, offs, pos1, pos2, pos3,
         load_w1(2)
         nc.sync.dma_start(pos_t[2][:], pos3)
         load_w1(3)
-        w1_wide = {}
+        w1_wide, w1_cut = {}, {}
         for c in range(2):
-            for s in range(PASSES):
-                place = WIDE_SLOTS + (2 * c + s) * WIDE_SLOT
-                w1_wide[c, s] = shared.tile([P, 4, WIDE], F32, name=f"w1_wide{c}{s}", offset=place, align_bytes=64)
-                nc.sync.dma_start(w1_wide[c, s][:], w1_view[s][:, :, PASS + c * WIDE : PASS + (c + 1) * WIDE])
+            first = PASS + c * WIDE
+            w1_wide[c] = shared.tile([P, 4, WIDE], F32, name=f"w1_wide{c}", offset=WIDE_SLOTS + c * SLOT, align_bytes=64)
+            nc.sync.dma_start(w1_wide[c][:], w1_view[0][:, :, first : first + WIDE])
+            for n in range(2):
+                place = CUT_SLOTS + (2 * c + n) * SLOT
+                w1_cut[c, n] = shared.tile([P, 4, P], F32, name=f"w1_cut{c}{n}", offset=place, align_bytes=64)
+                nc.sync.dma_start(w1_cut[c, n][:], w1_view[1][:, :, first + n * P : first + (n + 1) * P])
         w2_raw = [keep.tile([P, 4, N], F32, name=f"w2_raw{g}") for g in range(GROUPS)]
         nc.sync.dma_start(w2_raw[0][:], w2[0:PASS].rearrange("(p j) n -> p j n", j=4))
-        w2_dealt = w2[PASS:H].rearrange("(b j a) n -> j b a n", j=4, a=RUN)
-        for j in range(4):
-            nc.sync.dma_start(w2_raw[1][:, j, :], w2_dealt[j])
+        w2_dealt = w2[PASS:H].rearrange("(b u a e) n -> u b a (e n)", u=2, a=RUN, e=2)
+        for u in range(2):
+            nc.sync.dma_start(w2_raw[1][:, 2 * u : 2 * u + 2, :].rearrange("p e n -> p (e n)"), w2_dealt[u])
 
         def copy_on(engine, dst, src):
             if engine == "vector":
@@ -177,26 +178,30 @@ def tile_picked_sage_none_e_kernel(tc, xT, w1, w2, gate, offs, pos1, pos2, pos3,
             )
 
         def round_w1(r):
-            if r == PLAIN_ROWS + 1:
-                place = WIDE_SLOTS + WIDE_SLOT + HALF_SLOT + QUARTER_SLOT // 2
-                w1_rounded[r] = shared.tile([P, PASSES, P, 4], BF16, name=f"w1_bf16_{r}", offset=place, align_bytes=64)
-            else:
-                w1_rounded[r] = keep.tile([P, PASSES, P, 4], BF16, name=f"w1_bf16_{r}", align_bytes=64)
+            w1_rounded[r] = keep.tile([P, PASSES, P, 4], BF16, name=f"w1_bf16_{r}", align_bytes=64)
             for s in range(PASSES):
-                if r < PLAIN_ROWS:
-                    interleave("scalar", w1_rounded[r][:, s], w1_raw[r, s][:], 2)
-                else:
-                    deal(w1_rounded[r][:, s], w1_wide[r - PLAIN_ROWS, s], 0, 2 * RUN)
+                interleave("scalar", w1_rounded[r][:, s], w1_raw[r, s][:], 2)
 
-        high_rounded = {}
+        high_rounded = [
+            shared.tile([P, 2, P, 4], BF16, name="w1_high0", offset=CUT_SLOTS + 2 * SLOT - QUARTER_SLOT, align_bytes=64),
+            keep.tile([P, 2, P, 4], BF16, name="w1_high1", align_bytes=64),
+        ]
 
-        def round_high(c, s):
-            if c == 0 and s == 0:
-                high_rounded[s] = shared.tile([P, 2, P, 4], BF16, name="w1_high0", offset=LAST_SLOT - HALF_SLOT - QUARTER_SLOT // 2, align_bytes=64)
-            elif c == 0:
-                high_rounded[s] = keep.tile([P, 2, P, 4], BF16, name="w1_high1", align_bytes=64)
-            for e in range(2):
-                deal(high_rounded[s][:, e, c * P // 2 : (c + 1) * P // 2], w1_wide[c, s], (2 + e) * RUN, RUN)
+        def round_high(s, raw, first, columns):
+            dst = high_rounded[s][:, :, first : first + columns, :].rearrange("p e (b a) j -> p b a j e", a=RUN)
+            src = raw[:].rearrange("p j (b u a e) -> p b u a j e", u=2, a=RUN, e=2)[:, :, 1]
+            nc.scalar.copy(dst, src)
+
+        def round_cut_high(c, n):
+            round_high(1, w1_cut[c, n], (2 * c + n) * BLOCK, BLOCK)
+
+        def round_low(c):
+            r = PLAIN_ROWS + c
+            w1_rounded[r] = keep.tile([P, PASSES, P, 4], BF16, name=f"w1_bf16_{r}", align_bytes=64)
+            deal(w1_rounded[r][:, 0], w1_wide[c], 0, 2 * RUN)
+            deal(w1_rounded[r][:, 1, 0 : P // 2], w1_cut[c, 0], 0, 2 * RUN)
+            round_cut_high(c, 0)
+            deal(w1_rounded[r][:, 1, P // 2 : P], w1_cut[c, 1], 0, 2 * RUN)
 
         def quantise_high(s):
             high_codes[s] = keep.tile([P, 2, P], U32, name=f"high_codes{s}", align_bytes=64)
@@ -241,24 +246,27 @@ def tile_picked_sage_none_e_kernel(tc, xT, w1, w2, gate, offs, pos1, pos2, pos3,
         def fetch_row(r):
             if r + 1 < PLAIN_ROWS:
                 h_tiles[r] = shared.tile([P, S], F32, name=f"h{r}", offset=(r + 1) * SLOT)
+            elif r <= PLAIN_ROWS:
+                h_tiles[r] = shared.tile([P, S], F32, name=f"h{r}", offset=CUT_SLOTS + 2 * (r + 1 - PLAIN_ROWS) * SLOT + QUARTER_SLOT)
             elif r < ROWS - 2:
-                place = WIDE_SLOTS + HELD_BY_WIDE[r - 1] * WIDE_SLOT + QUARTER_SLOT // 2
-                h_tiles[r] = shared.tile([P, S], F32, name=f"h{r}", offset=place)
+                h_tiles[r] = keep.tile([P, S], F32, name=f"h{r}")
             else:
                 h_tiles[r] = shared.tile([P, S], F32, name=f"h{r}", offset=LAST_SLOT + (r - ROWS + 2) * HALF_SLOT)
             nc.scalar.activation(h_tiles[r][:], h_banks[r][:], COPY)
 
-        zT_place = WIDE_SLOTS + HELD_BY_WIDE[4] * WIDE_SLOT + HALF_SLOT + QUARTER_SLOT // 2
+        zT_place = WIDE_SLOTS
         zT = {
             (0, half): shared.tile([P, 2, P, 2], BF16, name=f"zT0{half}", offset=zT_place + half * QUARTER_SLOT)
             for half in range(HALVES)
         }
         z1_rounded = [keep.tile([P, P, 4], BF16, name=f"z1_bf16_{half}", align_bytes=64) for half in range(HALVES)]
         w2_scales = keep.tile([P, GROUPS, N], U8, name="w2_scales", align_bytes=64)
-        w2_place = WIDE_SLOTS + HELD_BY_WIDE[3] * WIDE_SLOT + QUARTER_SLOT // 2
+        w2_place = CUT_SLOTS + 2 * SLOT + QUARTER_SLOT
         w2_rounded = shared.tile([P, GROUPS, N, 4], BF16, name="w2_bf16", offset=w2_place, align_bytes=64)
         z0_rounded = keep.tile([P, HALVES, P, 4], BF16, name="z0_bf16", align_bytes=64)
         z_banks = {}
+
+        held_picks = {(2, 2): CUT_SLOTS + SLOT, (4, 1): CUT_SLOTS + 3 * SLOT, (4, 2): WIDE_SLOTS + SLOT + HALF_SLOT}
 
         def add_turned(dst, picked, d):
             nc.tensor.matmul(dst, picked, ident[:], start=(d == 0), stop=(d == D - 1), is_transpose=True)
@@ -270,8 +278,8 @@ def tile_picked_sage_none_e_kernel(tc, xT, w1, w2, gate, offs, pos1, pos2, pos3,
                     z_banks[g, half] = ps_z.tile([P, PASS], F32, name=f"z_bank{g}{half}")
             if d == D - 1 and r + AHEAD < PLAIN_ROWS:
                 picked = shared.tile([P, V], F32, name=f"third{r}", offset=(r + AHEAD) * SLOT + HALF_SLOT)
-            elif d == D - 1 and r in THIRD_HELD:
-                picked = shared.tile([P, V], F32, name=f"third{r}", offset=WIDE_SLOTS + HELD_BY_WIDE[r] * WIDE_SLOT - QUARTER_SLOT // 2)
+            elif (r, d) in held_picks:
+                picked = shared.tile([P, V], F32, name=f"held{r}{d}", offset=held_picks[r, d])
             else:
                 picked = picks.tile([P, V], F32, name=f"picked{d}")
             nc.vector.tensor_tensor(picked[:], h_tiles[r][:].indirect(pos_t[d][:]), gate_t[:, d, :], MULT)
@@ -303,8 +311,7 @@ def tile_picked_sage_none_e_kernel(tc, xT, w1, w2, gate, offs, pos1, pos2, pos3,
             turned = []
             for half in range(HALVES):
                 pairs = keep.tile([P, P, 2], BF16, name=f"zT1{half}")
-                sums = z_banks[1, half][:, 0 : 2 * P].rearrange("v (b e a) -> v b a e", e=2, a=RUN)
-                copy_on("scalar", pairs[:].rearrange("v (b a) e -> v b a e", a=RUN), sums)
+                copy_on("scalar", pairs[:].rearrange("v p e -> v (p e)"), z_banks[1, half][:, 0 : 2 * P])
                 turned.append(product_bank(ROWS + half))
                 nc.tensor.transpose(turned[half][:, 0:P], pairs[:].rearrange("v p e -> v (p e)").bitcast(F32), ident[:])
             return turned
@@ -467,23 +474,30 @@ def tile_picked_sage_none_e_kernel(tc, xT, w1, w2, gate, offs, pos1, pos2, pos3,
                     copy_on(copier, h_tiles[0][:, a:b], bank[:, a:b])
         project_row(1)
 
-        for r in range(PLAIN_ROWS):
+        for r in range(PLAIN_ROWS - AHEAD):
             pick_neighbours(r, 0)
             pick_neighbours(r, 1)
             round_w1(r + AHEAD)
-            if r + AHEAD >= PLAIN_ROWS:
-                round_high(r + AHEAD - PLAIN_ROWS, 1)
-            if r + 1 < PLAIN_ROWS:
-                quantise_w1(r + AHEAD, 0, PASSES)
-                project_row(r + AHEAD)
-                fetch_row(r + 1)
-                pick_neighbours(r, 2)
-            else:
-                quantise_w1(r + AHEAD, 0, 1)
-                pick_neighbours(r, 2)
-                quantise_w1(r + AHEAD, 1, 1)
-                project_row(r + AHEAD)
-                fetch_row(r + 1)
+            quantise_w1(r + AHEAD, 0, PASSES)
+            project_row(r + AHEAD)
+            fetch_row(r + 1)
+            pick_neighbours(r, 2)
+        pick_neighbours(2, 0)
+        pick_neighbours(2, 1)
+        round_low(0)
+        round_cut_high(0, 1)
+        quantise_w1(4, 0, PASSES)
+        project_row(4)
+        fetch_row(3)
+        pick_neighbours(2, 2)
+        for d in range(D):
+            pick_neighbours(3, d)
+        round_low(1)
+        quantise_w1(5, 0, 1)
+        quantise_w1(5, 1, 1)
+        project_row(5)
+        fetch_row(4)
+        round_cut_high(1, 1)
         pick_neighbours(4, 0)
         quantise_high(1)
         for r in (6, 7):
@@ -491,7 +505,7 @@ def tile_picked_sage_none_e_kernel(tc, xT, w1, w2, gate, offs, pos1, pos2, pos3,
             project(h_banks[r], r, 1, 0, S, first=1)
         pick_neighbours(4, 1)
         for c in range(2):
-            round_high(c, 0)
+            round_high(0, w1_wide[c], c * P // 2, P // 2)
         quantise_high(0)
         for r in (6, 7):
             project(h_banks[r], r, 0, 0, S, first=1)

@@ -44,6 +44,7 @@ WIDE_SLOTS = PLAIN_ROWS * SLOT
 QUARTER_SLOT = SLOT // 4
 CUT_SLOTS = WIDE_SLOTS + 2 * SLOT
 LAST_SLOT = CUT_SLOTS + 4 * SLOT
+W2_SLOT = LAST_SLOT + 2 * SLOT
 BLOCK = 32
 RUN = 8
 WIDE = 2 * P
@@ -135,7 +136,7 @@ def tile_picked_sage_none_e_kernel(tc, xT, w1, w2, gate, offs, pos1, pos2, pos3,
                 place = CUT_SLOTS + (2 * c + n) * SLOT
                 w1_cut[c, n] = shared.tile([P, 4, P], F32, name=f"w1_cut{c}{n}", offset=place, align_bytes=64)
                 nc.sync.dma_start(w1_cut[c, n][:], w1_view[1][:, :, first + n * P : first + (n + 1) * P])
-        w2_raw = [keep.tile([P, 4, N], F32, name=f"w2_raw{g}") for g in range(GROUPS)]
+        w2_raw = [shared.tile([P, 4, N], F32, name=f"w2_raw{g}", offset=W2_SLOT + g * HALF_SLOT) for g in range(GROUPS)]
         nc.sync.dma_start(w2_raw[0][:], w2[0:PASS].rearrange("(p j) n -> p j n", j=4))
         w2_dealt = w2[PASS:H].rearrange("(b u a e) n -> u b a (e n)", u=2, a=RUN, e=2)
         for u in range(2):
@@ -320,43 +321,31 @@ def tile_picked_sage_none_e_kernel(tc, xT, w1, w2, gate, offs, pos1, pos2, pos3,
             rows = (ROWS - 2, ROWS - 1)
             last = D - 1
             first_sums = [ps_z.tile([P, PASS], F32, name="z_bank00"), ps_back.tile([P, PASS], F32, name="turned")]
-            second_sums = ps_z.tile([P, PASS], F32, name="z_bank01")
             z1_pairs = keep.tile([P, 2, P], F32, name="z1_pairs")
 
-            def add_turn(half, e, d, picked, stop):
-                dst = second_sums[:, e * P : e * P + P] if half else first_sums[e][:, 0:P]
-                nc.tensor.matmul(dst, picked, ident[:], start=(d == 0), stop=stop, is_transpose=True)
+            def pick(dst, r, d, a, b):
+                nc.vector.tensor_tensor(dst, h_tiles[r][:].indirect(entries_of(pos_t[d], a, b)), gate_t[:, d, a:b], MULT)
 
-            def third_turn(dst, r, half):
-                entries = entries_of(pos_t[last], half * P, half * P + P)
-                nc.vector.tensor_tensor(dst, h_tiles[r][:].indirect(entries), gate_t[:, last, half * P : half * P + P], MULT)
-
-            early = {}
+            firsts = keep.tile([P, 2, V], F32, name="firsts")
             for e, r in enumerate(rows):
-                for d in range(last):
-                    if (e, d) == (0, 1):
-                        early[e, d] = shared.tile([P, V], F32, name="held_picked", offset=LAST_SLOT + SLOT + QUARTER_SLOT // 2)
-                    else:
-                        early[e, d] = picks.tile([P, V], F32, name=f"picked{d}")
-                    nc.vector.tensor_tensor(early[e, d][:], h_tiles[r][:].indirect(pos_t[d][:]), gate_t[:, d, :], MULT)
-                    add_turn(1, e, d, early[e, d][:, P:V], d == last - 1)
-                    add_turn(0, e, d, early[e, d][:, 0:P], False)
-            first_thirds = shared.tile([P, 2, P], F32, name="first_thirds", offset=LAST_SLOT + SLOT)
+                pick(firsts[:, e, :], r, 0, 0, V)
+                add_turned(first_sums[e][:, 0:P], firsts[:, e, 0:P], 0)
+                for d in range(1, D):
+                    picked = keep.tile([P, P], F32, name=f"first_half{e}{d}")
+                    pick(picked[:], r, d, 0, P)
+                    add_turned(first_sums[e][:, 0:P], picked[:], d)
+            seconds = keep.tile([P, 2, P], F32, name="seconds")
             for e, r in enumerate(rows):
-                third_turn(first_thirds[:, e, :], r, 0)
-                add_turn(0, e, last, first_thirds[:, e, :], True)
-            thirds = shared.tile([P, 2, P], F32, name="thirds", offset=LAST_SLOT + SLOT + QUARTER_SLOT)
-            for e, r in enumerate(rows):
-                third_turn(thirds[:, e, :], r, 1)
-            staged = shared.tile([P, 2 * P], F32, name="staged", offset=LAST_SLOT + SLOT + HALF_SLOT)
-            copy_on("scalar", staged[:], second_sums[:, 0 : 2 * P])
-            nc.scalar.copy(z1_pairs[:, 0, :], turned[1][:, 0:P])
-            partial = product_bank(ROWS + 2)
-            for e in range(2):
-                nc.tensor.transpose(partial[:, e * P : e * P + P], staged[:, e * P : e * P + P], ident[:])
+                pick(seconds[:, e, :], r, 1, P, V)
+            thirds = keep.tile([P, 2, P], F32, name="thirds")
+            pick(thirds[:, 0, :], rows[0], last, P, V)
+            staged = shared.tile([P, 2, P], F32, name="staged", offset=W2_SLOT + HALF_SLOT)
+            nc.vector.tensor_tensor(staged[:], firsts[:, :, P:V], seconds[:], ADD)
+            pick(thirds[:, 1, :], rows[1], last, P, V)
             high_pairs = keep.tile([P, P, 2], BF16, name="high_pairs")
             for e in range(2):
                 copy_on("scalar", high_pairs[:, :, e], first_sums[e][:, 0:P])
+            nc.scalar.copy(z1_pairs[:, 0, :], turned[1][:, 0:P])
             nc.tensor.transpose(turned[0][:, P : 2 * P], high_pairs[:].rearrange("v p e -> v (p e)").bitcast(F32), ident[:])
             words = [
                 z1_rounded[half][:].rearrange("p v j -> p (v j)").bitcast(dtype).rearrange("p (v u) -> p v u", u=2)
@@ -371,11 +360,11 @@ def tile_picked_sage_none_e_kernel(tc, xT, w1, w2, gate, offs, pos1, pos2, pos3,
             )
             nc.vector.tensor_tensor(
                 z1_pairs[:, 1, :].bitcast(BF16).rearrange("p (v e) -> p v e", e=2),
-                partial[:, 0 : 2 * P].rearrange("p (e v) -> p v e", e=2),
+                staged[:].rearrange("p e v -> p v e"),
                 thirds[:].rearrange("p e v -> p v e"),
                 ADD,
             )
-            z0_codes = shared.tile([P, V], U32, name="z0_codes", offset=LAST_SLOT + SLOT + HALF_SLOT, align_bytes=64)
+            z0_codes = shared.tile([P, V], U32, name="z0_codes", offset=W2_SLOT + HALF_SLOT + QUARTER_SLOT, align_bytes=64)
             z0_scales = keep.tile([P, V], U8, name="z0_scales", align_bytes=64)
             nc.vector.quantize_mx(
                 out=z0_codes[:].bitcast(FP8X4),

@@ -40,14 +40,13 @@ HALF_SLOT = 4 * P * 4
 SLOT = 2 * HALF_SLOT
 NODE_BYTES = 4 * 2
 PLAIN_ROWS = GROUP_ROWS
-WIDE_SLOTS = PLAIN_ROWS * SLOT
 QUARTER_SLOT = SLOT // 4
-CUT_SLOTS = WIDE_SLOTS + 2 * SLOT
-LAST_SLOT = CUT_SLOTS + 4 * SLOT
-W2_SLOT = LAST_SLOT + 2 * SLOT
 BLOCK = 32
 RUN = 8
-WIDE = 2 * P
+TURNED = 3 * RUN
+LOAD_BLOCKS = (6, 5, 5)
+LOAD_SLOTS = PLAIN_ROWS * SLOT
+LAST_SLOT = LOAD_SLOTS + 2 * len(LOAD_BLOCKS) * SLOT
 
 FLOPS = 2 * K * H * S + 2 * H * N * V
 
@@ -127,20 +126,26 @@ def tile_picked_sage_none_e_kernel(tc, xT, w1, w2, gate, offs, pos1, pos2, pos3,
         load_w1(2)
         nc.sync.dma_start(pos_t[2][:], pos3)
         load_w1(3)
-        w1_wide, w1_cut = {}, {}
-        for c in range(2):
-            first = PASS + c * WIDE
-            w1_wide[c] = shared.tile([P, 4, WIDE], F32, name=f"w1_wide{c}", offset=WIDE_SLOTS + c * SLOT, align_bytes=64)
-            nc.sync.dma_start(w1_wide[c][:], w1_view[0][:, :, first : first + WIDE])
-            for n in range(2):
-                place = CUT_SLOTS + (2 * c + n) * SLOT
-                w1_cut[c, n] = shared.tile([P, 4, P], F32, name=f"w1_cut{c}{n}", offset=place, align_bytes=64)
-                nc.sync.dma_start(w1_cut[c, n][:], w1_view[1][:, :, first + n * P : first + (n + 1) * P])
-        w2_raw = [shared.tile([P, 4, N], F32, name=f"w2_raw{g}", offset=W2_SLOT + g * HALF_SLOT) for g in range(GROUPS)]
+        w1_load = {}
+        first_block = [sum(LOAD_BLOCKS[:c]) for c in range(len(LOAD_BLOCKS))]
+
+        def load_place(c, s):
+            return LOAD_SLOTS + (2 * c + s) * SLOT + QUARTER_SLOT
+
+        for c, blocks in enumerate(LOAD_BLOCKS):
+            first = PASS + first_block[c] * BLOCK
+            for s in range(PASSES):
+                shape = [P, 4, blocks * BLOCK]
+                w1_load[c, s] = shared.tile(shape, F32, name=f"w1_load{c}{s}", offset=load_place(c, s), align_bytes=64)
+                nc.sync.dma_start(w1_load[c, s][:], w1_view[s][:, :, first : first + blocks * BLOCK])
+        w2_raw = [keep.tile([P, 4, N], F32, name=f"w2_raw{g}") for g in range(GROUPS)]
         nc.sync.dma_start(w2_raw[0][:], w2[0:PASS].rearrange("(p j) n -> p j n", j=4))
-        w2_dealt = w2[PASS:H].rearrange("(b u a e) n -> u b a (e n)", u=2, a=RUN, e=2)
-        for u in range(2):
-            nc.sync.dma_start(w2_raw[1][:, 2 * u : 2 * u + 2, :].rearrange("p e n -> p (e n)"), w2_dealt[u])
+        w2_blocks = w2[PASS:H].rearrange("(b r) n -> b r n", r=BLOCK)
+        nc.sync.dma_start(
+            w2_raw[1][:, 0:3, :].rearrange("p j n -> p (j n)"),
+            w2_blocks[:, 0:TURNED, :].rearrange("b (a j) n -> b a (j n)", j=3),
+        )
+        nc.sync.dma_start(w2_raw[1][:, 3, :], w2_blocks[:, TURNED:BLOCK, :])
 
         def copy_on(engine, dst, src):
             if engine == "vector":
@@ -170,48 +175,38 @@ def tile_picked_sage_none_e_kernel(tc, xT, w1, w2, gate, offs, pos1, pos2, pos3,
             return tile[:, a // PER_COLUMN : b // PER_COLUMN]
 
         w1_rounded, w1_codes, w1_scales, h_banks, h_tiles = {}, {}, {}, {}, {}
-        high_codes, high_scales = {}, {}
-
-        def deal(dst, raw, first, width):
-            runs = raw[:].rearrange("p j (b w) -> p b j w", w=BLOCK)[:, :, :, first : first + width]
-            nc.scalar.copy(
-                dst.rearrange("p (b q c) j -> p b q j c", q=width // 2, c=2), runs.rearrange("p b j (q c) -> p b q j c", c=2)
-            )
 
         def round_w1(r):
             w1_rounded[r] = keep.tile([P, PASSES, P, 4], BF16, name=f"w1_bf16_{r}", align_bytes=64)
             for s in range(PASSES):
                 interleave("scalar", w1_rounded[r][:, s], w1_raw[r, s][:], 2)
 
-        high_rounded = [
-            shared.tile([P, 2, P, 4], BF16, name="w1_high0", offset=CUT_SLOTS + 2 * SLOT - QUARTER_SLOT, align_bytes=64),
-            keep.tile([P, 2, P, 4], BF16, name="w1_high1", align_bytes=64),
-        ]
+        dealt_rounded = [keep.tile([P, PASS, 4], BF16, name=f"dealt_bf16_{s}", align_bytes=64) for s in range(PASSES)]
+        dealt_codes = [keep.tile([P, PASS], U32, name=f"dealt_codes{s}", align_bytes=64) for s in range(PASSES)]
+        dealt_scales = [keep.tile([P, PASS], U8, name=f"dealt_scales{s}", align_bytes=64) for s in range(PASSES)]
 
-        def round_high(s, raw, first, columns):
-            dst = high_rounded[s][:, :, first : first + columns, :].rearrange("p e (b a) j -> p b a j e", a=RUN)
-            src = raw[:].rearrange("p j (b u a e) -> p b u a j e", u=2, a=RUN, e=2)[:, :, 1]
-            nc.scalar.copy(dst, src)
-
-        def round_cut_high(c, n):
-            round_high(1, w1_cut[c, n], (2 * c + n) * BLOCK, BLOCK)
-
-        def round_low(c):
-            r = PLAIN_ROWS + c
-            w1_rounded[r] = keep.tile([P, PASSES, P, 4], BF16, name=f"w1_bf16_{r}", align_bytes=64)
-            deal(w1_rounded[r][:, 0], w1_wide[c], 0, 2 * RUN)
-            deal(w1_rounded[r][:, 1, 0 : P // 2], w1_cut[c, 0], 0, 2 * RUN)
-            round_cut_high(c, 0)
-            deal(w1_rounded[r][:, 1, P // 2 : P], w1_cut[c, 1], 0, 2 * RUN)
-
-        def quantise_high(s):
-            high_codes[s] = keep.tile([P, 2, P], U32, name=f"high_codes{s}", align_bytes=64)
-            high_scales[s] = keep.tile([P, 2, P], U8, name=f"high_scales{s}", align_bytes=64)
-            nc.vector.quantize_mx(
-                out=high_codes[s][:].rearrange("p e c -> p (e c)").bitcast(FP8X4),
-                scales=high_scales[s][:].rearrange("p e c -> p (e c)"),
-                in_=high_rounded[s][:].rearrange("p e c j -> p (e c j)"),
+        def deal(c, s, first, width, place):
+            blocks = LOAD_BLOCKS[c]
+            begin = place + first_block[c] * width
+            dst = dealt_rounded[s][:, begin : begin + blocks * width, :]
+            runs = w1_load[c, s][:].rearrange("p j (b w) -> p b j w", w=BLOCK)[:, :, :, first : first + width]
+            nc.scalar.copy(
+                dst.rearrange("p (b q c) j -> p b q j c", q=width // 2, c=2), runs.rearrange("p b j (q c) -> p b q j c", c=2)
             )
+
+        def deal_load(c):
+            for s in range(PASSES):
+                deal(c, s, 0, TURNED, 0)
+                deal(c, s, TURNED, RUN, 3 * P)
+
+        def quantise_dealt(r):
+            cols = slice((r - PLAIN_ROWS) * P, (r - PLAIN_ROWS + 1) * P)
+            for s in range(PASSES):
+                nc.vector.quantize_mx(
+                    out=dealt_codes[s][:, cols].bitcast(FP8X4),
+                    scales=dealt_scales[s][:, cols],
+                    in_=dealt_rounded[s][:, cols, :].rearrange("p c j -> p (c j)"),
+                )
 
         def quantise_w1(r, first, passes):
             if first == 0:
@@ -225,10 +220,11 @@ def tile_picked_sage_none_e_kernel(tc, xT, w1, w2, gate, offs, pos1, pos2, pos3,
             )
 
         def project(bank, r, s, a, b, first=0):
-            if r < ROWS - 2:
+            if r < PLAIN_ROWS:
                 codes, scales = w1_codes[r][:, s, :], w1_scales[r][:, s, :]
             else:
-                codes, scales = high_codes[s][:, r - ROWS + 2, :], high_scales[s][:, r - ROWS + 2, :]
+                cols = slice((r - PLAIN_ROWS) * P, (r - PLAIN_ROWS + 1) * P)
+                codes, scales = dealt_codes[s][:, cols], dealt_scales[s][:, cols]
             nc.tensor.matmul_mx(
                 out=bank[:, a:b],
                 lhsT=codes.bitcast(FP8X4),
@@ -247,27 +243,24 @@ def tile_picked_sage_none_e_kernel(tc, xT, w1, w2, gate, offs, pos1, pos2, pos3,
         def fetch_row(r):
             if r + 1 < PLAIN_ROWS:
                 h_tiles[r] = shared.tile([P, S], F32, name=f"h{r}", offset=(r + 1) * SLOT)
-            elif r <= PLAIN_ROWS:
-                h_tiles[r] = shared.tile([P, S], F32, name=f"h{r}", offset=CUT_SLOTS + 2 * (r + 1 - PLAIN_ROWS) * SLOT + QUARTER_SLOT)
             elif r < ROWS - 2:
-                h_tiles[r] = keep.tile([P, S], F32, name=f"h{r}")
+                h_tiles[r] = shared.tile([P, S], F32, name=f"h{r}", offset=load_place(r + 1 - PLAIN_ROWS, 0))
             else:
                 h_tiles[r] = shared.tile([P, S], F32, name=f"h{r}", offset=LAST_SLOT + (r - ROWS + 2) * HALF_SLOT)
             nc.scalar.activation(h_tiles[r][:], h_banks[r][:], COPY)
 
-        zT_place = WIDE_SLOTS
+        zT_places = (load_place(2, 1) - QUARTER_SLOT // 2, load_place(2, 1) + 3 * QUARTER_SLOT // 2)
         zT = {
-            (0, half): shared.tile([P, 2, P, 2], BF16, name=f"zT0{half}", offset=zT_place + half * QUARTER_SLOT)
-            for half in range(HALVES)
+            (0, half): shared.tile([P, 2, P, 2], BF16, name=f"zT0{half}", offset=zT_places[half]) for half in range(HALVES)
         }
         z1_rounded = [keep.tile([P, P, 4], BF16, name=f"z1_bf16_{half}", align_bytes=64) for half in range(HALVES)]
         w2_scales = keep.tile([P, GROUPS, N], U8, name="w2_scales", align_bytes=64)
-        w2_place = CUT_SLOTS + 2 * SLOT + QUARTER_SLOT
+        w2_place = load_place(2, 0)
         w2_rounded = shared.tile([P, GROUPS, N, 4], BF16, name="w2_bf16", offset=w2_place, align_bytes=64)
         z0_rounded = keep.tile([P, HALVES, P, 4], BF16, name="z0_bf16", align_bytes=64)
         z_banks = {}
 
-        held_picks = {(2, 2): CUT_SLOTS + SLOT, (4, 1): CUT_SLOTS + 3 * SLOT, (4, 2): WIDE_SLOTS + SLOT + HALF_SLOT}
+        held_picks = {(2, 2): load_place(0, 1), (3, 2): load_place(1, 1), (4, 2): load_place(2, 1) + QUARTER_SLOT // 2}
 
         def add_turned(dst, picked, d):
             nc.tensor.matmul(dst, picked, ident[:], start=(d == 0), stop=(d == D - 1), is_transpose=True)
@@ -308,73 +301,68 @@ def tile_picked_sage_none_e_kernel(tc, xT, w1, w2, gate, offs, pos1, pos2, pos3,
                 words.rearrange("p (h v u) -> p h v u", h=HALVES, u=2), turned[:].rearrange("p h u v -> p h v u")
             )
 
-        def low_slots_turn():
-            turned = []
-            for half in range(HALVES):
-                pairs = keep.tile([P, P, 2], BF16, name=f"zT1{half}")
-                copy_on("scalar", pairs[:].rearrange("v p e -> v (p e)"), z_banks[1, half][:, 0 : 2 * P])
-                turned.append(product_bank(ROWS + half))
-                nc.tensor.transpose(turned[half][:, 0:P], pairs[:].rearrange("v p e -> v (p e)").bitcast(F32), ident[:])
-            return turned
+        def last_rows_and_second_product():
+            turned_row, direct_row = ROWS - 2, ROWS - 1
 
-        def last_rows_and_second_product(turned):
-            rows = (ROWS - 2, ROWS - 1)
-            last = D - 1
-            first_sums = [ps_z.tile([P, PASS], F32, name="z_bank00"), ps_back.tile([P, PASS], F32, name="turned")]
-            z1_pairs = keep.tile([P, 2, P], F32, name="z1_pairs")
-
-            def pick(dst, r, d, a, b):
+            def pick(dst, r, d, half):
+                a, b = half * P, half * P + P
                 nc.vector.tensor_tensor(dst, h_tiles[r][:].indirect(entries_of(pos_t[d], a, b)), gate_t[:, d, a:b], MULT)
 
-            firsts = keep.tile([P, 2, V], F32, name="firsts")
-            for e, r in enumerate(rows):
-                pick(firsts[:, e, :], r, 0, 0, V)
-                add_turned(first_sums[e][:, 0:P], firsts[:, e, 0:P], 0)
+            pick_neighbours(turned_row, 0)
+            for half in (1, 0):
                 for d in range(1, D):
-                    picked = keep.tile([P, P], F32, name=f"first_half{e}{d}")
-                    pick(picked[:], r, d, 0, P)
-                    add_turned(first_sums[e][:, 0:P], picked[:], d)
-            seconds = keep.tile([P, 2, P], F32, name="seconds")
-            for e, r in enumerate(rows):
-                pick(seconds[:, e, :], r, 1, P, V)
-            thirds = keep.tile([P, 2, P], F32, name="thirds")
-            pick(thirds[:, 0, :], rows[0], last, P, V)
-            staged = shared.tile([P, 2, P], F32, name="staged", offset=W2_SLOT + HALF_SLOT)
-            nc.vector.tensor_tensor(staged[:], firsts[:, :, P:V], seconds[:], ADD)
-            pick(thirds[:, 1, :], rows[1], last, P, V)
-            high_pairs = keep.tile([P, P, 2], BF16, name="high_pairs")
-            for e in range(2):
-                copy_on("scalar", high_pairs[:, :, e], first_sums[e][:, 0:P])
-            nc.scalar.copy(z1_pairs[:, 0, :], turned[1][:, 0:P])
-            nc.tensor.transpose(turned[0][:, P : 2 * P], high_pairs[:].rearrange("v p e -> v (p e)").bitcast(F32), ident[:])
-            words = [
-                z1_rounded[half][:].rearrange("p v j -> p (v j)").bitcast(dtype).rearrange("p (v u) -> p v u", u=2)
-                for half, dtype in enumerate((F32, I32))
-            ]
-            nc.scalar.copy(words[0], turned[0][:, 0 : 2 * P].rearrange("p (u v) -> p v u", u=2))
-            w2_codes = shared.tile([P, GROUPS, N], U32, name="w2_codes", offset=LAST_SLOT, align_bytes=64)
+                    picked = keep.tile([P, P], F32, name=f"turned_half{half}{d}")
+                    pick(picked[:], turned_row, d, half)
+                    add_turned(z_banks[1, half][:, 2 * P : 3 * P], picked[:], d)
+            direct_sums = product_bank(ROWS)
+            for d in range(D):
+                picked = keep.tile([P, P], F32, name=f"direct_half{d}")
+                pick(picked[:], direct_row, d, 0)
+                add_turned(direct_sums[:, 0:P], picked[:], d)
+            directs = keep.tile([P, D, P], F32, name="directs")
+            for d in range(D):
+                pick(directs[:, d, :], direct_row, d, 1)
+            partial = keep.tile([P, P], F32, name="partial")
+            nc.vector.tensor_tensor(partial[:], directs[:, 0, :], directs[:, 1, :], ADD)
+
+            zT[1, 0] = shared.tile([P, 2, P, 2], BF16, name="zT10", offset=LAST_SLOT + SLOT)
+            zT[1, 1] = keep.tile([P, 2, P, 2], BF16, name="zT11")
+            back = [ps_z.tile([P, PASS], F32, name=f"z_bank0{half}") for half in range(HALVES)]
+
+            def words_back(half):
+                words = z1_rounded[half][:].rearrange("p v j -> p (v j)").bitcast(F32).rearrange("p (v u) -> p v u", u=2)
+                nc.scalar.copy(words, back[half][:, 0 : 2 * P].rearrange("p (u v) -> p v u", u=2))
+
+            for half in (1, 0):
+                sums = z_banks[1, half][:, 0 : 3 * P].rearrange("v (p j) -> v p j", j=3)
+                copy_on("scalar", zT[1, half][:, 0], sums[:, :, 0:2])
+                turn_back(back[half][:, 0:P], 1, half, 0)
+                if half:
+                    copy_on("scalar", zT[1, half][:, 1], sums[:, :, 2:3].to_broadcast([P, P, 2]))
+                    turn_back(back[half][:, P : 2 * P], 1, half, 1)
+                else:
+                    copy_on("scalar", zT[1, half][:, 1, :, 0], sums[:, :, 2])
+            words_back(1)
+            copy_on("scalar", zT[1, 0][:, 1, :, 1], direct_sums[:, 0:P])
+            turn_back(back[0][:, P : 2 * P], 1, 0, 1)
+            words_back(0)
+            w2_codes = shared.tile([P, GROUPS, N], U32, name="w2_codes", offset=LAST_SLOT + HALF_SLOT, align_bytes=64)
             nc.vector.quantize_mx(
                 out=w2_codes[:].rearrange("p g n -> p (g n)").bitcast(FP8X4),
                 scales=w2_scales[:].rearrange("p g n -> p (g n)"),
                 in_=w2_rounded[:].rearrange("p g n j -> p (g n j)"),
             )
-            nc.vector.tensor_tensor(
-                z1_pairs[:, 1, :].bitcast(BF16).rearrange("p (v e) -> p v e", e=2),
-                staged[:].rearrange("p e v -> p v e"),
-                thirds[:].rearrange("p e v -> p v e"),
-                ADD,
-            )
-            z0_codes = shared.tile([P, V], U32, name="z0_codes", offset=W2_SLOT + HALF_SLOT + QUARTER_SLOT, align_bytes=64)
+            nc.vector.tensor_tensor(z1_rounded[1][:, :, 3], partial[:], directs[:, D - 1, :], ADD)
+            z0_codes = shared.tile([P, V], U32, name="z0_codes", offset=LAST_SLOT + SLOT, align_bytes=64)
             z0_scales = keep.tile([P, V], U8, name="z0_scales", align_bytes=64)
             nc.vector.quantize_mx(
                 out=z0_codes[:].bitcast(FP8X4),
                 scales=z0_scales[:],
                 in_=z0_rounded[:].rearrange("p h v j -> p (h v j)"),
             )
-            nc.vector.tensor_copy(words[1], z1_pairs[:].bitcast(I32).rearrange("p u v -> p v u"))
             result = keep.tile([N, V], F32, name="result")
-            copier = ("scalar", "vector")
-            for half in range(HALVES):
+            copier = ("vector", "scalar")
+            for half in (1, 0):
                 cols = slice(half * P, half * P + P)
                 z1_codes = keep.tile([P, P], U32, name=f"z1_codes{half}", align_bytes=64)
                 z1_scales = keep.tile([P, P], U8, name=f"z1_scales{half}", align_bytes=64)
@@ -383,7 +371,7 @@ def tile_picked_sage_none_e_kernel(tc, xT, w1, w2, gate, offs, pos1, pos2, pos3,
                     scales=z1_scales[:],
                     in_=z1_rounded[half][:].rearrange("p v j -> p (v j)"),
                 )
-                acc = product_bank(ROWS + 2) if half else ps_back.tile([P, PASS], F32, name="turned")
+                acc = product_bank(ROWS + 1 + half)
                 operands = ((z0_codes[:, cols], z0_scales[:, cols]), (z1_codes[:], z1_scales[:]))
                 for g, (codes, scales) in enumerate(operands):
                     nc.tensor.matmul_mx(
@@ -471,44 +459,25 @@ def tile_picked_sage_none_e_kernel(tc, xT, w1, w2, gate, offs, pos1, pos2, pos3,
             project_row(r + AHEAD)
             fetch_row(r + 1)
             pick_neighbours(r, 2)
-        pick_neighbours(2, 0)
-        pick_neighbours(2, 1)
-        round_low(0)
-        round_cut_high(0, 1)
-        quantise_w1(4, 0, PASSES)
-        project_row(4)
-        fetch_row(3)
-        pick_neighbours(2, 2)
-        for d in range(D):
-            pick_neighbours(3, d)
-        round_low(1)
-        quantise_w1(5, 0, 1)
-        quantise_w1(5, 1, 1)
-        project_row(5)
-        fetch_row(4)
-        round_cut_high(1, 1)
-        pick_neighbours(4, 0)
-        quantise_high(1)
-        for r in (6, 7):
-            h_banks[r] = product_bank(r)
-            project(h_banks[r], r, 1, 0, S, first=1)
-        pick_neighbours(4, 1)
-        for c in range(2):
-            round_high(0, w1_wide[c], c * P // 2, P // 2)
-        quantise_high(0)
-        for r in (6, 7):
-            project(h_banks[r], r, 0, 0, S, first=1)
-        fetch_row(5)
+        for c in range(len(LOAD_BLOCKS)):
+            r = PLAIN_ROWS - AHEAD + c
+            pick_neighbours(r, 0)
+            pick_neighbours(r, 1)
+            deal_load(c)
+            quantise_dealt(r + AHEAD)
+            project_row(r + AHEAD)
+            fetch_row(r + 1)
+            pick_neighbours(r, 2)
         for half in range(HALVES):
             round_z("scalar", 0, half, z_banks[0, half][:], 0, GROUP_ROWS)
         turned0 = first_pass_turn()
-        pick_neighbours(4, 2)
-        fetch_row(6)
-        fetch_row(7)
+        quantise_dealt(ROWS - 1)
+        project_row(ROWS - 1)
+        fetch_row(ROWS - 2)
+        fetch_row(ROWS - 1)
         first_pass_back(turned0)
         for d in range(D):
-            pick_neighbours(5, d)
-        turned1 = low_slots_turn()
+            pick_neighbours(ROWS - 3, d)
         for g in range(GROUPS):
             interleave("scalar", w2_rounded[:, g], w2_raw[g][:], 2)
-        last_rows_and_second_product(turned1)
+        last_rows_and_second_product()

@@ -199,8 +199,8 @@ def tile_picked_sage_none_e_kernel(tc, xT, w1, w2, gate, offs, pos1, pos2, pos3,
                 deal(c, s, 0, TURNED, 0)
                 deal(c, s, TURNED, RUN, 3 * P)
 
-        def quantise_dealt(r):
-            cols = slice((r - PLAIN_ROWS) * P, (r - PLAIN_ROWS + 1) * P)
+        def quantise_dealt(r, rows):
+            cols = slice((r - PLAIN_ROWS) * P, (r - PLAIN_ROWS + rows) * P)
             for s in range(PASSES):
                 nc.vector.quantize_mx(
                     out=dealt_codes[s][:, cols].bitcast(FP8X4),
@@ -314,18 +314,7 @@ def tile_picked_sage_none_e_kernel(tc, xT, w1, w2, gate, offs, pos1, pos2, pos3,
                     picked = keep.tile([P, P], F32, name=f"turned_half{half}{d}")
                     pick(picked[:], turned_row, d, half)
                     add_turned(z_banks[1, half][:, 2 * P : 3 * P], picked[:], d)
-            direct_sums = product_bank(ROWS)
-            for d in range(D):
-                picked = keep.tile([P, P], F32, name=f"direct_half{d}")
-                pick(picked[:], direct_row, d, 0)
-                add_turned(direct_sums[:, 0:P], picked[:], d)
-            directs = keep.tile([P, D, P], F32, name="directs")
-            for d in range(D):
-                pick(directs[:, d, :], direct_row, d, 1)
-            partial = keep.tile([P, P], F32, name="partial")
-            nc.vector.tensor_tensor(partial[:], directs[:, 0, :], directs[:, 1, :], ADD)
-
-            zT[1, 0] = shared.tile([P, 2, P, 2], BF16, name="zT10", offset=LAST_SLOT + SLOT)
+            zT[1, 0] = shared.tile([P, 2, P, 2], BF16, name="zT10", offset=LAST_SLOT + SLOT + QUARTER_SLOT // 2)
             zT[1, 1] = keep.tile([P, 2, P, 2], BF16, name="zT11")
             back = [ps_z.tile([P, PASS], F32, name=f"z_bank0{half}") for half in range(HALVES)]
 
@@ -336,23 +325,33 @@ def tile_picked_sage_none_e_kernel(tc, xT, w1, w2, gate, offs, pos1, pos2, pos3,
             for half in (1, 0):
                 sums = z_banks[1, half][:, 0 : 3 * P].rearrange("v (p j) -> v p j", j=3)
                 copy_on("scalar", zT[1, half][:, 0], sums[:, :, 0:2])
-                turn_back(back[half][:, 0:P], 1, half, 0)
                 if half:
+                    turn_back(back[half][:, 0:P], 1, half, 0)
                     copy_on("scalar", zT[1, half][:, 1], sums[:, :, 2:3].to_broadcast([P, P, 2]))
                     turn_back(back[half][:, P : 2 * P], 1, half, 1)
                 else:
                     copy_on("scalar", zT[1, half][:, 1, :, 0], sums[:, :, 2])
+            direct_sums = z_banks[1, 1][:, 3 * P : 4 * P]
+            first_directs = shared.tile([P, D, P], F32, name="first_directs", offset=LAST_SLOT + SLOT + HALF_SLOT)
+            for d in range(D):
+                pick(first_directs[:, d, :], direct_row, d, 0)
+                add_turned(direct_sums, first_directs[:, d, :], d)
+            directs = keep.tile([P, D, P], F32, name="directs")
+            for d in range(D):
+                pick(directs[:, d, :], direct_row, d, 1)
+            turn_back(back[0][:, 0:P], 1, 0, 0)
             words_back(1)
-            copy_on("scalar", zT[1, 0][:, 1, :, 1], direct_sums[:, 0:P])
+            copy_on("scalar", zT[1, 0][:, 1, :, 1], direct_sums)
             turn_back(back[0][:, P : 2 * P], 1, 0, 1)
             words_back(0)
-            w2_codes = shared.tile([P, GROUPS, N], U32, name="w2_codes", offset=LAST_SLOT + HALF_SLOT, align_bytes=64)
+            w2_codes = shared.tile([P, GROUPS, N], U32, name="w2_codes", offset=LAST_SLOT + SLOT + HALF_SLOT, align_bytes=64)
             nc.vector.quantize_mx(
                 out=w2_codes[:].rearrange("p g n -> p (g n)").bitcast(FP8X4),
                 scales=w2_scales[:].rearrange("p g n -> p (g n)"),
                 in_=w2_rounded[:].rearrange("p g n j -> p (g n j)"),
             )
-            nc.vector.tensor_tensor(z1_rounded[1][:, :, 3], partial[:], directs[:, D - 1, :], ADD)
+            with nc.allow_low_precision("the sum is made in float32 and rounded once"):
+                nc.vector.tensor_reduce(z1_rounded[1][:, :, 3], directs[:].rearrange("p d v -> p v d"), mybir.AxisListType.X, ADD)
             z0_codes = shared.tile([P, V], U32, name="z0_codes", offset=LAST_SLOT + SLOT, align_bytes=64)
             z0_scales = keep.tile([P, V], U8, name="z0_scales", align_bytes=64)
             nc.vector.quantize_mx(
@@ -364,7 +363,11 @@ def tile_picked_sage_none_e_kernel(tc, xT, w1, w2, gate, offs, pos1, pos2, pos3,
             copier = ("vector", "scalar")
             for half in (1, 0):
                 cols = slice(half * P, half * P + P)
-                z1_codes = keep.tile([P, P], U32, name=f"z1_codes{half}", align_bytes=64)
+                if half:
+                    place = LAST_SLOT + SLOT + QUARTER_SLOT
+                    z1_codes = shared.tile([P, P], U32, name="z1_codes1", offset=place, align_bytes=64)
+                else:
+                    z1_codes = keep.tile([P, P], U32, name="z1_codes0", align_bytes=64)
                 z1_scales = keep.tile([P, P], U8, name=f"z1_scales{half}", align_bytes=64)
                 nc.vector.quantize_mx(
                     out=z1_codes[:].bitcast(FP8X4),
@@ -464,14 +467,13 @@ def tile_picked_sage_none_e_kernel(tc, xT, w1, w2, gate, offs, pos1, pos2, pos3,
             pick_neighbours(r, 0)
             pick_neighbours(r, 1)
             deal_load(c)
-            quantise_dealt(r + AHEAD)
+            quantise_dealt(r + AHEAD, 2 if r + AHEAD == ROWS - 2 else 1)
             project_row(r + AHEAD)
             fetch_row(r + 1)
             pick_neighbours(r, 2)
         for half in range(HALVES):
             round_z("scalar", 0, half, z_banks[0, half][:], 0, GROUP_ROWS)
         turned0 = first_pass_turn()
-        quantise_dealt(ROWS - 1)
         project_row(ROWS - 1)
         fetch_row(ROWS - 2)
         fetch_row(ROWS - 1)

@@ -309,12 +309,13 @@ def tile_picked_sage_none_e_kernel(tc, xT, w1, w2, gate, offs, pos1, pos2, pos3,
                 nc.vector.tensor_tensor(dst, h_tiles[r][:].indirect(entries_of(pos_t[d], a, b)), gate_t[:, d, a:b], MULT)
 
             pick_neighbours(turned_row, 0)
-            for half in (1, 0):
+            for half in range(HALVES):
                 for d in range(1, D):
                     picked = keep.tile([P, P], F32, name=f"turned_half{half}{d}")
                     pick(picked[:], turned_row, d, half)
                     add_turned(z_banks[1, half][:, 2 * P : 3 * P], picked[:], d)
-            zT[1, 0] = shared.tile([P, 2, P, 2], BF16, name="zT10", offset=LAST_SLOT + SLOT + QUARTER_SLOT // 2)
+            held = LAST_SLOT + SLOT + HALF_SLOT
+            zT[1, 0] = keep.tile([P, 2, P, 2], BF16, name="zT10")
             zT[1, 1] = keep.tile([P, 2, P, 2], BF16, name="zT11")
             back = [ps_z.tile([P, PASS], F32, name=f"z_bank0{half}") for half in range(HALVES)]
 
@@ -322,59 +323,60 @@ def tile_picked_sage_none_e_kernel(tc, xT, w1, w2, gate, offs, pos1, pos2, pos3,
                 words = z1_rounded[half][:].rearrange("p v j -> p (v j)").bitcast(F32).rearrange("p (v u) -> p v u", u=2)
                 nc.scalar.copy(words, back[half][:, 0 : 2 * P].rearrange("p (u v) -> p v u", u=2))
 
-            for half in (1, 0):
+            direct_sums = product_bank(ROWS)
+            for d in range(D):
+                picked = shared.tile([P, P], F32, name=f"first_direct{d}", offset=held + d * QUARTER_SLOT // 2)
+                pick(picked[:], direct_row, d, 0)
+                add_turned(direct_sums[:, 0:P], picked[:], d)
+            directs = keep.tile([P, D, P], F32, name="directs")
+            for d in range(D):
+                pick(directs[:, d, :], direct_row, d, 1)
+            for half in range(HALVES):
                 sums = z_banks[1, half][:, 0 : 3 * P].rearrange("v (p j) -> v p j", j=3)
                 copy_on("scalar", zT[1, half][:, 0], sums[:, :, 0:2])
+                turn_back(back[half][:, 0:P], 1, half, 0)
                 if half:
-                    turn_back(back[half][:, 0:P], 1, half, 0)
                     copy_on("scalar", zT[1, half][:, 1], sums[:, :, 2:3].to_broadcast([P, P, 2]))
                     turn_back(back[half][:, P : 2 * P], 1, half, 1)
                 else:
                     copy_on("scalar", zT[1, half][:, 1, :, 0], sums[:, :, 2])
-            direct_sums = z_banks[1, 1][:, 3 * P : 4 * P]
-            first_directs = shared.tile([P, D, P], F32, name="first_directs", offset=LAST_SLOT + SLOT + HALF_SLOT)
-            for d in range(D):
-                pick(first_directs[:, d, :], direct_row, d, 0)
-                add_turned(direct_sums, first_directs[:, d, :], d)
-            directs = keep.tile([P, D, P], F32, name="directs")
-            for d in range(D):
-                pick(directs[:, d, :], direct_row, d, 1)
-            turn_back(back[0][:, 0:P], 1, 0, 0)
-            words_back(1)
-            copy_on("scalar", zT[1, 0][:, 1, :, 1], direct_sums)
+            copy_on("scalar", zT[1, 0][:, 1, :, 1], direct_sums[:, 0:P])
             turn_back(back[0][:, P : 2 * P], 1, 0, 1)
+            words_back(1)
             words_back(0)
-            w2_codes = shared.tile([P, GROUPS, N], U32, name="w2_codes", offset=LAST_SLOT + SLOT + HALF_SLOT, align_bytes=64)
-            nc.vector.quantize_mx(
-                out=w2_codes[:].rearrange("p g n -> p (g n)").bitcast(FP8X4),
-                scales=w2_scales[:].rearrange("p g n -> p (g n)"),
-                in_=w2_rounded[:].rearrange("p g n j -> p (g n j)"),
-            )
-            with nc.allow_low_precision("the sum is made in float32 and rounded once"):
-                nc.vector.tensor_reduce(z1_rounded[1][:, :, 3], directs[:].rearrange("p d v -> p v d"), mybir.AxisListType.X, ADD)
-            z0_codes = shared.tile([P, V], U32, name="z0_codes", offset=LAST_SLOT + SLOT, align_bytes=64)
+            w2_codes = shared.tile([P, GROUPS, N], U32, name="w2_codes", offset=held + QUARTER_SLOT // 2, align_bytes=64)
+
+            def quantise_w2(g):
+                nc.vector.quantize_mx(
+                    out=w2_codes[:, g].bitcast(FP8X4),
+                    scales=w2_scales[:, g, :],
+                    in_=w2_rounded[:, g].rearrange("p n j -> p (n j)"),
+                )
+
+            partial = keep.tile([P, P], F32, name="partial")
+            nc.vector.tensor_tensor(partial[:], directs[:, 0, :], directs[:, 1, :], ADD)
+            z0_codes = shared.tile([P, V], U32, name="z0_codes", offset=held - QUARTER_SLOT // 2, align_bytes=64)
             z0_scales = keep.tile([P, V], U8, name="z0_scales", align_bytes=64)
             nc.vector.quantize_mx(
                 out=z0_codes[:].bitcast(FP8X4),
                 scales=z0_scales[:],
                 in_=z0_rounded[:].rearrange("p h v j -> p (h v j)"),
             )
+            quantise_w2(0)
+            nc.vector.tensor_tensor(z1_rounded[1][:, :, 3], partial[:], directs[:, D - 1, :], ADD)
+            quantise_w2(1)
             result = keep.tile([N, V], F32, name="result")
             copier = ("vector", "scalar")
             for half in (1, 0):
                 cols = slice(half * P, half * P + P)
-                if half:
-                    place = LAST_SLOT + SLOT + QUARTER_SLOT
-                    z1_codes = shared.tile([P, P], U32, name="z1_codes1", offset=place, align_bytes=64)
-                else:
-                    z1_codes = keep.tile([P, P], U32, name="z1_codes0", align_bytes=64)
+                z1_codes = keep.tile([P, P], U32, name=f"z1_codes{half}", align_bytes=64)
                 z1_scales = keep.tile([P, P], U8, name=f"z1_scales{half}", align_bytes=64)
                 nc.vector.quantize_mx(
                     out=z1_codes[:].bitcast(FP8X4),
                     scales=z1_scales[:],
                     in_=z1_rounded[half][:].rearrange("p v j -> p (v j)"),
                 )
-                acc = product_bank(ROWS + 1 + half)
+                acc = ps_z.tile([P, PASS], F32, name="z_bank00") if half else product_bank(ROWS)
                 operands = ((z0_codes[:, cols], z0_scales[:, cols]), (z1_codes[:], z1_scales[:]))
                 for g, (codes, scales) in enumerate(operands):
                     nc.tensor.matmul_mx(

from contextlib import ExitStack

import concourse.mybir as mybir

F32 = mybir.dt.float32
BF16 = mybir.dt.bfloat16
U32 = mybir.dt.uint32
I32 = mybir.dt.int32
U16 = mybir.dt.uint16
U8 = mybir.dt.uint8
FP8X4 = mybir.dt.float8_e4m3fn_x4
COPY = mybir.ActivationFunctionType.Copy
MULT = mybir.AluOpType.mult
ADD = mybir.AluOpType.add
IS_EQUAL = mybir.AluOpType.is_equal

P = 128
K, T, D, S, V, H, N = 1024, 1024, 3, 512, 256, 1024, 128
PASS = 512
PASSES = K // PASS
GROUPS = H // PASS
ROWS = H // P
GROUP_ROWS = PASS // P
HALVES = V // P
LIST_HALF = S // 2
LIST_QUARTER = S // 4
QUAD = 32
PER_COLUMN = 16

SCALAR_PLANE = (1, 1)
PASS0_PARTS = ((0, 192, "scalar"), (192, 384, "gpsimd"), (384, S, "scalar"))
PASS1_PARTS = (
    (0, LIST_HALF, "vector", "scalar"),
    (LIST_HALF, LIST_HALF + LIST_QUARTER, "vector", "vector"),
    (LIST_HALF + LIST_QUARTER, S, "scalar", "scalar"),
)
AHEAD = 2

HALF_SLOT = 4 * P * 4
SLOT = 2 * HALF_SLOT
NODE_BYTES = 4 * 2
PLAIN_ROWS = GROUP_ROWS
QUARTER_SLOT = SLOT // 4
BLOCK = 32
RUN = 8
TURNED = 3 * RUN
LOAD_BLOCKS = (6, 5, 5)
LOAD_SLOTS = PLAIN_ROWS * SLOT
LAST_SLOT = LOAD_SLOTS + 2 * len(LOAD_BLOCKS) * SLOT

FLOPS = 2 * K * H * S + 2 * H * N * V


def tile_picked_sage_none_e_kernel(tc, xT, w1, w2, gate, offs, pos1, pos2, pos3, out):
    nc = tc.nc
    with ExitStack() as ctx:
        lists = ctx.enter_context(tc.tile_pool(name="lists", bufs=1))
        keep = ctx.enter_context(tc.tile_pool(name="keep", bufs=1))
        shared = ctx.enter_context(tc.tile_pool(name="shared", bufs=1))
        picks = ctx.enter_context(tc.tile_pool(name="picks", bufs=3))
        ps_acc = ctx.enter_context(tc.psum_pool(name="ps_acc", bufs=1))
        ps_z = ctx.enter_context(tc.psum_pool(name="ps_z", bufs=1))
        ps_back = ctx.enter_context(tc.psum_pool(name="ps_back", bufs=1))

        def product_bank(n):
            return ps_acc.tile([P, S], F32, name=f"acc{n % 3}")

        offs_t = lists.tile([P, S // PER_COLUMN], U16, name="offs_t")
        pos_t = [lists.tile([P, V // PER_COLUMN], U16, name=f"pos_t{d}") for d in range(D)]
        ident = keep.tile([P, P], F32, name="ident")
        ones = keep.tile([P, QUAD], F32, name="ones")
        column_count = keep.tile([P, QUAD], F32, name="column_count", align_bytes=64)
        partition_count = keep.tile([P, QUAD], F32, name="partition_count", align_bytes=64)
        nc.vector.memset(ones[:], 1.0)
        nc.vector.memset(ident[:], 0.0)
        nc.vector.tensor_tensor_scan(column_count[:], ones[:], ones[:], 0.0, MULT, ADD)
        nc.vector.transpose(partition_count[:], column_count[:])
        for first in range(0, P, QUAD):
            rows = slice(first, first + QUAD)
            nc.vector.tensor_tensor(ident[rows, rows], column_count[rows], partition_count[rows], IS_EQUAL)

        x_view = xT.rearrange("(s p j) t -> s p j t", s=PASSES, p=P, j=4)
        w1_view = w1.rearrange("(s p j) c -> s p j c", s=PASSES, p=P, j=4)
        w1_raw = {}
        gate_t = keep.tile([P, D, V], F32, name="gate_t")

        def load_w1(r):
            for s in range(PASSES):
                place = r * SLOT + s * HALF_SLOT
                w1_raw[r, s] = shared.tile([P, 4, P], F32, name=f"w1_raw{r}{s}", offset=place, align_bytes=64)
                nc.sync.dma_start(w1_raw[r, s][:], w1_view[s][:, :, r * P : r * P + P])

        gate_rows = keep.tile([P, D, P], F32, name="gate_rows")
        planes = {}
        for s in range(PASSES):
            for j in range(4):
                planes[s, j] = keep.tile([P, T], F32, name=f"plane{s}{j}")
                nc.sync.dma_start(planes[s, j][:], x_view[s][:, j, :])
                if (s, j) == (0, 0):
                    nc.sync.dma_start(offs_t[:], offs)
                    nc.sync.dma_start(gate_rows[P - HALVES : P], gate[:, 0, :].rearrange("d (h v) -> h d v", h=HALVES))
        nc.vector.memset(gate_rows[0 : P - HALVES], 0.0)
        turned_gate = product_bank(0)
        for d in range(D):
            nc.tensor.transpose(turned_gate[:, d * P : d * P + P], gate_rows[:, d, :], ident[:])
        gate_columns = keep.tile([P, D, HALVES], F32, name="gate_columns")
        nc.scalar.activation(
            gate_columns[:], turned_gate[:, 0 : D * P].rearrange("v (d q) -> v d q", d=D)[:, :, P - HALVES : P], COPY
        )
        for first in range(0, D, 2):
            turns = range(first, min(first + 2, D))
            spread = product_bank(1 + first // 2)
            for d in turns:
                for half in range(HALVES):
                    place = (d - first) * V + half * P
                    column = gate_columns[:, d, half : half + 1].to_broadcast([P, P])
                    nc.tensor.transpose(spread[:, place : place + P], column, ident[:])
            nc.scalar.activation(
                gate_t[:, first : first + len(turns), :].rearrange("p d v -> p (d v)"), spread[:, 0 : len(turns) * V], COPY
            )

        load_w1(0)
        load_w1(1)
        nc.sync.dma_start(pos_t[0][:], pos1)
        nc.sync.dma_start(pos_t[1][:], pos2)
        load_w1(2)
        nc.sync.dma_start(pos_t[2][:], pos3)
        load_w1(3)
        w1_load = {}
        first_block = [sum(LOAD_BLOCKS[:c]) for c in range(len(LOAD_BLOCKS))]

        def load_place(c, s):
            return LOAD_SLOTS + (2 * c + s) * SLOT + QUARTER_SLOT

        for c, blocks in enumerate(LOAD_BLOCKS):
            first = PASS + first_block[c] * BLOCK
            for s in range(PASSES):
                shape = [P, 4, blocks * BLOCK]
                w1_load[c, s] = shared.tile(shape, F32, name=f"w1_load{c}{s}", offset=load_place(c, s), align_bytes=64)
                nc.sync.dma_start(w1_load[c, s][:], w1_view[s][:, :, first : first + blocks * BLOCK])
        w2_raw = [keep.tile([P, 4, N], F32, name=f"w2_raw{g}") for g in range(GROUPS)]
        nc.sync.dma_start(w2_raw[0][:], w2[0:PASS].rearrange("(p j) n -> p j n", j=4))
        w2_blocks = w2[PASS:H].rearrange("(b r) n -> b r n", r=BLOCK)
        nc.sync.dma_start(
            w2_raw[1][:, 0:3, :].rearrange("p j n -> p (j n)"),
            w2_blocks[:, 0:TURNED, :].rearrange("b (a j) n -> b a (j n)", j=3),
        )
        nc.sync.dma_start(w2_raw[1][:, 3, :], w2_blocks[:, TURNED:BLOCK, :])

        def copy_on(engine, dst, src):
            if engine == "vector":
                nc.vector.tensor_copy(dst, src)
            elif engine == "gpsimd":
                nc.gpsimd.tensor_scalar(dst, src, 1.0, 0.0, MULT, ADD)
            else:
                nc.scalar.activation(dst, src, COPY)

        def interleave(engine, dst, src, run=4):
            if engine == "gpsimd":
                copy_on(engine, dst, src.rearrange("p j c -> p c j"))
                return
            copy_on(engine, dst.rearrange("p (q c) j -> p q j c", c=run), src.rearrange("p j (q c) -> p q j c", c=run))

        picked_planes = [keep.tile([P, 4, S], BF16, name=f"picked_planes{s}") for s in range(PASSES)]
        x_codes, x_scales = {}, {}

        def quantise_x(s, a, b, interleaved):
            nc.vector.quantize_mx(
                out=x_codes[s][:, a:b].bitcast(FP8X4),
                scales=x_scales[s][:, a:b],
                in_=interleaved.rearrange("p n j -> p (n j)"),
            )

        def entries_of(tile, a, b):
            return tile[:, a // PER_COLUMN : b // PER_COLUMN]

        w1_rounded, w1_codes, w1_scales, h_banks, h_tiles = {}, {}, {}, {}, {}

        def round_w1(r):
            w1_rounded[r] = keep.tile([P, PASSES, P, 4], BF16, name=f"w1_bf16_{r}", align_bytes=64)
            for s in range(PASSES):
                interleave("scalar", w1_rounded[r][:, s], w1_raw[r, s][:], 2)

        dealt_rounded = [keep.tile([P, PASS, 4], BF16, name=f"dealt_bf16_{s}", align_bytes=64) for s in range(PASSES)]
        dealt_codes = [keep.tile([P, PASS], U32, name=f"dealt_codes{s}", align_bytes=64) for s in range(PASSES)]
        dealt_scales = [keep.tile([P, PASS], U8, name=f"dealt_scales{s}", align_bytes=64) for s in range(PASSES)]

        def deal(c, s, first, width, place):
            blocks = LOAD_BLOCKS[c]
            begin = place + first_block[c] * width
            dst = dealt_rounded[s][:, begin : begin + blocks * width, :]
            runs = w1_load[c, s][:].rearrange("p j (b w) -> p b j w", w=BLOCK)[:, :, :, first : first + width]
            nc.scalar.copy(
                dst.rearrange("p (b q c) j -> p b q j c", q=width // 2, c=2), runs.rearrange("p b j (q c) -> p b q j c", c=2)
            )

        def deal_load(c):
            for s in range(PASSES):
                deal(c, s, 0, TURNED, 0)
                deal(c, s, TURNED, RUN, 3 * P)

        def quantise_dealt(r, rows):
            cols = slice((r - PLAIN_ROWS) * P, (r - PLAIN_ROWS + rows) * P)
            for s in range(PASSES):
                nc.vector.quantize_mx(
                    out=dealt_codes[s][:, cols].bitcast(FP8X4),
                    scales=dealt_scales[s][:, cols],
                    in_=dealt_rounded[s][:, cols, :].rearrange("p c j -> p (c j)"),
                )

        def quantise_w1(r, first, passes):
            if first == 0:
                w1_codes[r] = keep.tile([P, PASSES, P], U32, name=f"w1_codes{r}", align_bytes=64)
                w1_scales[r] = keep.tile([P, PASSES, P], U8, name=f"w1_scales{r}", align_bytes=64)
            part = slice(first, first + passes)
            nc.vector.quantize_mx(
                out=w1_codes[r][:, part].rearrange("p s c -> p (s c)").bitcast(FP8X4),
                scales=w1_scales[r][:, part].rearrange("p s c -> p (s c)"),
                in_=w1_rounded[r][:, part].rearrange("p s c j -> p (s c j)"),
            )

        def project(bank, r, s, a, b, first=0):
            if r < PLAIN_ROWS:
                codes, scales = w1_codes[r][:, s, :], w1_scales[r][:, s, :]
            else:
                cols = slice((r - PLAIN_ROWS) * P, (r - PLAIN_ROWS + 1) * P)
                codes, scales = dealt_codes[s][:, cols], dealt_scales[s][:, cols]
            nc.tensor.matmul_mx(
                out=bank[:, a:b],
                lhsT=codes.bitcast(FP8X4),
                lhsT_scale=scales,
                rhs=x_codes[s][:, a:b].bitcast(FP8X4),
                rhs_scale=x_scales[s][:, a:b],
                start=(s == first),
                stop=(s != first),
            )

        def project_row(r):
            h_banks[r] = product_bank(r)
            for s in range(PASSES):
                project(h_banks[r], r, s, 0, S)

        def fetch_row(r):
            if r + 1 < PLAIN_ROWS:
                h_tiles[r] = shared.tile([P, S], F32, name=f"h{r}", offset=(r + 1) * SLOT)
            elif r < ROWS - 2:
                h_tiles[r] = shared.tile([P, S], F32, name=f"h{r}", offset=load_place(r + 1 - PLAIN_ROWS, 0))
            else:
                h_tiles[r] = shared.tile([P, S], F32, name=f"h{r}", offset=LAST_SLOT + (r - ROWS + 2) * HALF_SLOT)
            nc.scalar.activation(h_tiles[r][:], h_banks[r][:], COPY)

        zT_places = (load_place(2, 1) - QUARTER_SLOT // 2, load_place(2, 1) + 3 * QUARTER_SLOT // 2)
        zT = {
            (0, half): shared.tile([P, 2, P, 2], BF16, name=f"zT0{half}", offset=zT_places[half]) for half in range(HALVES)
        }
        z1_rounded = [keep.tile([P, P, 4], BF16, name=f"z1_bf16_{half}", align_bytes=64) for half in range(HALVES)]
        w2_scales = keep.tile([P, GROUPS, N], U8, name="w2_scales", align_bytes=64)
        w2_place = load_place(2, 0)
        w2_rounded = shared.tile([P, GROUPS, N, 4], BF16, name="w2_bf16", offset=w2_place, align_bytes=64)
        z0_rounded = keep.tile([P, HALVES, P, 4], BF16, name="z0_bf16", align_bytes=64)
        z_banks = {}

        held_picks = {(2, 2): load_place(0, 1), (3, 2): load_place(1, 1), (4, 2): load_place(2, 1) + QUARTER_SLOT // 2}

        def add_turned(dst, picked, d):
            nc.tensor.matmul(dst, picked, ident[:], start=(d == 0), stop=(d == D - 1), is_transpose=True)

        def pick_neighbours(r, d):
            g, place = divmod(r, GROUP_ROWS)
            if place == 0 and d == 0:
                for half in range(HALVES):
                    z_banks[g, half] = ps_z.tile([P, PASS], F32, name=f"z_bank{g}{half}")
            if d == D - 1 and r + AHEAD < PLAIN_ROWS:
                picked = shared.tile([P, V], F32, name=f"third{r}", offset=(r + AHEAD) * SLOT + HALF_SLOT)
            elif (r, d) in held_picks:
                picked = shared.tile([P, V], F32, name=f"held{r}{d}", offset=held_picks[r, d])
            else:
                picked = picks.tile([P, V], F32, name=f"picked{d}")
            nc.vector.tensor_tensor(picked[:], h_tiles[r][:].indirect(pos_t[d][:]), gate_t[:, d, :], MULT)
            for half in range(HALVES):
                add_turned(z_banks[g, half][:, place * P : place * P + P], picked[:, half * P : half * P + P], d)

        def round_z(engine, g, half, sums, place, rows):
            dst = zT[g, half][:, :, 32 * place : 32 * (place + rows), :]
            copy_on(engine, dst, sums.rearrange("v (p u e) -> v u p e", u=2, e=2))

        def turn_back(dst, g, half, u):
            words = zT[g, half][:].rearrange("v u p e -> v (u p e)").bitcast(F32)
            nc.tensor.transpose(dst, words[:, u * P : u * P + P], ident[:])

        def first_pass_turn():
            turned = ps_back.tile([P, HALVES, 2, P], F32, name="turned")
            for half in range(HALVES):
                for u in range(2):
                    turn_back(turned[:, half, u, :], 0, half, u)
            return turned

        def first_pass_back(turned):
            words = z0_rounded[:].rearrange("p h v j -> p (h v j)").bitcast(F32)
            nc.scalar.copy(
                words.rearrange("p (h v u) -> p h v u", h=HALVES, u=2), turned[:].rearrange("p h u v -> p h v u")
            )

        def last_rows_and_second_product():
            turned_row, direct_row = ROWS - 2, ROWS - 1

            def pick(dst, r, d, half):
                a, b = half * P, half * P + P
                nc.vector.tensor_tensor(dst, h_tiles[r][:].indirect(entries_of(pos_t[d], a, b)), gate_t[:, d, a:b], MULT)

            pick_neighbours(turned_row, 0)
            for half in range(HALVES):
                for d in range(1, D):
                    picked = keep.tile([P, P], F32, name=f"turned_half{half}{d}")
                    pick(picked[:], turned_row, d, half)
                    add_turned(z_banks[1, half][:, 2 * P : 3 * P], picked[:], d)
            held = LAST_SLOT + SLOT + HALF_SLOT
            zT[1, 0] = keep.tile([P, 2, P, 2], BF16, name="zT10")
            zT[1, 1] = keep.tile([P, 2, P, 2], BF16, name="zT11")
            back = [ps_z.tile([P, PASS], F32, name=f"z_bank0{half}") for half in range(HALVES)]

            def words_back(half):
                words = z1_rounded[half][:].rearrange("p v j -> p (v j)").bitcast(F32).rearrange("p (v u) -> p v u", u=2)
                nc.scalar.copy(words, back[half][:, 0 : 2 * P].rearrange("p (u v) -> p v u", u=2))

            direct_sums = product_bank(ROWS)
            for d in range(D):
                picked = shared.tile([P, P], F32, name=f"first_direct{d}", offset=held + d * QUARTER_SLOT // 2)
                pick(picked[:], direct_row, d, 0)
                add_turned(direct_sums[:, 0:P], picked[:], d)
            directs = keep.tile([P, D, P], F32, name="directs")
            for d in range(D):
                pick(directs[:, d, :], direct_row, d, 1)
            for half in range(HALVES):
                sums = z_banks[1, half][:, 0 : 3 * P].rearrange("v (p j) -> v p j", j=3)
                copy_on("scalar", zT[1, half][:, 0], sums[:, :, 0:2])
                turn_back(back[half][:, 0:P], 1, half, 0)
                if half:
                    copy_on("scalar", zT[1, half][:, 1], sums[:, :, 2:3].to_broadcast([P, P, 2]))
                    turn_back(back[half][:, P : 2 * P], 1, half, 1)
                else:
                    copy_on("scalar", zT[1, half][:, 1, :, 0], sums[:, :, 2])
            copy_on("scalar", zT[1, 0][:, 1, :, 1], direct_sums[:, 0:P])
            turn_back(back[0][:, P : 2 * P], 1, 0, 1)
            words_back(1)
            words_back(0)
            w2_codes = shared.tile([P, GROUPS, N], U32, name="w2_codes", offset=held + QUARTER_SLOT // 2, align_bytes=64)

            def quantise_w2(g):
                nc.vector.quantize_mx(
                    out=w2_codes[:, g].bitcast(FP8X4),
                    scales=w2_scales[:, g, :],
                    in_=w2_rounded[:, g].rearrange("p n j -> p (n j)"),
                )

            partial = keep.tile([P, P], F32, name="partial")
            nc.vector.tensor_tensor(partial[:], directs[:, 0, :], directs[:, 1, :], ADD)
            z0_codes = shared.tile([P, V], U32, name="z0_codes", offset=held - QUARTER_SLOT // 2, align_bytes=64)
            z0_scales = keep.tile([P, V], U8, name="z0_scales", align_bytes=64)
            nc.vector.quantize_mx(
                out=z0_codes[:].bitcast(FP8X4),
                scales=z0_scales[:],
                in_=z0_rounded[:].rearrange("p h v j -> p (h v j)"),
            )
            quantise_w2(0)
            nc.vector.tensor_tensor(z1_rounded[1][:, :, 3], partial[:], directs[:, D - 1, :], ADD)
            quantise_w2(1)
            result = keep.tile([N, V], F32, name="result")
            copier = ("vector", "scalar")
            for half in (1, 0):
                cols = slice(half * P, half * P + P)
                z1_codes = keep.tile([P, P], U32, name=f"z1_codes{half}", align_bytes=64)
                z1_scales = keep.tile([P, P], U8, name=f"z1_scales{half}", align_bytes=64)
                nc.vector.quantize_mx(
                    out=z1_codes[:].bitcast(FP8X4),
                    scales=z1_scales[:],
                    in_=z1_rounded[half][:].rearrange("p v j -> p (v j)"),
                )
                acc = ps_z.tile([P, PASS], F32, name="z_bank00") if half else product_bank(ROWS)
                operands = ((z0_codes[:, cols], z0_scales[:, cols]), (z1_codes[:], z1_scales[:]))
                for g, (codes, scales) in enumerate(operands):
                    nc.tensor.matmul_mx(
                        out=acc[:, 0:P],
                        lhsT=w2_codes[:, g, :].bitcast(FP8X4),
                        lhsT_scale=w2_scales[:, g, :],
                        rhs=codes.bitcast(FP8X4),
                        rhs_scale=scales,
                        start=(g == 0),
                        stop=(g == GROUPS - 1),
                    )
                copy_on(copier[half], result[:, cols], acc[:, 0:P])
                nc.sync.dma_start(out[:, cols], result[:, cols])

        def pick_plane(s, j, parts):
            if (s, j) == SCALAR_PLANE:
                plane_bf16 = keep.tile([P, T], BF16, name="plane_bf16")
                nc.scalar.activation(plane_bf16[:], planes[s, j][:], COPY)
                nc.scalar.activation(picked_planes[s][:, j, :], plane_bf16[:].indirect(offs_t[:]), COPY)
                return
            for a, b in parts:
                nc.vector.tensor_copy(picked_planes[s][:, j, a:b], planes[s, j][:].indirect(entries_of(offs_t, a, b)))

        whole_list = ((0, S),)
        x_codes[0] = keep.tile([P, S], U32, name="x_codes0", align_bytes=64)
        x_scales[0] = keep.tile([P, S], U8, name="x_scales0", align_bytes=64)
        for j in range(3):
            pick_plane(0, j, whole_list)
        pick_plane(0, 3, [(a, b) for a, b, engine in PASS0_PARTS])
        x0_interleaved = keep.tile([P, S, 4], BF16, name="x0_bf16", align_bytes=64)
        for a, b, engine in PASS0_PARTS:
            interleave(engine, x0_interleaved[:, a:b], picked_planes[0][:, :, a:b])
        quantise_x(0, 0, S, x0_interleaved[:])

        for j in range(3):
            pick_plane(1, j, whole_list)
        pick_plane(1, 3, ((0, LIST_HALF), (LIST_HALF, S)))
        x1_interleaved = {}
        for a, b, interleaver, copier in PASS1_PARTS:
            shape, name = [P, b - a, 4], f"x1_bf16_{a}"
            if a < LIST_HALF:
                x1_interleaved[a] = keep.tile(shape, BF16, name=name, align_bytes=64)
            else:
                place = NODE_BYTES * (a - LIST_HALF)
                x1_interleaved[a] = shared.tile(shape, BF16, name=name, offset=place, align_bytes=64)
        x_scales[1] = keep.tile([P, S], U8, name="x_scales1", align_bytes=64)
        round_w1(0)
        for a, b, interleaver, copier in PASS1_PARTS:
            interleave(interleaver, x1_interleaved[a][:], picked_planes[1][:, :, a:b])
            if a == 0:
                quantise_w1(0, 0, 1)
        quantise_w1(0, 1, 1)
        x_codes[1] = shared.tile([P, S], U32, name="x_codes1", offset=HALF_SLOT, align_bytes=64)
        for a, b, interleaver, copier in PASS1_PARTS:
            quantise_x(1, a, b, x1_interleaved[a][:])
        part_banks = [product_bank(0), product_bank(2), ps_z.tile([P, PASS], F32, name="z_bank10")]
        for s in range(PASSES):
            for bank, (a, b, interleaver, copier) in zip(part_banks, PASS1_PARTS):
                project(bank, 0, s, a, b)
        w1_codes[1] = keep.tile([P, PASSES, P], U32, name="w1_codes1", align_bytes=64)
        w1_scales[1] = keep.tile([P, PASSES, P], U8, name="w1_scales1", align_bytes=64)
        second_rounded = [
            keep.tile([P, P, 4], BF16, name="w1_bf16_10", align_bytes=64),
            shared.tile([P, P, 4], BF16, name="w1_bf16_11", offset=0, align_bytes=64),
        ]
        for s, engine in enumerate(("scalar", "vector")):
            interleave(engine, second_rounded[s][:], w1_raw[1, s][:], 4 if s else 2)
        h_tiles[0] = keep.tile([P, S], F32, name="h0")
        for s in range(PASSES):
            nc.vector.quantize_mx(
                out=w1_codes[1][:, s].bitcast(FP8X4),
                scales=w1_scales[1][:, s],
                in_=second_rounded[s][:].rearrange("p c j -> p (c j)"),
            )
            if s == 0:
                for bank, (a, b, interleaver, copier) in zip(part_banks, PASS1_PARTS):
                    copy_on(copier, h_tiles[0][:, a:b], bank[:, a:b])
        project_row(1)

        for r in range(PLAIN_ROWS - AHEAD):
            pick_neighbours(r, 0)
            pick_neighbours(r, 1)
            round_w1(r + AHEAD)
            quantise_w1(r + AHEAD, 0, PASSES)
            project_row(r + AHEAD)
            fetch_row(r + 1)
            pick_neighbours(r, 2)
        for c in range(len(LOAD_BLOCKS)):
            r = PLAIN_ROWS - AHEAD + c
            pick_neighbours(r, 0)
            pick_neighbours(r, 1)
            deal_load(c)
            quantise_dealt(r + AHEAD, 2 if r + AHEAD == ROWS - 2 else 1)
            project_row(r + AHEAD)
            fetch_row(r + 1)
            pick_neighbours(r, 2)
        for half in range(HALVES):
            round_z("scalar", 0, half, z_banks[0, half][:], 0, GROUP_ROWS)
        turned0 = first_pass_turn()
        project_row(ROWS - 1)
        fetch_row(ROWS - 2)
        fetch_row(ROWS - 1)
        first_pass_back(turned0)
        for d in range(D):
            pick_neighbours(ROWS - 3, d)
        for g in range(GROUPS):
            interleave("scalar", w2_rounded[:, g], w2_raw[g][:], 2)
        last_rows_and_second_product()
